import numpy as np
import ml_dtypes


def mxq(x, axis, fmt="e4m3"):
    dtype, down = {"e4m3": (ml_dtypes.float8_e4m3fn, 7), "e5m2": (ml_dtypes.float8_e5m2, 14)}[fmt]
    v = np.moveaxis(np.asarray(x, np.float32).astype(ml_dtypes.bfloat16).astype(np.float64), axis, -1)
    blocks = v.reshape(v.shape[:-1] + (-1, 32))
    amax = np.abs(blocks).max(-1, keepdims=True)
    byte = np.maximum(np.where(amax > 0, np.frexp(amax)[1] - 1 + 127, 0) - down, 1)
    scale = np.exp2(byte - 127.0)
    codes = (blocks / scale).astype(np.float32).astype(dtype).astype(np.float64)
    return np.moveaxis((codes * scale).reshape(v.shape), -1, axis)


WIDE = False


def mx_kscale(k):
    if not WIDE:
        return np.ones(k)
    levels = np.array([18, -18])
    if k % 512:
        return np.exp2(np.random.permutation(np.resize(levels, k // 32))).repeat(32)
    a = np.empty((k // 512, 16))
    for p in range(k // 512):
        a[p, :8] = np.random.permutation(np.resize(levels, 8))
        for g in range(8):
            far = levels[np.abs(levels - a[p, g]) >= 10]
            a[p, g + 8] = far[np.random.randint(len(far))]
    return np.exp2(a.ravel()).repeat(32)


def f64(x):
    return np.asarray(x).astype(np.float64)


def striped(idx):
    return np.tile(np.asarray(idx).reshape(-1, 16).T, (8, 1)).astype(np.uint16)


def unstriped(offs):
    return offs[:16].T.reshape(-1).astype(np.int64)

def planes(y):
    n, m = y.shape
    v = y.astype(np.float32).astype(ml_dtypes.bfloat16).astype(np.float64).reshape(n // 32, 32, m)
    top = np.abs(v).max(1)
    byte = np.clip(np.where(top > 0, np.frexp(top)[1] - 1 + 127 - 7, 1), 1, 254)
    codes = (v * np.exp2(127.0 - byte)[:, None, :]).reshape(n, m).astype(np.float32).astype(ml_dtypes.float8_e4m3fn).view(np.uint8)
    words = codes.reshape(n // 512, 128, 4, m).transpose(0, 1, 3, 2)
    return np.ascontiguousarray(words), np.ascontiguousarray(byte.astype(np.uint8).reshape(n // 512, 16, m))


def sig(x):
    return 1.0 / (1.0 + np.exp(-x))


def setup_inputs():
    n = np.random.standard_normal
    uni = np.random.uniform
    idx = np.random.permutation(2048)[:512]
    f_d = mx_kscale(512)
    f_r = mx_kscale(512)
    return {
        "wT": (np.round(n((512, 2048)) * 64) / 64 * f_d[:, None]).astype(np.float32),
        "mT": (np.round(0.5 * n((512, 2048)) * 64) / 64 * f_d[:, None]).astype(np.float32),
        "xT": (n((512, 512)) / np.sqrt(512) / f_d[:, None] * f_r[None, :]).astype(np.float32),
        "y": (np.random.randint(0, 2, (512, 512))).astype(np.float32),
        "ts": np.tile(uni(0.75, 1.3, 2048), (128, 1)).astype(np.float32),
        "us": (uni(0.75, 1.3, (512, 1)) / f_r[:, None]).astype(np.float32),
        "wt": (uni(0.75, 1.3, (512, 1)) / np.sqrt(512)).astype(np.float32),
        "offs": striped(idx),
    }


def reference(wT, mT, xT, y, ts, us, wt, offs):
    idx = unstriped(offs)
    wT_i = f64(wT)[:, idx]
    mT_i = f64(mT)[:, idx]
    ts_i = f64(ts)[:1][:, idx]
    w2 = wT_i + mT_i
    a = mxq(f64(xT), 0, "e4m3").T @ mxq(w2, 0, "e4m3")
    g = f64(wt) * f64(us) * ts_i * (sig(f64(us) * ts_i * a) - f64(y))
    dw = mxq(f64(xT), 1, "e4m3") @ mxq(g, 0, "e5m2")
    out_0 = np.zeros((512, 2048))
    out_0[:, idx] = dw
    return (out_0,) + planes(out_0)

@@ -1,0 +1,284 @@
+from contextlib import ExitStack
+
+import concourse.mybir as mybir
+from concourse.masks import make_identity
+
+D, R, SLOTS, COLS = 512, 512, 512, 2048
+FLOPS = 2 * 2 * D * R * SLOTS
+
+F32 = mybir.dt.float32
+BF16 = mybir.dt.bfloat16
+I32 = mybir.dt.int32
+U32 = mybir.dt.uint32
+U16 = mybir.dt.uint16
+U8 = mybir.dt.uint8
+E4M3 = mybir.dt.float8_e4m3fn_x4
+E5M2 = mybir.dt.float8_e5m2_x4
+ALU = mybir.AluOpType
+ACT = mybir.ActivationFunctionType
+
+P = 128
+LANES = 4
+CHUNK = 128
+CHUNKS = SLOTS // CHUNK
+PIECE = 256
+PIECES = COLS // PIECE
+SCALAR_PIECES = 2
+
+
+def tile_attend_gahead_sam_log_pl_kernel(tc, wT, mT, xT, y, ts, us, wt, offs, out_0, out_1, out_2):
+    nc = tc.nc
+    with ExitStack() as ctx:
+        keep = ctx.enter_context(tc.tile_pool(name="keep", bufs=1))
+        psum = ctx.enter_context(tc.psum_pool(name="psum", bufs=1))
+
+        def sb(name, shape, dtype):
+            return keep.tile(shape, dtype, name=name, align_bytes=64)
+
+        def slot_list(first, count):
+            return offsets[:, first // 16 : (first + count) // 16]
+
+        offsets = keep.tile([P, SLOTS // 16], U16, name="offsets")
+        x = sb("x", [P, LANES, R], F32)
+        nc.sync.dma_start(out=x[:], in_=xT.rearrange("(p t) r -> p t r", t=LANES))
+        nc.sync.dma_start(offsets[:], offs)
+
+        us_col = sb("us_col", [P, LANES], F32)
+        wt_col = sb("wt_col", [P, LANES], F32)
+        nc.scalar.dma_start(out=us_col[:], in_=us.rearrange("(p u) one -> p (u one)", u=LANES))
+        nc.scalar.dma_start(out=wt_col[:], in_=wt.rearrange("(p u) one -> p (u one)", u=LANES))
+        ts_table = sb("ts_table", [P, COLS], F32)
+        nc.vector.memset(ts_table[:], 0.0)
+        nc.scalar.dma_start(out=ts_table[0:1, :], in_=ts[0:1, :])
+
+        w_rows = wT.rearrange("(p t) c -> p t c", t=LANES)
+        m_rows = mT.rearrange("(p t) c -> p t c", t=LANES)
+        w_table, m_table = [], []
+        for t in range(LANES):
+            w_table.append(sb("w_table%d" % t, [P, COLS], F32))
+            m_table.append(sb("m_table%d" % t, [P, COLS], F32))
+            nc.sync.dma_start(out=w_table[t][:], in_=w_rows[:, t, :])
+            nc.sync.dma_start(out=m_table[t][:], in_=m_rows[:, t, :])
+        labels = sb("labels", [P, LANES, SLOTS], F32)
+        nc.sync.dma_start(out=labels[:], in_=y.rearrange("(p u) i -> p u i", u=LANES))
+
+        ident_f32 = sb("ident_f32", [P, P], F32)
+        ident_bf16 = sb("ident_bf16", [P, P], BF16)
+        make_identity(nc, ident_f32[:])
+        make_identity(nc, ident_bf16[:])
+
+        window = [sb("window%d" % t, [P, COLS], F32) for t in range(LANES)]
+        for t in range(LANES):
+            nc.vector.memset(window[t][:], 0.0)
+
+        x_by_d = sb("x_by_d", [P, LANES, P, LANES], BF16)
+        nc.scalar.copy(
+            out=x_by_d[:].rearrange("p u s t -> p s u t"),
+            in_=x[:].rearrange("p t (s u) -> p s u t", u=LANES),
+        )
+        xd_codes = sb("xd_codes", [P, R], U32)
+        xd_scales = sb("xd_scales", [P, R], U8)
+        nc.vector.quantize_mx(
+            out=xd_codes[:].bitcast(E4M3), scales=xd_scales[:], in_=x_by_d[:].rearrange("p u s t -> p (u s t)")
+        )
+
+        x_by_r = sb("x_by_r", [P, LANES, P, LANES], BF16)
+        for t in range(LANES):
+            turned = psum.tile([P, LANES, P], BF16, name="turned%d" % t, tag="a%d" % t)
+            for u in range(LANES):
+                nc.tensor.transpose(turned[:, u, :], x_by_d[:, u, :, t], ident_bf16[:])
+            nc.scalar.copy(out=x_by_r[:, t, :, :], in_=turned[:].rearrange("s u p -> s p u"))
+        xr_codes = sb("xr_codes", [P, D], U32)
+        xr_scales = sb("xr_scales", [P, D], U8)
+        nc.vector.quantize_mx(
+            out=xr_codes[:].bitcast(E4M3), scales=xr_scales[:], in_=x_by_r[:].rearrange("s t p u -> s (t p u)")
+        )
+
+        ts_row = sb("ts_row", [P, SLOTS], F32)
+        nc.vector.tensor_copy(out=ts_row[:], in_=ts_table[:].indirect(offsets[:]))
+        ts_turned = psum.tile([P, CHUNKS, P], F32, name="ts_turned", tag="b0")
+        for j in range(CHUNKS):
+            nc.tensor.transpose(ts_turned[:, j, :], ts_row[:, j * P : (j + 1) * P], ident_f32[:])
+        ts_col = sb("ts_col", [P, CHUNKS], F32)
+        nc.scalar.copy(out=ts_col[:], in_=ts_turned[:, :, 0])
+        ts_all = psum.tile([P, SLOTS], F32, name="ts_all", tag="b1")
+        for j in range(CHUNKS):
+            nc.tensor.transpose(ts_all[:, j * P : (j + 1) * P], ts_col[:, j : j + 1].to_broadcast([P, P]), ident_f32[:])
+        wu_col = sb("wu_col", [P, LANES], F32)
+        nc.vector.tensor_tensor(out=wu_col[:], in0=wt_col[:], in1=us_col[:], op=ALU.mult)
+        logit_scale = sb("logit_scale", [P, LANES, SLOTS], F32)
+        grad_scale = sb("grad_scale", [P, LANES, SLOTS], F32)
+        for u in range(LANES):
+            nc.scalar.activation(out=logit_scale[:, u, :], in_=ts_all[:], func=ACT.Copy, scale=us_col[:, u : u + 1])
+        for u in range(LANES):
+            nc.scalar.activation(out=grad_scale[:, u, :], in_=ts_all[:], func=ACT.Copy, scale=wu_col[:, u : u + 1])
+
+        w_picked = [keep.tile([P, SLOTS], F32, name="w_picked%d" % t, tag="w_picked%d" % (t % 2)) for t in range(2)]
+        w2_low = sb("w2_low", [P, 2, SLOTS], F32)
+        w2_high = [sb("w2_high%d" % j, [P, 2, CHUNK], F32) for j in range(CHUNKS)]
+        w2_by_d = [sb("w2_by_d%d" % j, [P, CHUNK, LANES], BF16) for j in range(CHUNKS)]
+        w2_codes = [sb("w2_codes%d" % j, [P, CHUNK], U32) for j in range(CHUNKS)]
+        w2_scales = [sb("w2_scales%d" % j, [P, CHUNK], U8) for j in range(CHUNKS)]
+
+        def chunk(j):
+            return slice(j * CHUNK, (j + 1) * CHUNK)
+
+        for t in range(2):
+            nc.vector.tensor_copy(out=w_picked[t][:], in_=w_table[t][:].indirect(offsets[:]))
+            nc.vector.tensor_tensor(
+                out=w2_low[:, t, :], in0=m_table[t][:].indirect(offsets[:]), in1=w_picked[t][:], op=ALU.add
+            )
+        for j in range(CHUNKS):
+            nc.scalar.copy(out=w2_by_d[j][:, :, 0:2], in_=w2_low[:, :, chunk(j)].rearrange("p e i -> p i e"))
+
+        def add_high(t, j):
+            nc.vector.tensor_tensor(
+                out=w2_high[j][:, t - 2, :],
+                in0=m_table[t][:].indirect(slot_list(j * CHUNK, CHUNK)),
+                in1=w_picked[t - 2][:, chunk(j)],
+                op=ALU.add,
+            )
+
+        nc.vector.tensor_copy(out=w_picked[0][:], in_=w_table[2][:].indirect(offsets[:]))
+        for j in range(CHUNKS):
+            add_high(2, j)
+        nc.vector.tensor_copy(out=w_picked[1][:], in_=w_table[3][:].indirect(offsets[:]))
+
+        scores = [None] * CHUNKS
+        work = [sb("work%d" % j, [P, LANES, CHUNK], F32) for j in range(CHUNKS)]
+        g_by_r = [sb("g_by_r%d" % j, [P, CHUNK, LANES], BF16) for j in range(CHUNKS)]
+        g_codes = sb("g_codes", [P, SLOTS], U32)
+        g_scales = sb("g_scales", [P, SLOTS], U8)
+
+        def finish_w2(j):
+            add_high(3, j)
+            nc.scalar.copy(out=w2_by_d[j][:, :, 2:4], in_=w2_high[j][:].rearrange("p e i -> p i e"))
+
+        def score(j):
+            nc.vector.quantize_mx(
+                out=w2_codes[j][:].bitcast(E4M3), scales=w2_scales[j][:], in_=w2_by_d[j][:].rearrange("p i t -> p (i t)")
+            )
+            scores[j] = psum.tile([P, LANES, CHUNK], F32, name="scores%d" % j, tag="a%d" % j)
+            for u in range(LANES):
+                rows = slice(u * P, (u + 1) * P)
+                nc.tensor.matmul_mx(
+                    out=scores[j][:, u, :],
+                    lhsT=xd_codes[:, rows].bitcast(E4M3),
+                    lhsT_scale=xd_scales[:, rows],
+                    rhs=w2_codes[j][:].bitcast(E4M3),
+                    rhs_scale=w2_scales[j][:],
+                    start=True,
+                    stop=True,
+                )
+
+        def logits(j):
+            nc.vector.tensor_tensor(out=work[j][:], in0=scores[j][:], in1=logit_scale[:, :, chunk(j)], op=ALU.mult)
+            nc.scalar.activation(out=work[j][:], in_=work[j][:], func=ACT.Sigmoid)
+
+        def residual(j):
+            nc.vector.tensor_tensor(out=work[j][:], in0=work[j][:], in1=labels[:, :, chunk(j)], op=ALU.subtract)
+
+        def gradient(j):
+            nc.vector.tensor_tensor(
+                out=g_by_r[j][:].rearrange("p (c i) u -> p c u i", i=2),
+                in0=work[j][:].rearrange("p u (c i) -> p c u i", i=2),
+                in1=grad_scale[:, :, chunk(j)].rearrange("p u (c i) -> p c u i", i=2),
+                op=ALU.mult,
+            )
+
+        def quantise_g(j):
+            nc.vector.quantize_mx(
+                out=g_codes[:, chunk(j)].bitcast(E5M2),
+                scales=g_scales[:, chunk(j)],
+                in_=g_by_r[j][:].rearrange("p i u -> p (i u)"),
+            )
+
+        finish_w2(0)
+        finish_w2(1)
+        finish_w2(2)
+        score(0)
+        finish_w2(3)
+        score(1)
+        score(2)
+        logits(0)
+        score(3)
+        logits(1)
+        residual(0)
+        logits(2)
+        gradient(0)
+        residual(1)
+        logits(3)
+        quantise_g(0)
+        gradient(1)
+        residual(2)
+        quantise_g(1)
+        residual(3)
+        gradient(2)
+        gradient(3)
+        quantise_g(2)
+        quantise_g(3)
+
+        out_rows = out_0.rearrange("(p t) c -> p t c", t=LANES)
+        pairs = [sb("pairs%d" % k, [P, 2, PIECE, 2], BF16) for k in range(PIECES)]
+
+        def piece(k):
+            return slice(k * PIECE, (k + 1) * PIECE)
+
+        def round_plane(t, k):
+            nc.scalar.copy(out=pairs[k][:, t // 2, :, t % 2], in_=window[t][:, piece(k)])
+
+        dw = [sb("dw%d" % t, [P, SLOTS], F32) for t in range(LANES)]
+        for t in range(LANES):
+            features = slice(t * P, (t + 1) * P)
+            sums = psum.tile([P, SLOTS], F32, name="sums%d" % t, tag="b%d" % t)
+            nc.tensor.matmul_mx(
+                out=sums[:],
+                lhsT=xr_codes[:, features].bitcast(E4M3),
+                lhsT_scale=xr_scales[:, features],
+                rhs=g_codes[:].bitcast(E5M2),
+                rhs_scale=g_scales[:],
+                start=True,
+                stop=True,
+            )
+            nc.scalar.copy(out=dw[t][:], in_=sums[:])
+        for t in range(LANES):
+            nc.vector.tensor_copy(out=window[t][:].indirect(offsets[:]), in_=dw[t][:])
+            nc.sync.dma_start(out=out_rows[:, t, :], in_=window[t][:])
+            if t < LANES - 1:
+                for k in range(PIECES):
+                    round_plane(t, k)
+
+        out_by_d = [sb("out_by_d%d" % k, [P, PIECE * LANES], BF16) for k in range(PIECES)]
+        out_codes = [sb("out_codes%d" % h, [P, 2 * PIECE], U32) for h in range(PIECES // 2)]
+        out_scales = sb("out_scales", [P, COLS], U8)
+        code_rows = out_1[0].rearrange("p c l -> p (c l)").bitcast(I32)
+
+        def weave(k):
+            words_in = pairs[k][:].rearrange("p h c e -> p (h c e)").bitcast(F32).rearrange("p (h c) -> p c h", h=2)
+            words_out = out_by_d[k][:].bitcast(F32).rearrange("p (c h) -> p c h", h=2)
+            if k < PIECES - SCALAR_PIECES:
+                nc.vector.tensor_copy(out=words_out, in_=words_in)
+            else:
+                nc.scalar.copy(out=words_out, in_=words_in)
+
+        def quantise_out(k):
+            half = slice((k % 2) * PIECE, (k % 2 + 1) * PIECE)
+            nc.vector.quantize_mx(
+                out=out_codes[k // 2][:, half].bitcast(E4M3), scales=out_scales[:, piece(k)], in_=out_by_d[k][:]
+            )
+            if k % 2 == 1:
+                nc.sync.dma_start(
+                    out=code_rows[:, (k - 1) * PIECE : (k + 1) * PIECE], in_=out_codes[k // 2][:].bitcast(I32)
+                )
+
+        for k in range(PIECES):
+            round_plane(LANES - 1, k)
+        for k in range(PIECES + 1):
+            if k < PIECES:
+                weave(k)
+            if k > 0:
+                quantise_out(k - 1)
+        scale_rows = out_2[0].bitcast(I32)
+        for q in range(4):
+            queue = nc.sync if q % 2 == 0 else nc.scalar
+            queue.dma_start(out=scale_rows[4 * q : 4 * q + 4, :], in_=out_scales[32 * q : 32 * q + 4, :].bitcast(I32))

@@ -23,7 +23,8 @@ CHUNK = 128
 CHUNKS = SLOTS // CHUNK
 PIECE = 256
 PIECES = COLS // PIECE
-SCALAR_PIECES = 2
+SCALAR_PIECES = 3
+VECTOR_PIECES = 2
 
 
 def tile_attend_gahead_sam_log_pl_kernel(tc, wT, mT, xT, y, ts, us, wt, offs, out_0, out_1, out_2):
@@ -47,6 +48,8 @@ def tile_attend_gahead_sam_log_pl_kernel(tc, wT, mT, xT, y, ts, us, wt, offs, ou
         wt_col = sb("wt_col", [P, LANES], F32)
         nc.scalar.dma_start(out=us_col[:], in_=us.rearrange("(p u) one -> p (u one)", u=LANES))
         nc.scalar.dma_start(out=wt_col[:], in_=wt.rearrange("(p u) one -> p (u one)", u=LANES))
+        warm = sb("warm", [P, 1], F32)
+        nc.scalar.activation(out=warm[:], in_=us_col[:, 0:1], func=ACT.Sigmoid)
         ts_table = sb("ts_table", [P, COLS], F32)
         nc.vector.memset(ts_table[:], 0.0)
         nc.scalar.dma_start(out=ts_table[0:1, :], in_=ts[0:1, :])
@@ -114,8 +117,8 @@ def tile_attend_gahead_sam_log_pl_kernel(tc, wT, mT, xT, y, ts, us, wt, offs, ou
             nc.scalar.activation(out=grad_scale[:, u, :], in_=ts_all[:], func=ACT.Copy, scale=wu_col[:, u : u + 1])
 
         w_picked = [keep.tile([P, SLOTS], F32, name="w_picked%d" % t, tag="w_picked%d" % (t % 2)) for t in range(2)]
-        w2_low = sb("w2_low", [P, 2, SLOTS], F32)
-        w2_high = [sb("w2_high%d" % j, [P, 2, CHUNK], F32) for j in range(CHUNKS)]
+        w2_early = sb("w2_early", [P, LANES - 1, SLOTS], F32)
+        w2_last = [sb("w2_last%d" % j, [P, CHUNK], F32) for j in range(CHUNKS)]
         w2_by_d = [sb("w2_by_d%d" % j, [P, CHUNK, LANES], BF16) for j in range(CHUNKS)]
         w2_codes = [sb("w2_codes%d" % j, [P, CHUNK], U32) for j in range(CHUNKS)]
         w2_scales = [sb("w2_scales%d" % j, [P, CHUNK], U8) for j in range(CHUNKS)]
@@ -123,25 +126,13 @@ def tile_attend_gahead_sam_log_pl_kernel(tc, wT, mT, xT, y, ts, us, wt, offs, ou
         def chunk(j):
             return slice(j * CHUNK, (j + 1) * CHUNK)
 
-        for t in range(2):
-            nc.vector.tensor_copy(out=w_picked[t][:], in_=w_table[t][:].indirect(offsets[:]))
+        for t in range(LANES - 1):
+            nc.vector.tensor_copy(out=w_picked[t % 2][:], in_=w_table[t][:].indirect(offsets[:]))
             nc.vector.tensor_tensor(
-                out=w2_low[:, t, :], in0=m_table[t][:].indirect(offsets[:]), in1=w_picked[t][:], op=ALU.add
+                out=w2_early[:, t, :], in0=m_table[t][:].indirect(offsets[:]), in1=w_picked[t % 2][:], op=ALU.add
             )
         for j in range(CHUNKS):
-            nc.scalar.copy(out=w2_by_d[j][:, :, 0:2], in_=w2_low[:, :, chunk(j)].rearrange("p e i -> p i e"))
-
-        def add_high(t, j):
-            nc.vector.tensor_tensor(
-                out=w2_high[j][:, t - 2, :],
-                in0=m_table[t][:].indirect(slot_list(j * CHUNK, CHUNK)),
-                in1=w_picked[t - 2][:, chunk(j)],
-                op=ALU.add,
-            )
-
-        nc.vector.tensor_copy(out=w_picked[0][:], in_=w_table[2][:].indirect(offsets[:]))
-        for j in range(CHUNKS):
-            add_high(2, j)
+            nc.scalar.copy(out=w2_by_d[j][:, :, 0:3], in_=w2_early[:, :, chunk(j)].rearrange("p t i -> p i t"))
         nc.vector.tensor_copy(out=w_picked[1][:], in_=w_table[3][:].indirect(offsets[:]))
 
         scores = [None] * CHUNKS
@@ -149,10 +140,38 @@ def tile_attend_gahead_sam_log_pl_kernel(tc, wT, mT, xT, y, ts, us, wt, offs, ou
         g_by_r = [sb("g_by_r%d" % j, [P, CHUNK, LANES], BF16) for j in range(CHUNKS)]
         g_codes = sb("g_codes", [P, SLOTS], U32)
         g_scales = sb("g_scales", [P, SLOTS], U8)
+        half = SLOTS // 2
+        nc.vector.memset(g_codes[:, half:], 0)
+        nc.vector.memset(g_scales[:, half:], 0)
+        dw = [sb("dw%d" % t, [P, SLOTS], F32) for t in range(LANES)]
+
+        def table_gradient(t, bank, slots, into):
+            features = slice(t * P, (t + 1) * P)
+            sums = psum.tile([P, SLOTS], F32, name="sums_" + bank, tag=bank)
+            nc.tensor.matmul_mx(
+                out=sums[:],
+                lhsT=xr_codes[:, features].bitcast(E4M3),
+                lhsT_scale=xr_scales[:, features],
+                rhs=g_codes[:].bitcast(E5M2),
+                rhs_scale=g_scales[:],
+                start=True,
+                stop=True,
+            )
+            nc.scalar.copy(out=into[:, slots], in_=sums[:, slots])
+
+        def scatter(t, slots, source):
+            nc.vector.tensor_copy(
+                out=window[t][:].indirect(slot_list(slots.start, slots.stop - slots.start)), in_=source[:, slots]
+            )
 
         def finish_w2(j):
-            add_high(3, j)
-            nc.scalar.copy(out=w2_by_d[j][:, :, 2:4], in_=w2_high[j][:].rearrange("p e i -> p i e"))
+            nc.vector.tensor_tensor(
+                out=w2_last[j][:],
+                in0=m_table[3][:].indirect(slot_list(j * CHUNK, CHUNK)),
+                in1=w_picked[1][:, chunk(j)],
+                op=ALU.add,
+            )
+            nc.scalar.copy(out=w2_by_d[j][:, :, 3], in_=w2_last[j][:])
 
         def score(j):
             nc.vector.quantize_mx(
@@ -215,6 +234,8 @@ def tile_attend_gahead_sam_log_pl_kernel(tc, wT, mT, xT, y, ts, us, wt, offs, ou
         residual(3)
         gradient(2)
         gradient(3)
+        dw_early = keep.tile([P, half], F32, name="dw_early", tag="work3", align_bytes=64)
+        table_gradient(0, "a0", slice(0, half), dw_early)
         quantise_g(2)
         quantise_g(3)
 
@@ -225,27 +246,17 @@ def tile_attend_gahead_sam_log_pl_kernel(tc, wT, mT, xT, y, ts, us, wt, offs, ou
             return slice(k * PIECE, (k + 1) * PIECE)
 
         def round_plane(t, k):
-            nc.scalar.copy(out=pairs[k][:, t // 2, :, t % 2], in_=window[t][:, piece(k)])
+            copy = nc.vector.tensor_copy if t >= 2 and k < VECTOR_PIECES else nc.scalar.copy
+            copy(out=pairs[k][:, t // 2, :, t % 2], in_=window[t][:, piece(k)])
 
-        dw = [sb("dw%d" % t, [P, SLOTS], F32) for t in range(LANES)]
         for t in range(LANES):
-            features = slice(t * P, (t + 1) * P)
-            sums = psum.tile([P, SLOTS], F32, name="sums%d" % t, tag="b%d" % t)
-            nc.tensor.matmul_mx(
-                out=sums[:],
-                lhsT=xr_codes[:, features].bitcast(E4M3),
-                lhsT_scale=xr_scales[:, features],
-                rhs=g_codes[:].bitcast(E5M2),
-                rhs_scale=g_scales[:],
-                start=True,
-                stop=True,
-            )
-            nc.scalar.copy(out=dw[t][:], in_=sums[:])
+            table_gradient(t, "b%d" % t, slice(half if t == 0 else 0, SLOTS), dw[t])
+        scatter(0, slice(0, half), dw_early)
         for t in range(LANES):
-            nc.vector.tensor_copy(out=window[t][:].indirect(offsets[:]), in_=dw[t][:])
+            scatter(t, slice(half if t == 0 else 0, SLOTS), dw[t])
             nc.sync.dma_start(out=out_rows[:, t, :], in_=window[t][:])
             if t < LANES - 1:
-                for k in range(PIECES):
+                for k in range(VECTOR_PIECES if t == 2 else 0, PIECES):
                     round_plane(t, k)
 
         out_by_d = [sb("out_by_d%d" % k, [P, PIECE * LANES], BF16) for k in range(PIECES)]
@@ -262,17 +273,19 @@ def tile_attend_gahead_sam_log_pl_kernel(tc, wT, mT, xT, y, ts, us, wt, offs, ou
                 nc.scalar.copy(out=words_out, in_=words_in)
 
         def quantise_out(k):
-            half = slice((k % 2) * PIECE, (k % 2 + 1) * PIECE)
+            side = slice((k % 2) * PIECE, (k % 2 + 1) * PIECE)
             nc.vector.quantize_mx(
-                out=out_codes[k // 2][:, half].bitcast(E4M3), scales=out_scales[:, piece(k)], in_=out_by_d[k][:]
+                out=out_codes[k // 2][:, side].bitcast(E4M3), scales=out_scales[:, piece(k)], in_=out_by_d[k][:]
             )
             if k % 2 == 1:
                 nc.sync.dma_start(
                     out=code_rows[:, (k - 1) * PIECE : (k + 1) * PIECE], in_=out_codes[k // 2][:].bitcast(I32)
                 )
 
+        for k in range(VECTOR_PIECES):
+            round_plane(2, k)
         for k in range(PIECES):
-            round_plane(LANES - 1, k)
+            round_plane(3, k)
         for k in range(PIECES + 1):
             if k < PIECES:
                 weave(k)

@@ -25,6 +25,8 @@ PIECE = 256
 PIECES = COLS // PIECE
 SCALAR_PIECES = 3
 VECTOR_PIECES = 2
+FOLD = COLS // P
+TURNED = (2, 3)
 
 
 def tile_attend_gahead_sam_log_pl_kernel(tc, wT, mT, xT, y, ts, us, wt, offs, out_0, out_1, out_2):
@@ -48,11 +50,10 @@ def tile_attend_gahead_sam_log_pl_kernel(tc, wT, mT, xT, y, ts, us, wt, offs, ou
         wt_col = sb("wt_col", [P, LANES], F32)
         nc.scalar.dma_start(out=us_col[:], in_=us.rearrange("(p u) one -> p (u one)", u=LANES))
         nc.scalar.dma_start(out=wt_col[:], in_=wt.rearrange("(p u) one -> p (u one)", u=LANES))
+        ts_folded = sb("ts_folded", [P, FOLD], F32)
+        nc.scalar.dma_start(out=ts_folded[:], in_=ts[0].rearrange("(n c) -> n c", c=FOLD))
         warm = sb("warm", [P, 1], F32)
         nc.scalar.activation(out=warm[:], in_=us_col[:, 0:1], func=ACT.Sigmoid)
-        ts_table = sb("ts_table", [P, COLS], F32)
-        nc.vector.memset(ts_table[:], 0.0)
-        nc.scalar.dma_start(out=ts_table[0:1, :], in_=ts[0:1, :])
 
         w_rows = wT.rearrange("(p t) c -> p t c", t=LANES)
         m_rows = mT.rearrange("(p t) c -> p t c", t=LANES)
@@ -72,7 +73,8 @@ def tile_attend_gahead_sam_log_pl_kernel(tc, wT, mT, xT, y, ts, us, wt, offs, ou
 
         window = [sb("window%d" % t, [P, COLS], F32) for t in range(LANES)]
         for t in range(LANES):
-            nc.vector.memset(window[t][:], 0.0)
+            engine = nc.vector if t < 2 else nc.gpsimd
+            engine.memset(window[t][:], 0.0)
 
         x_by_d = sb("x_by_d", [P, LANES, P, LANES], BF16)
         nc.scalar.copy(
@@ -97,22 +99,29 @@ def tile_attend_gahead_sam_log_pl_kernel(tc, wT, mT, xT, y, ts, us, wt, offs, ou
             out=xr_codes[:].bitcast(E4M3), scales=xr_scales[:], in_=x_by_r[:].rearrange("s t p u -> s (t p u)")
         )
 
-        ts_row = sb("ts_row", [P, SLOTS], F32)
-        nc.vector.tensor_copy(out=ts_row[:], in_=ts_table[:].indirect(offsets[:]))
-        ts_turned = psum.tile([P, CHUNKS, P], F32, name="ts_turned", tag="b0")
-        for j in range(CHUNKS):
-            nc.tensor.transpose(ts_turned[:, j, :], ts_row[:, j * P : (j + 1) * P], ident_f32[:])
-        ts_col = sb("ts_col", [P, CHUNKS], F32)
+        ts_table = sb("ts_table", [P, COLS], F32)
+        for b in range(FOLD // 4):
+            spread = psum.tile([P, 4, P], F32, name="spread%d" % b, tag="b%d" % b)
+            for c in range(4):
+                column = ts_folded[:, 4 * b + c : 4 * b + c + 1]
+                nc.tensor.transpose(spread[:, c, :], column.to_broadcast([P, P]), ident_f32[:])
+            nc.scalar.copy(
+                out=ts_table[:].rearrange("p (n c) -> p n c", c=FOLD)[:, :, 4 * b : 4 * b + 4],
+                in_=spread[:].rearrange("p c n -> p n c"),
+            )
+        ts_all = sb("ts_all", [P, SLOTS], F32)
+        nc.vector.tensor_copy(out=ts_all[:], in_=ts_table[:].indirect(offsets[:]))
+        ts_turned = psum.tile([P, len(TURNED), P], F32, name="ts_turned", tag="b0")
+        for n, j in enumerate(TURNED):
+            nc.tensor.transpose(ts_turned[:, n, :], ts_all[:, j * P : (j + 1) * P], ident_f32[:])
+        ts_col = sb("ts_col", [P, len(TURNED)], F32)
         nc.scalar.copy(out=ts_col[:], in_=ts_turned[:, :, 0])
-        ts_all = psum.tile([P, SLOTS], F32, name="ts_all", tag="b1")
-        for j in range(CHUNKS):
-            nc.tensor.transpose(ts_all[:, j * P : (j + 1) * P], ts_col[:, j : j + 1].to_broadcast([P, P]), ident_f32[:])
         wu_col = sb("wu_col", [P, LANES], F32)
         nc.vector.tensor_tensor(out=wu_col[:], in0=wt_col[:], in1=us_col[:], op=ALU.mult)
-        logit_scale = sb("logit_scale", [P, LANES, SLOTS], F32)
+        logit_scale = sb("logit_scale", [P, LANES, 2 * CHUNK], F32)
         grad_scale = sb("grad_scale", [P, LANES, SLOTS], F32)
         for u in range(LANES):
-            nc.scalar.activation(out=logit_scale[:, u, :], in_=ts_all[:], func=ACT.Copy, scale=us_col[:, u : u + 1])
+            nc.scalar.activation(out=logit_scale[:, u, :], in_=ts_all[:, : 2 * CHUNK], func=ACT.Copy, scale=us_col[:, u : u + 1])
         for u in range(LANES):
             nc.scalar.activation(out=grad_scale[:, u, :], in_=ts_all[:], func=ACT.Copy, scale=wu_col[:, u : u + 1])
 
@@ -178,6 +187,17 @@ def tile_attend_gahead_sam_log_pl_kernel(tc, wT, mT, xT, y, ts, us, wt, offs, ou
                 out=w2_codes[j][:].bitcast(E4M3), scales=w2_scales[j][:], in_=w2_by_d[j][:].rearrange("p i t -> p (i t)")
             )
             scores[j] = psum.tile([P, LANES, CHUNK], F32, name="scores%d" % j, tag="a%d" % j)
+            if j in TURNED:
+                nc.tensor.matmul_mx(
+                    out=scores[j][:].rearrange("i u s -> i (u s)"),
+                    lhsT=w2_codes[j][:].bitcast(E4M3),
+                    lhsT_scale=w2_scales[j][:],
+                    rhs=xd_codes[:].bitcast(E4M3),
+                    rhs_scale=xd_scales[:],
+                    start=True,
+                    stop=True,
+                )
+                return
             for u in range(LANES):
                 rows = slice(u * P, (u + 1) * P)
                 nc.tensor.matmul_mx(
@@ -193,6 +213,20 @@ def tile_attend_gahead_sam_log_pl_kernel(tc, wT, mT, xT, y, ts, us, wt, offs, ou
         def logits(j):
             nc.vector.tensor_tensor(out=work[j][:], in0=scores[j][:], in1=logit_scale[:, :, chunk(j)], op=ALU.mult)
             nc.scalar.activation(out=work[j][:], in_=work[j][:], func=ACT.Sigmoid)
+
+        def turn_logits(j):
+            n = TURNED.index(j)
+            scaled = sb("scaled%d" % j, [P, LANES, P], F32)
+            nc.scalar.activation(out=scaled[:], in_=scores[j][:], func=ACT.Copy, scale=ts_col[:, n : n + 1])
+            scores[j] = psum.tile([P, LANES, CHUNK], F32, name="back%d" % j, tag="b%d" % j)
+            for u in range(LANES):
+                nc.tensor.transpose(scores[j][:, u, :], scaled[:, u, :], ident_f32[:])
+
+        def turned_sigmoid(j):
+            for u in range(LANES):
+                nc.scalar.activation(
+                    out=work[j][:, u, :], in_=scores[j][:, u, :], func=ACT.Sigmoid, scale=us_col[:, u : u + 1]
+                )
 
         def residual(j):
             nc.vector.tensor_tensor(out=work[j][:], in0=work[j][:], in1=labels[:, :, chunk(j)], op=ALU.subtract)
@@ -219,18 +253,20 @@ def tile_attend_gahead_sam_log_pl_kernel(tc, wT, mT, xT, y, ts, us, wt, offs, ou
         finish_w2(3)
         score(1)
         score(2)
-        logits(0)
         score(3)
+        logits(0)
         logits(1)
+        turn_logits(2)
+        turn_logits(3)
+        turned_sigmoid(2)
+        turned_sigmoid(3)
         residual(0)
-        logits(2)
-        gradient(0)
         residual(1)
-        logits(3)
-        quantise_g(0)
+        gradient(0)
         gradient(1)
-        residual(2)
+        quantise_g(0)
         quantise_g(1)
+        residual(2)
         residual(3)
         gradient(2)
         gradient(3)
@@ -277,7 +313,9 @@ def tile_attend_gahead_sam_log_pl_kernel(tc, wT, mT, xT, y, ts, us, wt, offs, ou
             nc.vector.quantize_mx(
                 out=out_codes[k // 2][:, side].bitcast(E4M3), scales=out_scales[:, piece(k)], in_=out_by_d[k][:]
             )
-            if k % 2 == 1:
+            if k >= PIECES - 2:
+                nc.sync.dma_start(out=code_rows[:, piece(k)], in_=out_codes[k // 2][:, side].bitcast(I32))
+            elif k % 2 == 1:
                 nc.sync.dma_start(
                     out=code_rows[:, (k - 1) * PIECE : (k + 1) * PIECE], in_=out_codes[k // 2][:].bitcast(I32)
                 )

@@ -26,7 +26,7 @@ PIECES = COLS // PIECE
 SCALAR_PIECES = 3
 VECTOR_PIECES = 2
 FOLD = COLS // P
-TURNED = (2, 3)
+TURNED = (3,)
 
 
 def tile_attend_gahead_sam_log_pl_kernel(tc, wT, mT, xT, y, ts, us, wt, offs, out_0, out_1, out_2):
@@ -73,8 +73,7 @@ def tile_attend_gahead_sam_log_pl_kernel(tc, wT, mT, xT, y, ts, us, wt, offs, ou
 
         window = [sb("window%d" % t, [P, COLS], F32) for t in range(LANES)]
         for t in range(LANES):
-            engine = nc.vector if t < 2 else nc.gpsimd
-            engine.memset(window[t][:], 0.0)
+            nc.vector.memset(window[t][:], 0.0)
 
         x_by_d = sb("x_by_d", [P, LANES, P, LANES], BF16)
         nc.scalar.copy(
@@ -118,16 +117,15 @@ def tile_attend_gahead_sam_log_pl_kernel(tc, wT, mT, xT, y, ts, us, wt, offs, ou
         nc.scalar.copy(out=ts_col[:], in_=ts_turned[:, :, 0])
         wu_col = sb("wu_col", [P, LANES], F32)
         nc.vector.tensor_tensor(out=wu_col[:], in0=wt_col[:], in1=us_col[:], op=ALU.mult)
-        logit_scale = sb("logit_scale", [P, LANES, 2 * CHUNK], F32)
+        logit_scale = sb("logit_scale", [P, LANES, 3 * CHUNK], F32)
         grad_scale = sb("grad_scale", [P, LANES, SLOTS], F32)
         for u in range(LANES):
-            nc.scalar.activation(out=logit_scale[:, u, :], in_=ts_all[:, : 2 * CHUNK], func=ACT.Copy, scale=us_col[:, u : u + 1])
+            nc.scalar.activation(out=logit_scale[:, u, :], in_=ts_all[:, : 3 * CHUNK], func=ACT.Copy, scale=us_col[:, u : u + 1])
         for u in range(LANES):
             nc.scalar.activation(out=grad_scale[:, u, :], in_=ts_all[:], func=ACT.Copy, scale=wu_col[:, u : u + 1])
 
         w_picked = [keep.tile([P, SLOTS], F32, name="w_picked%d" % t, tag="w_picked%d" % (t % 2)) for t in range(2)]
         w2_early = sb("w2_early", [P, LANES - 1, SLOTS], F32)
-        w2_last = [sb("w2_last%d" % j, [P, CHUNK], F32) for j in range(CHUNKS)]
         w2_by_d = [sb("w2_by_d%d" % j, [P, CHUNK, LANES], BF16) for j in range(CHUNKS)]
         w2_codes = [sb("w2_codes%d" % j, [P, CHUNK], U32) for j in range(CHUNKS)]
         w2_scales = [sb("w2_scales%d" % j, [P, CHUNK], U8) for j in range(CHUNKS)]
@@ -174,13 +172,15 @@ def tile_attend_gahead_sam_log_pl_kernel(tc, wT, mT, xT, y, ts, us, wt, offs, ou
             )
 
         def finish_w2(j):
+            tag = "w2_by_d0" if j == CHUNKS - 1 else "w2_last%d" % j
+            w2_last = keep.tile([P, CHUNK], F32, name="w2_last%d" % j, tag=tag, align_bytes=64)
             nc.vector.tensor_tensor(
-                out=w2_last[j][:],
+                out=w2_last[:],
                 in0=m_table[3][:].indirect(slot_list(j * CHUNK, CHUNK)),
                 in1=w_picked[1][:, chunk(j)],
                 op=ALU.add,
             )
-            nc.scalar.copy(out=w2_by_d[j][:, :, 3], in_=w2_last[j][:])
+            nc.scalar.copy(out=w2_by_d[j][:, :, 3], in_=w2_last[:])
 
         def score(j):
             nc.vector.quantize_mx(
@@ -250,23 +250,22 @@ def tile_attend_gahead_sam_log_pl_kernel(tc, wT, mT, xT, y, ts, us, wt, offs, ou
         finish_w2(1)
         finish_w2(2)
         score(0)
-        finish_w2(3)
         score(1)
+        finish_w2(3)
         score(2)
-        score(3)
         logits(0)
+        score(3)
         logits(1)
-        turn_logits(2)
         turn_logits(3)
-        turned_sigmoid(2)
+        logits(2)
         turned_sigmoid(3)
         residual(0)
         residual(1)
         gradient(0)
         gradient(1)
+        residual(2)
         quantise_g(0)
         quantise_g(1)
-        residual(2)
         residual(3)
         gradient(2)
         gradient(3)
@@ -297,7 +296,7 @@ def tile_attend_gahead_sam_log_pl_kernel(tc, wT, mT, xT, y, ts, us, wt, offs, ou
 
         out_by_d = [sb("out_by_d%d" % k, [P, PIECE * LANES], BF16) for k in range(PIECES)]
         out_codes = [sb("out_codes%d" % h, [P, 2 * PIECE], U32) for h in range(PIECES // 2)]
-        out_scales = sb("out_scales", [P, COLS], U8)
+        out_scales = sb("out_scales", [P, 2 * PIECE], U8)
         code_rows = out_1[0].rearrange("p c l -> p (c l)").bitcast(I32)
 
         def weave(k):
@@ -311,7 +310,7 @@ def tile_attend_gahead_sam_log_pl_kernel(tc, wT, mT, xT, y, ts, us, wt, offs, ou
         def quantise_out(k):
             side = slice((k % 2) * PIECE, (k % 2 + 1) * PIECE)
             nc.vector.quantize_mx(
-                out=out_codes[k // 2][:, side].bitcast(E4M3), scales=out_scales[:, piece(k)], in_=out_by_d[k][:]
+                out=out_codes[k // 2][:, side].bitcast(E4M3), scales=out_scales[4 * (k // 2) :, side], in_=out_by_d[k][:]
             )
             if k >= PIECES - 2:
                 nc.sync.dma_start(out=code_rows[:, piece(k)], in_=out_codes[k // 2][:, side].bitcast(I32))
@@ -332,4 +331,7 @@ def tile_attend_gahead_sam_log_pl_kernel(tc, wT, mT, xT, y, ts, us, wt, offs, ou
         scale_rows = out_2[0].bitcast(I32)
         for q in range(4):
             queue = nc.sync if q % 2 == 0 else nc.scalar
-            queue.dma_start(out=scale_rows[4 * q : 4 * q + 4, :], in_=out_scales[32 * q : 32 * q + 4, :].bitcast(I32))
+            queue.dma_start(
+                out=scale_rows[4 * q : 4 * q + 4, :].rearrange("j (h c) -> h j c", h=4),
+                in_=out_scales[32 * q : 32 * q + 16, :].bitcast(I32),
+            )

@@ -23,8 +23,6 @@ CHUNK = 128
 CHUNKS = SLOTS // CHUNK
 PIECE = 256
 PIECES = COLS // PIECE
-SCALAR_PIECES = 3
-VECTOR_PIECES = 2
 FOLD = COLS // P
 TURNED = (3,)
 
@@ -275,14 +273,22 @@ def tile_attend_gahead_sam_log_pl_kernel(tc, wT, mT, xT, y, ts, us, wt, offs, ou
         quantise_g(3)
 
         out_rows = out_0.rearrange("(p t) c -> p t c", t=LANES)
-        pairs = [sb("pairs%d" % k, [P, 2, PIECE, 2], BF16) for k in range(PIECES)]
+        out_by_d = [sb("out_by_d%d" % h, [P, COLS // 2, LANES], BF16) for h in range(2)]
+
+        def round_early(t):
+            width = 2 if t == 2 else 1
+            left = window[t][:, : COLS // 2].unsqueeze(2).to_broadcast([P, COLS // 2, width])
+            right = window[t][:, COLS // 2 :].unsqueeze(2).to_broadcast([P, COLS // 2, width])
+            nc.scalar.copy(out=out_by_d[0][:, :, t : t + width], in_=left)
+            nc.gpsimd.tensor_scalar(
+                out=out_by_d[1][:, :, t : t + width], in0=right, scalar1=1.0, scalar2=0.0, op0=ALU.mult, op1=ALU.add
+            )
 
         def piece(k):
             return slice(k * PIECE, (k + 1) * PIECE)
 
-        def round_plane(t, k):
-            copy = nc.vector.tensor_copy if t >= 2 and k < VECTOR_PIECES else nc.scalar.copy
-            copy(out=pairs[k][:, t // 2, :, t % 2], in_=window[t][:, piece(k)])
+        def piece_by_d(k):
+            return out_by_d[k // (PIECES // 2)][:, piece(k % (PIECES // 2)), :]
 
         for t in range(LANES):
             table_gradient(t, "b%d" % t, slice(half if t == 0 else 0, SLOTS), dw[t])
@@ -291,26 +297,23 @@ def tile_attend_gahead_sam_log_pl_kernel(tc, wT, mT, xT, y, ts, us, wt, offs, ou
             scatter(t, slice(half if t == 0 else 0, SLOTS), dw[t])
             nc.sync.dma_start(out=out_rows[:, t, :], in_=window[t][:])
             if t < LANES - 1:
-                for k in range(VECTOR_PIECES if t == 2 else 0, PIECES):
-                    round_plane(t, k)
+                round_early(t)
 
-        out_by_d = [sb("out_by_d%d" % k, [P, PIECE * LANES], BF16) for k in range(PIECES)]
-        out_codes = [sb("out_codes%d" % h, [P, 2 * PIECE], U32) for h in range(PIECES // 2)]
+        out_codes = [
+            keep.tile([P, 2 * PIECE], U32, name="out_codes%d" % h, tag="window2" if h == 0 else "out_codes%d" % h, align_bytes=64)
+            for h in range(PIECES // 2)
+        ]
         out_scales = sb("out_scales", [P, 2 * PIECE], U8)
         code_rows = out_1[0].rearrange("p c l -> p (c l)").bitcast(I32)
 
-        def weave(k):
-            words_in = pairs[k][:].rearrange("p h c e -> p (h c e)").bitcast(F32).rearrange("p (h c) -> p c h", h=2)
-            words_out = out_by_d[k][:].bitcast(F32).rearrange("p (c h) -> p c h", h=2)
-            if k < PIECES - SCALAR_PIECES:
-                nc.vector.tensor_copy(out=words_out, in_=words_in)
-            else:
-                nc.scalar.copy(out=words_out, in_=words_in)
+        def round_last(k):
+            copy = nc.vector.tensor_copy if k % 2 == 0 else nc.scalar.copy
+            copy(out=piece_by_d(k)[:, :, LANES - 1], in_=window[LANES - 1][:, piece(k)])
 
         def quantise_out(k):
             side = slice((k % 2) * PIECE, (k % 2 + 1) * PIECE)
             nc.vector.quantize_mx(
-                out=out_codes[k // 2][:, side].bitcast(E4M3), scales=out_scales[4 * (k // 2) :, side], in_=out_by_d[k][:]
+                out=out_codes[k // 2][:, side].bitcast(E4M3), scales=out_scales[4 * (k // 2) :, side], in_=piece_by_d(k).rearrange("p c t -> p (c t)")
             )
             if k >= PIECES - 2:
                 nc.sync.dma_start(out=code_rows[:, piece(k)], in_=out_codes[k // 2][:, side].bitcast(I32))
@@ -319,15 +322,14 @@ def tile_attend_gahead_sam_log_pl_kernel(tc, wT, mT, xT, y, ts, us, wt, offs, ou
                     out=code_rows[:, (k - 1) * PIECE : (k + 1) * PIECE], in_=out_codes[k // 2][:].bitcast(I32)
                 )
 
-        for k in range(VECTOR_PIECES):
-            round_plane(2, k)
-        for k in range(PIECES):
-            round_plane(3, k)
-        for k in range(PIECES + 1):
-            if k < PIECES:
-                weave(k)
-            if k > 0:
-                quantise_out(k - 1)
+        round_last(0)
+        round_last(1)
+        for k in range(0, PIECES, 2):
+            if k + 2 < PIECES:
+                round_last(k + 2)
+                round_last(k + 3)
+            quantise_out(k)
+            quantise_out(k + 1)
         scale_rows = out_2[0].bitcast(I32)
         for q in range(4):
             queue = nc.sync if q % 2 == 0 else nc.scalar

@@ -23,8 +23,10 @@ CHUNK = 128
 CHUNKS = SLOTS // CHUNK
 PIECE = 256
 PIECES = COLS // PIECE
+PAIRED_PIECES = 3
+GPSIMD_COLS = 448
 FOLD = COLS // P
-TURNED = (3,)
+TURNED = (2, 3)
 
 
 def tile_attend_gahead_sam_log_pl_kernel(tc, wT, mT, xT, y, ts, us, wt, offs, out_0, out_1, out_2):
@@ -33,8 +35,8 @@ def tile_attend_gahead_sam_log_pl_kernel(tc, wT, mT, xT, y, ts, us, wt, offs, ou
         keep = ctx.enter_context(tc.tile_pool(name="keep", bufs=1))
         psum = ctx.enter_context(tc.psum_pool(name="psum", bufs=1))
 
-        def sb(name, shape, dtype):
-            return keep.tile(shape, dtype, name=name, align_bytes=64)
+        def sb(name, shape, dtype, tag=None):
+            return keep.tile(shape, dtype, name=name, tag=tag or name, align_bytes=64)
 
         def slot_list(first, count):
             return offsets[:, first // 16 : (first + count) // 16]
@@ -113,14 +115,29 @@ def tile_attend_gahead_sam_log_pl_kernel(tc, wT, mT, xT, y, ts, us, wt, offs, ou
             nc.tensor.transpose(ts_turned[:, n, :], ts_all[:, j * P : (j + 1) * P], ident_f32[:])
         ts_col = sb("ts_col", [P, len(TURNED)], F32)
         nc.scalar.copy(out=ts_col[:], in_=ts_turned[:, :, 0])
+        minus_ts_col = sb("minus_ts_col", [P, len(TURNED)], F32)
+        nc.scalar.activation(out=minus_ts_col[:], in_=ts_turned[:, :, 0], func=ACT.Copy, scale=-1.0)
+        minus_us_col = sb("minus_us_col", [P, LANES], F32)
+        nc.scalar.activation(out=minus_us_col[:], in_=us_col[:], func=ACT.Copy, scale=-1.0)
         wu_col = sb("wu_col", [P, LANES], F32)
         nc.vector.tensor_tensor(out=wu_col[:], in0=wt_col[:], in1=us_col[:], op=ALU.mult)
-        logit_scale = sb("logit_scale", [P, LANES, 3 * CHUNK], F32)
-        grad_scale = sb("grad_scale", [P, LANES, SLOTS], F32)
+        logit_scale = sb("logit_scale", [P, LANES, 2 * CHUNK], F32)
+        grad_scale = sb("grad_scale", [P, LANES, 2 * CHUNK], F32)
         for u in range(LANES):
-            nc.scalar.activation(out=logit_scale[:, u, :], in_=ts_all[:, : 3 * CHUNK], func=ACT.Copy, scale=us_col[:, u : u + 1])
+            nc.scalar.activation(out=logit_scale[:, u, :], in_=ts_all[:, : 2 * CHUNK], func=ACT.Copy, scale=us_col[:, u : u + 1])
         for u in range(LANES):
-            nc.scalar.activation(out=grad_scale[:, u, :], in_=ts_all[:], func=ACT.Copy, scale=wu_col[:, u : u + 1])
+            nc.scalar.activation(out=grad_scale[:, u, :], in_=ts_all[:, : 2 * CHUNK], func=ACT.Copy, scale=wu_col[:, u : u + 1])
+        wu_rows = psum.tile([P, LANES, P], F32, name="wu_rows", tag="b1")
+        for u in range(LANES):
+            nc.tensor.transpose(wu_rows[:, u, :], wu_col[:, u : u + 1].to_broadcast([P, P]), ident_f32[:])
+        minus_scale = [sb("minus_scale%d" % j, [P, 2, P, 2], F32) for j in TURNED]
+        for n in range(len(TURNED)):
+            nc.scalar.activation(
+                out=minus_scale[n][:],
+                in_=wu_rows[:].rearrange("i (h e) s -> i h s e", e=2),
+                func=ACT.Copy,
+                scale=minus_ts_col[:, n : n + 1],
+            )
 
         w_picked = [keep.tile([P, SLOTS], F32, name="w_picked%d" % t, tag="w_picked%d" % (t % 2)) for t in range(2)]
         w2_early = sb("w2_early", [P, LANES - 1, SLOTS], F32)
@@ -152,7 +169,7 @@ def tile_attend_gahead_sam_log_pl_kernel(tc, wT, mT, xT, y, ts, us, wt, offs, ou
 
         def table_gradient(t, bank, slots, into):
             features = slice(t * P, (t + 1) * P)
-            sums = psum.tile([P, SLOTS], F32, name="sums_" + bank, tag=bank)
+            sums = psum.tile([P, SLOTS], F32, name="sums%d_%s" % (t, bank), tag=bank)
             nc.tensor.matmul_mx(
                 out=sums[:],
                 lhsT=xr_codes[:, features].bitcast(E4M3),
@@ -223,8 +240,47 @@ def tile_attend_gahead_sam_log_pl_kernel(tc, wT, mT, xT, y, ts, us, wt, offs, ou
         def turned_sigmoid(j):
             for u in range(LANES):
                 nc.scalar.activation(
-                    out=work[j][:, u, :], in_=scores[j][:, u, :], func=ACT.Sigmoid, scale=us_col[:, u : u + 1]
+                    out=work[j][:, u, :], in_=scores[j][:, u, :], func=ACT.Sigmoid, scale=minus_us_col[:, u : u + 1]
                 )
+
+        misses = {}
+
+        def turn_labels(j):
+            misses[j] = psum.tile([P, LANES, P], F32, name="misses%d" % j, tag="b%d" % (j - 2))
+            for u in range(LANES):
+                nc.tensor.matmul(
+                    misses[j][:, u, :], labels[:, u, chunk(j)], ident_f32[:], start=(u == 0), stop=False, is_transpose=True
+                )
+
+        def add_sigmoid(j):
+            for u in range(LANES):
+                nc.tensor.matmul(
+                    misses[j][:, u, :], work[j][:, u, :], ident_f32[:], start=False, stop=(u == LANES - 1), is_transpose=True
+                )
+
+        g_turned = {}
+
+        def turned_gradient(j):
+            g_turned[j] = sb("g_turned%d" % j, [P, 2, P, 2], BF16)
+            for h in range(2):
+                nc.vector.scalar_tensor_tensor(
+                    out=g_turned[j][:, h, :, :],
+                    in0=misses[j][:, 2 * h : 2 * h + 2, :].rearrange("i e s -> i s e"),
+                    scalar=1.0,
+                    in1=minus_scale[TURNED.index(j)][:, h, :, :],
+                    op0=ALU.subtract,
+                    op1=ALU.mult,
+                )
+
+        def turn_gradient(j):
+            words = g_turned[j][:].rearrange("i h s e -> i (h s e)").bitcast(F32)
+            back = psum.tile([P, 2, P], F32, name="g_back%d" % j, tag="a%d" % j)
+            for h in range(2):
+                nc.tensor.transpose(back[:, h, :], words[:, h * P : (h + 1) * P], ident_f32[:])
+            nc.scalar.copy(
+                out=g_by_r[j][:].rearrange("s i u -> s (i u)").bitcast(F32).rearrange("s (i h) -> s i h", h=2),
+                in_=back[:].rearrange("s h i -> s i h"),
+            )
 
         def residual(j):
             nc.vector.tensor_tensor(out=work[j][:], in0=work[j][:], in1=labels[:, :, chunk(j)], op=ALU.subtract)
@@ -253,48 +309,63 @@ def tile_attend_gahead_sam_log_pl_kernel(tc, wT, mT, xT, y, ts, us, wt, offs, ou
         score(2)
         logits(0)
         score(3)
+        turn_logits(2)
         logits(1)
         turn_logits(3)
-        logits(2)
+        turn_labels(2)
+        turn_labels(3)
+        turned_sigmoid(2)
+        add_sigmoid(2)
         turned_sigmoid(3)
+        add_sigmoid(3)
         residual(0)
         residual(1)
         gradient(0)
         gradient(1)
-        residual(2)
         quantise_g(0)
         quantise_g(1)
-        residual(3)
-        gradient(2)
-        gradient(3)
-        dw_early = keep.tile([P, half], F32, name="dw_early", tag="work3", align_bytes=64)
-        table_gradient(0, "a0", slice(0, half), dw_early)
+        turned_gradient(2)
+        dw_early = [sb("dw_early%d" % t, [P, half], F32, ("x", "ts_table")[t]) for t in range(2)]
+        table_gradient(0, "a0", slice(0, half), dw_early[0])
+        turned_gradient(3)
+        turn_gradient(2)
+        turn_gradient(3)
+        table_gradient(1, "a3", slice(0, half), dw_early[1])
         quantise_g(2)
         quantise_g(3)
 
         out_rows = out_0.rearrange("(p t) c -> p t c", t=LANES)
-        out_by_d = [sb("out_by_d%d" % h, [P, COLS // 2, LANES], BF16) for h in range(2)]
+        paired = PAIRED_PIECES * PIECE
+        pairs = sb("pairs", [P, 2, paired, 2], BF16)
+        woven = [sb("woven%d" % k, [P, PIECE, LANES], BF16) for k in range(PAIRED_PIECES)]
+        in_lanes = sb("in_lanes", [P, COLS - paired, LANES], BF16)
+
+        def lanes_of(first, last):
+            return in_lanes[:, first - paired : last - paired, :]
+
+        def gpsimd_round(out, t, first, last, width):
+            source = window[t][:, first:last].unsqueeze(2).to_broadcast([P, last - first, width])
+            nc.gpsimd.tensor_scalar(out=out, in0=source, scalar1=1.0, scalar2=0.0, op0=ALU.mult, op1=ALU.add)
 
         def round_early(t):
             width = 2 if t == 2 else 1
-            left = window[t][:, : COLS // 2].unsqueeze(2).to_broadcast([P, COLS // 2, width])
-            right = window[t][:, COLS // 2 :].unsqueeze(2).to_broadcast([P, COLS // 2, width])
-            nc.scalar.copy(out=out_by_d[0][:, :, t : t + width], in_=left)
-            nc.gpsimd.tensor_scalar(
-                out=out_by_d[1][:, :, t : t + width], in0=right, scalar1=1.0, scalar2=0.0, op0=ALU.mult, op1=ALU.add
-            )
+            split = COLS - (PIECE if t == 2 else GPSIMD_COLS)
+            nc.scalar.copy(out=lanes_of(paired, split)[:, :, t], in_=window[t][:, paired:split])
+            gpsimd_round(pairs[:, t // 2, :, t % 2 : t % 2 + width], t, 0, paired, width)
+            gpsimd_round(lanes_of(split, COLS)[:, :, t : t + width], t, split, COLS, width)
 
         def piece(k):
             return slice(k * PIECE, (k + 1) * PIECE)
 
         def piece_by_d(k):
-            return out_by_d[k // (PIECES // 2)][:, piece(k % (PIECES // 2)), :]
+            return woven[k][:] if k < PAIRED_PIECES else lanes_of(k * PIECE, (k + 1) * PIECE)
 
         for t in range(LANES):
-            table_gradient(t, "b%d" % t, slice(half if t == 0 else 0, SLOTS), dw[t])
-        scatter(0, slice(0, half), dw_early)
+            table_gradient(t, ("b0", "a1", "b2", "b3")[t], slice(half if t < 2 else 0, SLOTS), dw[t])
+        scatter(0, slice(0, half), dw_early[0])
+        scatter(1, slice(0, half), dw_early[1])
         for t in range(LANES):
-            scatter(t, slice(half if t == 0 else 0, SLOTS), dw[t])
+            scatter(t, slice(half if t < 2 else 0, SLOTS), dw[t])
             nc.sync.dma_start(out=out_rows[:, t, :], in_=window[t][:])
             if t < LANES - 1:
                 round_early(t)
@@ -306,9 +377,12 @@ def tile_attend_gahead_sam_log_pl_kernel(tc, wT, mT, xT, y, ts, us, wt, offs, ou
         out_scales = sb("out_scales", [P, 2 * PIECE], U8)
         code_rows = out_1[0].rearrange("p c l -> p (c l)").bitcast(I32)
 
-        def round_last(k):
-            copy = nc.vector.tensor_copy if k % 2 == 0 else nc.scalar.copy
-            copy(out=piece_by_d(k)[:, :, LANES - 1], in_=window[LANES - 1][:, piece(k)])
+        def weave(k):
+            words = pairs[:].rearrange("p h c e -> p (h c e)").bitcast(F32).rearrange("p (h c) -> p c h", h=2)
+            nc.vector.tensor_copy(
+                out=woven[k][:].rearrange("p c t -> p (c t)").bitcast(F32).rearrange("p (c h) -> p c h", h=2),
+                in_=words[:, piece(k), :],
+            )
 
         def quantise_out(k):
             side = slice((k % 2) * PIECE, (k % 2 + 1) * PIECE)
@@ -322,14 +396,18 @@ def tile_attend_gahead_sam_log_pl_kernel(tc, wT, mT, xT, y, ts, us, wt, offs, ou
                     out=code_rows[:, (k - 1) * PIECE : (k + 1) * PIECE], in_=out_codes[k // 2][:].bitcast(I32)
                 )
 
-        round_last(0)
-        round_last(1)
-        for k in range(0, PIECES, 2):
-            if k + 2 < PIECES:
-                round_last(k + 2)
-                round_last(k + 3)
+        last = window[LANES - 1]
+        middle = COLS - PIECE // 2
+        nc.vector.tensor_copy(out=pairs[:, 1, :, 1], in_=last[:, :paired])
+        nc.vector.tensor_copy(out=lanes_of(middle, COLS)[:, :, LANES - 1], in_=last[:, middle:])
+        for first in range(paired, middle, PIECE):
+            end = min(first + PIECE, middle)
+            nc.scalar.copy(out=lanes_of(first, end)[:, :, LANES - 1], in_=last[:, first:end])
+        weave(0)
+        for k in range(PIECES):
+            if k + 1 < PAIRED_PIECES:
+                weave(k + 1)
             quantise_out(k)
-            quantise_out(k + 1)
         scale_rows = out_2[0].bitcast(I32)
         for q in range(4):
             queue = nc.sync if q % 2 == 0 else nc.scalar

@@ -23,8 +23,8 @@ CHUNK = 128
 CHUNKS = SLOTS // CHUNK
 PIECE = 256
 PIECES = COLS // PIECE
-PAIRED_PIECES = 3
-GPSIMD_COLS = 448
+VECTOR_PIECES = 2
+GPSIMD_COLS = 1152
 FOLD = COLS // P
 TURNED = (2, 3)
 
@@ -163,28 +163,29 @@ def tile_attend_gahead_sam_log_pl_kernel(tc, wT, mT, xT, y, ts, us, wt, offs, ou
         g_codes = sb("g_codes", [P, SLOTS], U32)
         g_scales = sb("g_scales", [P, SLOTS], U8)
         half = SLOTS // 2
-        nc.vector.memset(g_codes[:, half:], 0)
-        nc.vector.memset(g_scales[:, half:], 0)
+        first_half, second_half, every_slot = slice(0, half), slice(half, SLOTS), slice(0, SLOTS)
         dw = [sb("dw%d" % t, [P, SLOTS], F32) for t in range(LANES)]
 
-        def table_gradient(t, bank, slots, into):
+        def table_gradient(t, bank, slots, into, copy):
             features = slice(t * P, (t + 1) * P)
-            sums = psum.tile([P, SLOTS], F32, name="sums%d_%s" % (t, bank), tag=bank)
+            sums = psum.tile([P, slots.stop - slots.start], F32, name="sums%d_%s" % (t, bank), tag=bank)
             nc.tensor.matmul_mx(
                 out=sums[:],
                 lhsT=xr_codes[:, features].bitcast(E4M3),
                 lhsT_scale=xr_scales[:, features],
-                rhs=g_codes[:].bitcast(E5M2),
-                rhs_scale=g_scales[:],
+                rhs=g_codes[:, slots].bitcast(E5M2),
+                rhs_scale=g_scales[:, slots],
                 start=True,
                 stop=True,
             )
-            nc.scalar.copy(out=into[:, slots], in_=sums[:, slots])
+            copy(out=into[:, slots], in_=sums[:])
 
         def scatter(t, slots, source):
-            nc.vector.tensor_copy(
-                out=window[t][:].indirect(slot_list(slots.start, slots.stop - slots.start)), in_=source[:, slots]
-            )
+            out = window[t][:].indirect(slot_list(slots.start, slots.stop - slots.start))
+            if t % 2 == 0:
+                nc.vector.tensor_copy(out=out, in_=source[:, slots])
+            else:
+                nc.scalar.activation(out=out, in_=source[:, slots], func=ACT.Copy)
 
         def finish_w2(j):
             tag = "w2_by_d0" if j == CHUNKS - 1 else "w2_last%d" % j
@@ -326,59 +327,60 @@ def tile_attend_gahead_sam_log_pl_kernel(tc, wT, mT, xT, y, ts, us, wt, offs, ou
         quantise_g(1)
         turned_gradient(2)
         dw_early = [sb("dw_early%d" % t, [P, half], F32, ("x", "ts_table")[t]) for t in range(2)]
-        table_gradient(0, "a0", slice(0, half), dw_early[0])
+        table_gradient(0, "a0", first_half, dw_early[0], nc.scalar.copy)
         turned_gradient(3)
         turn_gradient(2)
         turn_gradient(3)
-        table_gradient(1, "a3", slice(0, half), dw_early[1])
+        table_gradient(1, "a3", first_half, dw_early[1], nc.scalar.copy)
         quantise_g(2)
         quantise_g(3)
 
         out_rows = out_0.rearrange("(p t) c -> p t c", t=LANES)
-        paired = PAIRED_PIECES * PIECE
-        pairs = sb("pairs", [P, 2, paired, 2], BF16)
-        woven = [sb("woven%d" % k, [P, PIECE, LANES], BF16) for k in range(PAIRED_PIECES)]
-        in_lanes = sb("in_lanes", [P, COLS - paired, LANES], BF16)
-
-        def lanes_of(first, last):
-            return in_lanes[:, first - paired : last - paired, :]
-
-        def gpsimd_round(out, t, first, last, width):
-            source = window[t][:, first:last].unsqueeze(2).to_broadcast([P, last - first, width])
-            nc.gpsimd.tensor_scalar(out=out, in0=source, scalar1=1.0, scalar2=0.0, op0=ALU.mult, op1=ALU.add)
-
-        def round_early(t):
-            width = 2 if t == 2 else 1
-            split = COLS - (PIECE if t == 2 else GPSIMD_COLS)
-            nc.scalar.copy(out=lanes_of(paired, split)[:, :, t], in_=window[t][:, paired:split])
-            gpsimd_round(pairs[:, t // 2, :, t % 2 : t % 2 + width], t, 0, paired, width)
-            gpsimd_round(lanes_of(split, COLS)[:, :, t : t + width], t, split, COLS, width)
+        pair_words = sb("pair_words", [P, 2, COLS, 2], BF16)
+        woven = [sb("woven%d" % k, [P, PIECE, LANES], BF16, ("w_table%d", "m_table%d")[k % 2] % (k // 2)) for k in range(PIECES)]
 
         def piece(k):
             return slice(k * PIECE, (k + 1) * PIECE)
 
-        def piece_by_d(k):
-            return woven[k][:] if k < PAIRED_PIECES else lanes_of(k * PIECE, (k + 1) * PIECE)
+        def store_plane(t):
+            queue = nc.sync if t % 2 == 0 else nc.scalar
+            queue.dma_start(out=out_rows[:, t, :], in_=window[t][:])
 
-        for t in range(LANES):
-            table_gradient(t, ("b0", "a1", "b2", "b3")[t], slice(half if t < 2 else 0, SLOTS), dw[t])
-        scatter(0, slice(0, half), dw_early[0])
-        scatter(1, slice(0, half), dw_early[1])
-        for t in range(LANES):
-            scatter(t, slice(half if t < 2 else 0, SLOTS), dw[t])
-            nc.sync.dma_start(out=out_rows[:, t, :], in_=window[t][:])
-            if t < LANES - 1:
-                round_early(t)
+        scatter(0, first_half, dw_early[0])
+        scatter(1, first_half, dw_early[1])
+        table_gradient(0, "b0", second_half, dw[0], nc.vector.tensor_copy)
+        table_gradient(1, "a1", second_half, dw[1], nc.scalar.copy)
+        scatter(0, second_half, dw[0])
+        scatter(1, second_half, dw[1])
+        store_plane(0)
+        store_plane(1)
+        table_gradient(2, "b2", every_slot, dw[2], nc.vector.tensor_copy)
+        table_gradient(3, "b3", every_slot, dw[3], nc.scalar.copy)
+        scatter(2, every_slot, dw[2])
+        scatter(3, first_half, dw[3])
+        scatter(3, second_half, dw[3])
+        store_plane(2)
+        store_plane(3)
 
-        out_codes = [
-            keep.tile([P, 2 * PIECE], U32, name="out_codes%d" % h, tag="window2" if h == 0 else "out_codes%d" % h, align_bytes=64)
-            for h in range(PIECES // 2)
-        ]
+        for t in range(2):
+            nc.gpsimd.tensor_scalar(
+                out=pair_words[:, 0, :GPSIMD_COLS, t], in0=window[t][:, :GPSIMD_COLS], scalar1=1.0, scalar2=0.0, op0=ALU.mult, op1=ALU.add
+            )
+        for t in range(2):
+            nc.vector.tensor_copy(out=pair_words[:, 0, GPSIMD_COLS:, t], in_=window[t][:, GPSIMD_COLS:])
+        vector_cols = VECTOR_PIECES * PIECE
+        for t in range(2, LANES):
+            nc.vector.tensor_copy(out=pair_words[:, 1, :vector_cols, t % 2], in_=window[t][:, :vector_cols])
+        for k in range(VECTOR_PIECES, PIECES):
+            for t in range(2, LANES):
+                nc.scalar.copy(out=pair_words[:, 1, piece(k), t % 2], in_=window[t][:, piece(k)])
+
+        out_codes = [sb("out_codes%d" % h, [P, 2 * PIECE], U32) for h in range(PIECES // 2)]
         out_scales = sb("out_scales", [P, 2 * PIECE], U8)
         code_rows = out_1[0].rearrange("p c l -> p (c l)").bitcast(I32)
 
         def weave(k):
-            words = pairs[:].rearrange("p h c e -> p (h c e)").bitcast(F32).rearrange("p (h c) -> p c h", h=2)
+            words = pair_words[:].rearrange("p h c e -> p (h c e)").bitcast(F32).rearrange("p (h c) -> p c h", h=2)
             nc.vector.tensor_copy(
                 out=woven[k][:].rearrange("p c t -> p (c t)").bitcast(F32).rearrange("p (c h) -> p c h", h=2),
                 in_=words[:, piece(k), :],
@@ -387,7 +389,9 @@ def tile_attend_gahead_sam_log_pl_kernel(tc, wT, mT, xT, y, ts, us, wt, offs, ou
         def quantise_out(k):
             side = slice((k % 2) * PIECE, (k % 2 + 1) * PIECE)
             nc.vector.quantize_mx(
-                out=out_codes[k // 2][:, side].bitcast(E4M3), scales=out_scales[4 * (k // 2) :, side], in_=piece_by_d(k).rearrange("p c t -> p (c t)")
+                out=out_codes[k // 2][:, side].bitcast(E4M3),
+                scales=out_scales[4 * (k // 2) :, side],
+                in_=woven[k][:].rearrange("p c t -> p (c t)"),
             )
             if k >= PIECES - 2:
                 nc.sync.dma_start(out=code_rows[:, piece(k)], in_=out_codes[k // 2][:, side].bitcast(I32))
@@ -396,16 +400,9 @@ def tile_attend_gahead_sam_log_pl_kernel(tc, wT, mT, xT, y, ts, us, wt, offs, ou
                     out=code_rows[:, (k - 1) * PIECE : (k + 1) * PIECE], in_=out_codes[k // 2][:].bitcast(I32)
                 )
 
-        last = window[LANES - 1]
-        middle = COLS - PIECE // 2
-        nc.vector.tensor_copy(out=pairs[:, 1, :, 1], in_=last[:, :paired])
-        nc.vector.tensor_copy(out=lanes_of(middle, COLS)[:, :, LANES - 1], in_=last[:, middle:])
-        for first in range(paired, middle, PIECE):
-            end = min(first + PIECE, middle)
-            nc.scalar.copy(out=lanes_of(first, end)[:, :, LANES - 1], in_=last[:, first:end])
         weave(0)
         for k in range(PIECES):
-            if k + 1 < PAIRED_PIECES:
+            if k + 1 < PIECES:
                 weave(k + 1)
             quantise_out(k)
         scale_rows = out_2[0].bitcast(I32)

@@ -23,8 +23,7 @@ CHUNK = 128
 CHUNKS = SLOTS // CHUNK
 PIECE = 256
 PIECES = COLS // PIECE
-VECTOR_PIECES = 2
-GPSIMD_COLS = 1152
+SCALAR_WEAVES = 3
 FOLD = COLS // P
 TURNED = (2, 3)
 
@@ -336,14 +335,15 @@ def tile_attend_gahead_sam_log_pl_kernel(tc, wT, mT, xT, y, ts, us, wt, offs, ou
         quantise_g(3)
 
         out_rows = out_0.rearrange("(p t) c -> p t c", t=LANES)
-        pair_words = sb("pair_words", [P, 2, COLS, 2], BF16)
+        shared_cols = COLS // 2
+        pair_words = [sb("pair_words%d" % side, [P, 2, shared_cols, 2], BF16, ("pair_words0", "dw3")[side]) for side in range(2)]
         woven = [sb("woven%d" % k, [P, PIECE, LANES], BF16, ("w_table%d", "m_table%d")[k % 2] % (k // 2)) for k in range(PIECES)]
 
         def piece(k):
             return slice(k * PIECE, (k + 1) * PIECE)
 
         def store_plane(t):
-            queue = nc.sync if t % 2 == 0 else nc.scalar
+            queue = nc.scalar if t % 2 else nc.sync
             queue.dma_start(out=out_rows[:, t, :], in_=window[t][:])
 
         scatter(0, first_half, dw_early[0])
@@ -355,35 +355,37 @@ def tile_attend_gahead_sam_log_pl_kernel(tc, wT, mT, xT, y, ts, us, wt, offs, ou
         store_plane(0)
         store_plane(1)
         table_gradient(2, "b2", every_slot, dw[2], nc.vector.tensor_copy)
-        table_gradient(3, "b3", every_slot, dw[3], nc.scalar.copy)
+        table_gradient(3, "b3", every_slot, dw[3], nc.vector.tensor_copy)
         scatter(2, every_slot, dw[2])
         scatter(3, first_half, dw[3])
         scatter(3, second_half, dw[3])
         store_plane(2)
         store_plane(3)
 
+        left, right = slice(0, shared_cols), slice(shared_cols, COLS)
         for t in range(2):
             nc.gpsimd.tensor_scalar(
-                out=pair_words[:, 0, :GPSIMD_COLS, t], in0=window[t][:, :GPSIMD_COLS], scalar1=1.0, scalar2=0.0, op0=ALU.mult, op1=ALU.add
+                out=pair_words[0][:, 0, :, t], in0=window[t][:, left], scalar1=1.0, scalar2=0.0, op0=ALU.mult, op1=ALU.add
             )
+        nc.vector.tensor_copy(out=pair_words[0][:, 1, :, 0], in_=window[2][:, left])
         for t in range(2):
-            nc.vector.tensor_copy(out=pair_words[:, 0, GPSIMD_COLS:, t], in_=window[t][:, GPSIMD_COLS:])
-        vector_cols = VECTOR_PIECES * PIECE
-        for t in range(2, LANES):
-            nc.vector.tensor_copy(out=pair_words[:, 1, :vector_cols, t % 2], in_=window[t][:, :vector_cols])
-        for k in range(VECTOR_PIECES, PIECES):
+            nc.vector.tensor_copy(out=pair_words[1][:, 0, :, t], in_=window[t][:, right])
+        nc.vector.tensor_copy(out=pair_words[0][:, 1, :, 1], in_=window[3][:, left])
+        for k in range(PIECES // 2, PIECES):
             for t in range(2, LANES):
-                nc.scalar.copy(out=pair_words[:, 1, piece(k), t % 2], in_=window[t][:, piece(k)])
+                nc.scalar.copy(out=pair_words[1][:, 1, piece(k - PIECES // 2), t % 2], in_=window[t][:, piece(k)])
 
         out_codes = [sb("out_codes%d" % h, [P, 2 * PIECE], U32) for h in range(PIECES // 2)]
         out_scales = sb("out_scales", [P, 2 * PIECE], U8)
         code_rows = out_1[0].rearrange("p c l -> p (c l)").bitcast(I32)
 
         def weave(k):
-            words = pair_words[:].rearrange("p h c e -> p (h c e)").bitcast(F32).rearrange("p (h c) -> p c h", h=2)
-            nc.vector.tensor_copy(
+            side, place = divmod(k, PIECES // 2)
+            words = pair_words[side][:].rearrange("p h c e -> p (h c e)").bitcast(F32).rearrange("p (h c) -> p c h", h=2)
+            copy = nc.scalar.copy if k >= PIECES - SCALAR_WEAVES else nc.vector.tensor_copy
+            copy(
                 out=woven[k][:].rearrange("p c t -> p (c t)").bitcast(F32).rearrange("p (c h) -> p c h", h=2),
-                in_=words[:, piece(k), :],
+                in_=words[:, piece(place), :],
             )
 
         def quantise_out(k):

@@ -23,7 +23,10 @@ CHUNK = 128
 CHUNKS = SLOTS // CHUNK
 PIECE = 256
 PIECES = COLS // PIECE
-SCALAR_WEAVES = 3
+WHOLE_WORDS = 32
+NEAR_PIECES = 4
+STORE_EDGES = (0, 4, 6, 7, 8)
+SCALAR_WEAVES = 4
 FOLD = COLS // P
 TURNED = (2, 3)
 
@@ -32,6 +35,7 @@ def tile_attend_gahead_sam_log_pl_kernel(tc, wT, mT, xT, y, ts, us, wt, offs, ou
     nc = tc.nc
     with ExitStack() as ctx:
         keep = ctx.enter_context(tc.tile_pool(name="keep", bufs=1))
+        relay = ctx.enter_context(tc.tile_pool(name="relay", bufs=1))
         psum = ctx.enter_context(tc.psum_pool(name="psum", bufs=1))
 
         def sb(name, shape, dtype, tag=None):
@@ -163,7 +167,7 @@ def tile_attend_gahead_sam_log_pl_kernel(tc, wT, mT, xT, y, ts, us, wt, offs, ou
         g_scales = sb("g_scales", [P, SLOTS], U8)
         half = SLOTS // 2
         first_half, second_half, every_slot = slice(0, half), slice(half, SLOTS), slice(0, SLOTS)
-        dw = [sb("dw%d" % t, [P, SLOTS], F32) for t in range(LANES)]
+        dw = [sb("dw%d" % t, [P, SLOTS], F32) for t in range(LANES - 1)]
 
         def table_gradient(t, bank, slots, into, copy):
             features = slice(t * P, (t + 1) * P)
@@ -179,9 +183,9 @@ def tile_attend_gahead_sam_log_pl_kernel(tc, wT, mT, xT, y, ts, us, wt, offs, ou
             )
             copy(out=into[:, slots], in_=sums[:])
 
-        def scatter(t, slots, source):
+        def scatter(t, slots, source, on_scalar=False):
             out = window[t][:].indirect(slot_list(slots.start, slots.stop - slots.start))
-            if t % 2 == 0:
+            if not on_scalar:
                 nc.vector.tensor_copy(out=out, in_=source[:, slots])
             else:
                 nc.scalar.activation(out=out, in_=source[:, slots], func=ACT.Copy)
@@ -330,58 +334,58 @@ def tile_attend_gahead_sam_log_pl_kernel(tc, wT, mT, xT, y, ts, us, wt, offs, ou
         turned_gradient(3)
         turn_gradient(2)
         turn_gradient(3)
-        table_gradient(1, "a3", first_half, dw_early[1], nc.scalar.copy)
+        table_gradient(1, "a2", first_half, dw_early[1], nc.scalar.copy)
         quantise_g(2)
         quantise_g(3)
 
         out_rows = out_0.rearrange("(p t) c -> p t c", t=LANES)
-        shared_cols = COLS // 2
-        pair_words = [sb("pair_words%d" % side, [P, 2, shared_cols, 2], BF16, ("pair_words0", "dw3")[side]) for side in range(2)]
+        near_cols = NEAR_PIECES * PIECE
+        near, far = slice(0, near_cols), slice(near_cols, COLS)
         woven = [sb("woven%d" % k, [P, PIECE, LANES], BF16, ("w_table%d", "m_table%d")[k % 2] % (k // 2)) for k in range(PIECES)]
 
         def piece(k):
             return slice(k * PIECE, (k + 1) * PIECE)
 
         def store_plane(t):
-            queue = nc.scalar if t % 2 else nc.sync
-            queue.dma_start(out=out_rows[:, t, :], in_=window[t][:])
+            nc.sync.dma_start(out=out_rows[:, t, :], in_=window[t][:])
 
         scatter(0, first_half, dw_early[0])
         scatter(1, first_half, dw_early[1])
-        table_gradient(0, "b0", second_half, dw[0], nc.vector.tensor_copy)
+        dw_scalar = relay.tile([P, half], F32, name="dw_scalar", offset=1536)
+        table_gradient(0, "b0", second_half, dw[0], nc.scalar.copy)
+        table_gradient(2, "b0", first_half, dw_scalar, nc.scalar.copy)
         table_gradient(1, "a1", second_half, dw[1], nc.scalar.copy)
-        scatter(0, second_half, dw[0])
-        scatter(1, second_half, dw[1])
-        store_plane(0)
-        store_plane(1)
-        table_gradient(2, "b2", every_slot, dw[2], nc.vector.tensor_copy)
-        table_gradient(3, "b3", every_slot, dw[3], nc.vector.tensor_copy)
-        scatter(2, every_slot, dw[2])
-        scatter(3, first_half, dw[3])
-        scatter(3, second_half, dw[3])
-        store_plane(2)
-        store_plane(3)
+        table_gradient(2, "b2", second_half, dw[2], nc.scalar.copy)
+        scatter(2, first_half, dw_scalar, on_scalar=True)
+        dw.append(relay.tile([P, SLOTS], F32, name="dw3", offset=0))
+        table_gradient(3, "b3", every_slot, dw[3], nc.scalar.copy)
+        for t in range(LANES):
+            scatter(t, every_slot if t == LANES - 1 else second_half, dw[t])
+            store_plane(t)
 
-        left, right = slice(0, shared_cols), slice(shared_cols, COLS)
-        for t in range(2):
-            nc.gpsimd.tensor_scalar(
-                out=pair_words[0][:, 0, :, t], in0=window[t][:, left], scalar1=1.0, scalar2=0.0, op0=ALU.mult, op1=ALU.add
-            )
-        nc.vector.tensor_copy(out=pair_words[0][:, 1, :, 0], in_=window[2][:, left])
-        for t in range(2):
-            nc.vector.tensor_copy(out=pair_words[1][:, 0, :, t], in_=window[t][:, right])
-        nc.vector.tensor_copy(out=pair_words[0][:, 1, :, 1], in_=window[3][:, left])
-        for k in range(PIECES // 2, PIECES):
-            for t in range(2, LANES):
-                nc.scalar.copy(out=pair_words[1][:, 1, piece(k - PIECES // 2), t % 2], in_=window[t][:, piece(k)])
+        def gpsimd_round(out, source):
+            nc.gpsimd.tensor_scalar(out=out, in0=source, scalar1=1.0, scalar2=0.0, op0=ALU.mult, op1=ALU.add)
 
-        out_codes = [sb("out_codes%d" % h, [P, 2 * PIECE], U32) for h in range(PIECES // 2)]
+        near_words = sb("near_words", [P, 2, near_cols, 2], BF16)
+        far_words = relay.tile([P, 2, COLS - near_cols, 2], BF16, name="far_words", offset=2048)
+        for t in range(2):
+            gpsimd_round(near_words[:, 0, :, t], window[t][:, near])
+        single = near_cols - WHOLE_WORDS
+        gpsimd_round(near_words[:, 1, :single, 0], window[2][:, :single])
+        gpsimd_round(near_words[:, 1, single:, :], window[2][:, single:near_cols].unsqueeze(2).to_broadcast([P, WHOLE_WORDS, 2]))
+        for t in range(LANES - 1):
+            nc.scalar.copy(out=far_words[:, t // 2, :, t % 2], in_=window[t][:, far])
+        nc.vector.tensor_copy(out=near_words[:, 1, :, 1], in_=window[3][:, near])
+        for k in range(NEAR_PIECES, PIECES):
+            nc.scalar.copy(out=far_words[:, 1, piece(k - NEAR_PIECES), 1], in_=window[3][:, piece(k)])
+
+        out_codes = sb("out_codes", [P, COLS], U32)
         out_scales = sb("out_scales", [P, 2 * PIECE], U8)
         code_rows = out_1[0].rearrange("p c l -> p (c l)").bitcast(I32)
 
         def weave(k):
-            side, place = divmod(k, PIECES // 2)
-            words = pair_words[side][:].rearrange("p h c e -> p (h c e)").bitcast(F32).rearrange("p (h c) -> p c h", h=2)
+            halves, place = (near_words, k) if k < NEAR_PIECES else (far_words, k - NEAR_PIECES)
+            words = halves[:].rearrange("p h c e -> p (h c e)").bitcast(F32).rearrange("p (h c) -> p c h", h=2)
             copy = nc.scalar.copy if k >= PIECES - SCALAR_WEAVES else nc.vector.tensor_copy
             copy(
                 out=woven[k][:].rearrange("p c t -> p (c t)").bitcast(F32).rearrange("p (c h) -> p c h", h=2),
@@ -391,16 +395,13 @@ def tile_attend_gahead_sam_log_pl_kernel(tc, wT, mT, xT, y, ts, us, wt, offs, ou
         def quantise_out(k):
             side = slice((k % 2) * PIECE, (k % 2 + 1) * PIECE)
             nc.vector.quantize_mx(
-                out=out_codes[k // 2][:, side].bitcast(E4M3),
+                out=out_codes[:, piece(k)].bitcast(E4M3),
                 scales=out_scales[4 * (k // 2) :, side],
                 in_=woven[k][:].rearrange("p c t -> p (c t)"),
             )
-            if k >= PIECES - 2:
-                nc.sync.dma_start(out=code_rows[:, piece(k)], in_=out_codes[k // 2][:, side].bitcast(I32))
-            elif k % 2 == 1:
-                nc.sync.dma_start(
-                    out=code_rows[:, (k - 1) * PIECE : (k + 1) * PIECE], in_=out_codes[k // 2][:].bitcast(I32)
-                )
+            if k + 1 in STORE_EDGES:
+                cols = slice(STORE_EDGES[list(STORE_EDGES).index(k + 1) - 1] * PIECE, (k + 1) * PIECE)
+                nc.sync.dma_start(out=code_rows[:, cols], in_=out_codes[:, cols].bitcast(I32))
 
         weave(0)
         for k in range(PIECES):

@@ -23,7 +23,7 @@ CHUNK = 128
 CHUNKS = SLOTS // CHUNK
 PIECE = 256
 PIECES = COLS // PIECE
-WHOLE_WORDS = 32
+WHOLE_WORDS = 16
 NEAR_PIECES = 4
 STORE_EDGES = (0, 4, 6, 7, 8)
 SCALAR_WEAVES = 4
@@ -49,14 +49,15 @@ def tile_attend_gahead_sam_log_pl_kernel(tc, wT, mT, xT, y, ts, us, wt, offs, ou
         nc.sync.dma_start(out=x[:], in_=xT.rearrange("(p t) r -> p t r", t=LANES))
         nc.sync.dma_start(offsets[:], offs)
 
-        us_col = sb("us_col", [P, LANES], F32)
-        wt_col = sb("wt_col", [P, LANES], F32)
-        nc.scalar.dma_start(out=us_col[:], in_=us.rearrange("(p u) one -> p (u one)", u=LANES))
-        nc.scalar.dma_start(out=wt_col[:], in_=wt.rearrange("(p u) one -> p (u one)", u=LANES))
-        ts_folded = sb("ts_folded", [P, FOLD], F32)
-        nc.scalar.dma_start(out=ts_folded[:], in_=ts[0].rearrange("(n c) -> n c", c=FOLD))
+        ts_rows = sb("ts_rows", [P, P], F32)
+        row_scales = sb("row_scales", [P, R], F32)
+        nc.vector.memset(ts_rows[:], 0.0)
+        nc.vector.memset(row_scales[:], 0.0)
+        nc.sync.dma_start(out=ts_rows[:FOLD, :], in_=ts[0].rearrange("(n c) -> n c", c=P))
+        nc.sync.dma_start(out=row_scales[0:1, :], in_=us.rearrange("r one -> one r"))
+        nc.sync.dma_start(out=row_scales[1:2, :], in_=wt.rearrange("r one -> one r"))
         warm = sb("warm", [P, 1], F32)
-        nc.scalar.activation(out=warm[:], in_=us_col[:, 0:1], func=ACT.Sigmoid)
+        nc.scalar.activation(out=warm[:], in_=ts_rows[:, 0:1], func=ACT.Sigmoid)
 
         w_rows = wT.rearrange("(p t) c -> p t c", t=LANES)
         m_rows = mT.rearrange("(p t) c -> p t c", t=LANES)
@@ -101,16 +102,24 @@ def tile_attend_gahead_sam_log_pl_kernel(tc, wT, mT, xT, y, ts, us, wt, offs, ou
             out=xr_codes[:].bitcast(E4M3), scales=xr_scales[:], in_=x_by_r[:].rearrange("s t p u -> s (t p u)")
         )
 
+        ts_down = psum.tile([P, P], F32, name="ts_down", tag="b0")
+        nc.tensor.transpose(ts_down[:], ts_rows[:], ident_f32[:])
+        ts_folded = sb("ts_folded", [P, FOLD], F32)
+        nc.scalar.copy(out=ts_folded[:], in_=ts_down[:, :FOLD])
+        scales_down = psum.tile([P, LANES, P], F32, name="scales_down", tag="b1")
+        for u in range(LANES):
+            nc.tensor.transpose(scales_down[:, u, :], row_scales[:, u::LANES], ident_f32[:])
+        us_col = sb("us_col", [P, LANES], F32)
+        wt_col = sb("wt_col", [P, LANES], F32)
+        nc.scalar.copy(out=us_col[:], in_=scales_down[:, :, 0])
+        nc.scalar.copy(out=wt_col[:], in_=scales_down[:, :, 1])
         ts_table = sb("ts_table", [P, COLS], F32)
         for b in range(FOLD // 4):
             spread = psum.tile([P, 4, P], F32, name="spread%d" % b, tag="b%d" % b)
             for c in range(4):
                 column = ts_folded[:, 4 * b + c : 4 * b + c + 1]
                 nc.tensor.transpose(spread[:, c, :], column.to_broadcast([P, P]), ident_f32[:])
-            nc.scalar.copy(
-                out=ts_table[:].rearrange("p (n c) -> p n c", c=FOLD)[:, :, 4 * b : 4 * b + 4],
-                in_=spread[:].rearrange("p c n -> p n c"),
-            )
+            nc.scalar.copy(out=ts_table[:, 4 * b * P : 4 * (b + 1) * P], in_=spread[:].rearrange("p c n -> p (c n)"))
         ts_all = sb("ts_all", [P, SLOTS], F32)
         nc.vector.tensor_copy(out=ts_all[:], in_=ts_table[:].indirect(offsets[:]))
         ts_turned = psum.tile([P, len(TURNED), P], F32, name="ts_turned", tag="b0")
@@ -370,12 +379,15 @@ def tile_attend_gahead_sam_log_pl_kernel(tc, wT, mT, xT, y, ts, us, wt, offs, ou
         far_words = relay.tile([P, 2, COLS - near_cols, 2], BF16, name="far_words", offset=2048)
         for t in range(2):
             gpsimd_round(near_words[:, 0, :, t], window[t][:, near])
-        single = near_cols - WHOLE_WORDS
-        gpsimd_round(near_words[:, 1, :single, 0], window[2][:, :single])
-        gpsimd_round(near_words[:, 1, single:, :], window[2][:, single:near_cols].unsqueeze(2).to_broadcast([P, WHOLE_WORDS, 2]))
+        single = 2 * PIECE - WHOLE_WORDS
+        runs = near_words[:, 1, :, :].rearrange("p (n c) e -> p n c e", c=2 * PIECE)
+        source = window[2][:, near].rearrange("p (n c) -> p n c", c=2 * PIECE)
+        gpsimd_round(runs[:, :, :single, 0], source[:, :, :single])
+        gpsimd_round(runs[:, :, single:, :], source[:, :, single:].unsqueeze(3).to_broadcast([P, NEAR_PIECES // 2, WHOLE_WORDS, 2]))
         for t in range(LANES - 1):
             nc.scalar.copy(out=far_words[:, t // 2, :, t % 2], in_=window[t][:, far])
-        nc.vector.tensor_copy(out=near_words[:, 1, :, 1], in_=window[3][:, near])
+        for first in range(0, near_cols, 2 * PIECE):
+            nc.vector.tensor_copy(out=near_words[:, 1, first : first + 2 * PIECE, 1], in_=window[3][:, first : first + 2 * PIECE])
         for k in range(NEAR_PIECES, PIECES):
             nc.scalar.copy(out=far_words[:, 1, piece(k - NEAR_PIECES), 1], in_=window[3][:, piece(k)])
 

@@ -199,22 +199,27 @@ def tile_attend_gahead_sam_log_pl_kernel(tc, wT, mT, xT, y, ts, us, wt, offs, ou
             else:
                 nc.scalar.activation(out=out, in_=source[:, slots], func=ACT.Copy)
 
-        def finish_w2(j):
+        def finish_w2(j, parts=1):
             tag = "w2_by_d0" if j == CHUNKS - 1 else "w2_last%d" % j
             w2_last = keep.tile([P, CHUNK], F32, name="w2_last%d" % j, tag=tag, align_bytes=64)
-            nc.vector.tensor_tensor(
-                out=w2_last[:],
-                in0=m_table[3][:].indirect(slot_list(j * CHUNK, CHUNK)),
-                in1=w_picked[1][:, chunk(j)],
-                op=ALU.add,
-            )
-            nc.scalar.copy(out=w2_by_d[j][:, :, 3], in_=w2_last[:])
+            width = CHUNK // parts
+            for first in range(0, CHUNK, width):
+                part = slice(first, first + width)
+                nc.vector.tensor_tensor(
+                    out=w2_last[:, part],
+                    in0=m_table[3][:].indirect(slot_list(j * CHUNK + first, width)),
+                    in1=w_picked[1][:, j * CHUNK + first : j * CHUNK + first + width],
+                    op=ALU.add,
+                )
+                nc.scalar.copy(out=w2_by_d[j][:, part, 3], in_=w2_last[:, part])
 
         def score(j):
             nc.vector.quantize_mx(
                 out=w2_codes[j][:].bitcast(E4M3), scales=w2_scales[j][:], in_=w2_by_d[j][:].rearrange("p i t -> p (i t)")
             )
             scores[j] = psum.tile([P, LANES, CHUNK], F32, name="scores%d" % j, tag="a%d" % j)
+            if j == 0:
+                scores[j] = [scores[j], psum.tile([P, LANES, CHUNK], F32, name="scores0_late", tag="b1")]
             if j in TURNED:
                 nc.tensor.matmul_mx(
                     out=scores[j][:].rearrange("i u s -> i (u s)"),
@@ -229,7 +234,7 @@ def tile_attend_gahead_sam_log_pl_kernel(tc, wT, mT, xT, y, ts, us, wt, offs, ou
             for u in range(LANES):
                 rows = slice(u * P, (u + 1) * P)
                 nc.tensor.matmul_mx(
-                    out=scores[j][:, u, :],
+                    out=(scores[j][u // 2] if j == 0 else scores[j])[:, u, :],
                     lhsT=xd_codes[:, rows].bitcast(E4M3),
                     lhsT_scale=xd_scales[:, rows],
                     rhs=w2_codes[j][:].bitcast(E4M3),
@@ -237,6 +242,13 @@ def tile_attend_gahead_sam_log_pl_kernel(tc, wT, mT, xT, y, ts, us, wt, offs, ou
                     start=True,
                     stop=True,
                 )
+
+        def first_logits(h):
+            lanes = slice(2 * h, 2 * h + 2)
+            nc.vector.tensor_tensor(
+                out=work[0][:, lanes, :], in0=scores[0][h][:, lanes, :], in1=logit_scale[:, lanes, chunk(0)], op=ALU.mult
+            )
+            nc.scalar.activation(out=work[0][:, lanes, :], in_=work[0][:, lanes, :], func=ACT.Sigmoid)
 
         def logits(j):
             nc.vector.tensor_tensor(out=work[j][:], in0=scores[j][:], in1=logit_scale[:, :, chunk(j)], op=ALU.mult)
@@ -313,14 +325,15 @@ def tile_attend_gahead_sam_log_pl_kernel(tc, wT, mT, xT, y, ts, us, wt, offs, ou
                 in_=g_by_r[j][:].rearrange("p i u -> p (i u)"),
             )
 
-        finish_w2(0)
+        finish_w2(0, parts=2)
         finish_w2(1)
         finish_w2(2)
         score(0)
         score(1)
         finish_w2(3)
         score(2)
-        logits(0)
+        first_logits(0)
+        first_logits(1)
         score(3)
         turn_logits(2)
         logits(1)

@@ -326,6 +326,18 @@ def tile_attend_gahead_sam_log_pl_kernel(tc, wT, mT, xT, y, ts, us, wt, offs, ou
             )
 
         finish_w2(0, parts=2)
+        idle = psum.tile([P, R], F32, name="idle", tag="a3")
+        nc.tensor.transpose(idle[:, :P], m_table[3][:, :P], ident_f32[:])
+        for n in range(2):
+            nc.tensor.matmul_mx(
+                out=idle[:],
+                lhsT=xd_codes[:, :P].bitcast(E4M3),
+                lhsT_scale=xd_scales[:, :P],
+                rhs=xd_codes[:].bitcast(E4M3),
+                rhs_scale=xd_scales[:],
+                start=True,
+                stop=True,
+            )
         finish_w2(1)
         finish_w2(2)
         score(0)

@@ -28,7 +28,7 @@ NEAR_PIECES = 4
 STORE_EDGES = (0, 4, 6, 7, 8)
 SCALAR_WEAVES = 4
 FOLD = COLS // P
-TURNED = (2, 3)
+TURNED = CHUNKS - 1
 
 
 def tile_attend_gahead_sam_log_pl_kernel(tc, wT, mT, xT, y, ts, us, wt, offs, out_0, out_1, out_2):
@@ -62,11 +62,14 @@ def tile_attend_gahead_sam_log_pl_kernel(tc, wT, mT, xT, y, ts, us, wt, offs, ou
         w_rows = wT.rearrange("(p t) c -> p t c", t=LANES)
         m_rows = mT.rearrange("(p t) c -> p t c", t=LANES)
         w_table, m_table = [], []
-        for t in range(LANES):
-            w_table.append(sb("w_table%d" % t, [P, COLS], F32))
-            m_table.append(sb("m_table%d" % t, [P, COLS], F32))
-            nc.sync.dma_start(out=w_table[t][:], in_=w_rows[:, t, :])
-            nc.sync.dma_start(out=m_table[t][:], in_=m_rows[:, t, :])
+        for h in range(2):
+            w_pair = sb("w_pair%d" % h, [P, 2, COLS], F32)
+            nc.sync.dma_start(out=w_pair[:], in_=w_rows[:, 2 * h : 2 * h + 2, :])
+            for e in range(2):
+                t = 2 * h + e
+                w_table.append(w_pair[:, e, :])
+                m_table.append(sb("m_table%d" % t, [P, COLS], F32))
+                nc.sync.dma_start(out=m_table[t][:], in_=m_rows[:, t, :])
         labels = sb("labels", [P, LANES, SLOTS], F32)
         nc.sync.dma_start(out=labels[:], in_=y.rearrange("(p u) i -> p u i", u=LANES))
 
@@ -122,36 +125,23 @@ def tile_attend_gahead_sam_log_pl_kernel(tc, wT, mT, xT, y, ts, us, wt, offs, ou
             nc.scalar.copy(out=ts_table[:, 4 * b * P : 4 * (b + 1) * P], in_=spread[:].rearrange("p c n -> p (c n)"))
         ts_all = sb("ts_all", [P, SLOTS], F32)
         nc.vector.tensor_copy(out=ts_all[:], in_=ts_table[:].indirect(offsets[:]))
-        ts_turned = psum.tile([P, len(TURNED), P], F32, name="ts_turned", tag="b0")
-        for n, j in enumerate(TURNED):
-            nc.tensor.transpose(ts_turned[:, n, :], ts_all[:, j * P : (j + 1) * P], ident_f32[:])
-        ts_col = sb("ts_col", [P, len(TURNED)], F32)
-        nc.scalar.copy(out=ts_col[:], in_=ts_turned[:, :, 0])
-        minus_ts_col = sb("minus_ts_col", [P, len(TURNED)], F32)
-        nc.scalar.activation(out=minus_ts_col[:], in_=ts_turned[:, :, 0], func=ACT.Copy, scale=-1.0)
-        minus_us_col = sb("minus_us_col", [P, LANES], F32)
-        nc.scalar.activation(out=minus_us_col[:], in_=us_col[:], func=ACT.Copy, scale=-1.0)
+        ts_turned = psum.tile([P, P], F32, name="ts_turned", tag="b0")
+        nc.tensor.transpose(ts_turned[:], ts_all[:, TURNED * P : (TURNED + 1) * P], ident_f32[:])
+        ts_col = sb("ts_col", [P, 1], F32)
+        nc.scalar.copy(out=ts_col[:], in_=ts_turned[:, 0:1])
         wu_col = sb("wu_col", [P, LANES], F32)
         nc.vector.tensor_tensor(out=wu_col[:], in0=wt_col[:], in1=us_col[:], op=ALU.mult)
-        logit_scale = sb("logit_scale", [P, LANES, 2 * CHUNK], F32)
-        grad_scale = sb("grad_scale", [P, LANES, 2 * CHUNK], F32)
+        logit_scale = [sb("logit_scale%d" % j, [P, LANES, CHUNK], F32) for j in range(TURNED)]
+        grad_scale = sb("grad_scale", [P, LANES, SLOTS], F32)
+        for j in range(TURNED):
+            for u in range(LANES):
+                nc.scalar.activation(
+                    out=logit_scale[j][:, u, :], in_=ts_all[:, j * CHUNK : (j + 1) * CHUNK], func=ACT.Copy, scale=us_col[:, u : u + 1]
+                )
         for u in range(LANES):
-            nc.scalar.activation(out=logit_scale[:, u, :], in_=ts_all[:, : 2 * CHUNK], func=ACT.Copy, scale=us_col[:, u : u + 1])
-        for u in range(LANES):
-            nc.scalar.activation(out=grad_scale[:, u, :], in_=ts_all[:, : 2 * CHUNK], func=ACT.Copy, scale=wu_col[:, u : u + 1])
-        wu_rows = psum.tile([P, LANES, P], F32, name="wu_rows", tag="b1")
-        for u in range(LANES):
-            nc.tensor.transpose(wu_rows[:, u, :], wu_col[:, u : u + 1].to_broadcast([P, P]), ident_f32[:])
-        minus_scale = [sb("minus_scale%d" % j, [P, 2, P, 2], F32) for j in TURNED]
-        for n in range(len(TURNED)):
-            nc.scalar.activation(
-                out=minus_scale[n][:],
-                in_=wu_rows[:].rearrange("i (h e) s -> i h s e", e=2),
-                func=ACT.Copy,
-                scale=minus_ts_col[:, n : n + 1],
-            )
+            nc.scalar.activation(out=grad_scale[:, u, :], in_=ts_all[:], func=ACT.Copy, scale=wu_col[:, u : u + 1])
 
-        w_picked = [keep.tile([P, SLOTS], F32, name="w_picked%d" % t, tag="w_picked%d" % (t % 2)) for t in range(2)]
+        w_picked = [sb("w_picked%d" % t, [P, SLOTS], F32) for t in range(LANES)]
         w2_early = sb("w2_early", [P, LANES - 1, SLOTS], F32)
         w2_by_d = [sb("w2_by_d%d" % j, [P, CHUNK, LANES], BF16) for j in range(CHUNKS)]
         w2_codes = [sb("w2_codes%d" % j, [P, CHUNK], U32) for j in range(CHUNKS)]
@@ -160,14 +150,14 @@ def tile_attend_gahead_sam_log_pl_kernel(tc, wT, mT, xT, y, ts, us, wt, offs, ou
         def chunk(j):
             return slice(j * CHUNK, (j + 1) * CHUNK)
 
-        for t in range(LANES - 1):
-            nc.vector.tensor_copy(out=w_picked[t % 2][:], in_=w_table[t][:].indirect(offsets[:]))
-            nc.vector.tensor_tensor(
-                out=w2_early[:, t, :], in0=m_table[t][:].indirect(offsets[:]), in1=w_picked[t % 2][:], op=ALU.add
-            )
+        for t in range(LANES):
+            nc.vector.tensor_copy(out=w_picked[t][:], in_=w_table[t].indirect(offsets[:]))
+            if t < LANES - 1:
+                nc.vector.tensor_tensor(
+                    out=w2_early[:, t, :], in0=m_table[t][:].indirect(offsets[:]), in1=w_picked[t][:], op=ALU.add
+                )
         for j in range(CHUNKS):
             nc.scalar.copy(out=w2_by_d[j][:, :, 0:3], in_=w2_early[:, :, chunk(j)].rearrange("p t i -> p i t"))
-        nc.vector.tensor_copy(out=w_picked[1][:], in_=w_table[3][:].indirect(offsets[:]))
 
         scores = [None] * CHUNKS
         work = [sb("work%d" % j, [P, LANES, CHUNK], F32) for j in range(CHUNKS)]
@@ -176,11 +166,10 @@ def tile_attend_gahead_sam_log_pl_kernel(tc, wT, mT, xT, y, ts, us, wt, offs, ou
         g_scales = sb("g_scales", [P, SLOTS], U8)
         half = SLOTS // 2
         first_half, second_half, every_slot = slice(0, half), slice(half, SLOTS), slice(0, SLOTS)
-        dw = [sb("dw%d" % t, [P, SLOTS], F32) for t in range(LANES - 1)]
 
         def table_gradient(t, bank, slots, into, copy):
             features = slice(t * P, (t + 1) * P)
-            sums = psum.tile([P, slots.stop - slots.start], F32, name="sums%d_%s" % (t, bank), tag=bank)
+            sums = psum.tile([P, slots.stop - slots.start], F32, name="sums%d_%d" % (t, slots.start), tag=bank)
             nc.tensor.matmul_mx(
                 out=sums[:],
                 lhsT=xr_codes[:, features].bitcast(E4M3),
@@ -190,14 +179,14 @@ def tile_attend_gahead_sam_log_pl_kernel(tc, wT, mT, xT, y, ts, us, wt, offs, ou
                 start=True,
                 stop=True,
             )
-            copy(out=into[:, slots], in_=sums[:])
+            copy(out=into[:], in_=sums[:])
 
         def scatter(t, slots, source, on_scalar=False):
             out = window[t][:].indirect(slot_list(slots.start, slots.stop - slots.start))
             if not on_scalar:
-                nc.vector.tensor_copy(out=out, in_=source[:, slots])
+                nc.vector.tensor_copy(out=out, in_=source[:])
             else:
-                nc.scalar.activation(out=out, in_=source[:, slots], func=ACT.Copy)
+                nc.scalar.activation(out=out, in_=source[:], func=ACT.Copy)
 
         def finish_w2(j, parts=1):
             tag = "w2_by_d0" if j == CHUNKS - 1 else "w2_last%d" % j
@@ -208,7 +197,7 @@ def tile_attend_gahead_sam_log_pl_kernel(tc, wT, mT, xT, y, ts, us, wt, offs, ou
                 nc.vector.tensor_tensor(
                     out=w2_last[:, part],
                     in0=m_table[3][:].indirect(slot_list(j * CHUNK + first, width)),
-                    in1=w_picked[1][:, j * CHUNK + first : j * CHUNK + first + width],
+                    in1=w_picked[3][:, j * CHUNK + first : j * CHUNK + first + width],
                     op=ALU.add,
                 )
                 nc.scalar.copy(out=w2_by_d[j][:, part, 3], in_=w2_last[:, part])
@@ -220,7 +209,7 @@ def tile_attend_gahead_sam_log_pl_kernel(tc, wT, mT, xT, y, ts, us, wt, offs, ou
             scores[j] = psum.tile([P, LANES, CHUNK], F32, name="scores%d" % j, tag="a%d" % j)
             if j == 0:
                 scores[j] = [scores[j], psum.tile([P, LANES, CHUNK], F32, name="scores0_late", tag="b1")]
-            if j in TURNED:
+            if j == TURNED:
                 nc.tensor.matmul_mx(
                     out=scores[j][:].rearrange("i u s -> i (u s)"),
                     lhsT=w2_codes[j][:].bitcast(E4M3),
@@ -246,69 +235,30 @@ def tile_attend_gahead_sam_log_pl_kernel(tc, wT, mT, xT, y, ts, us, wt, offs, ou
         def first_logits(h):
             lanes = slice(2 * h, 2 * h + 2)
             nc.vector.tensor_tensor(
-                out=work[0][:, lanes, :], in0=scores[0][h][:, lanes, :], in1=logit_scale[:, lanes, chunk(0)], op=ALU.mult
+                out=work[0][:, lanes, :], in0=scores[0][h][:, lanes, :], in1=logit_scale[0][:, lanes, :], op=ALU.mult
             )
             nc.scalar.activation(out=work[0][:, lanes, :], in_=work[0][:, lanes, :], func=ACT.Sigmoid)
 
         def logits(j):
-            nc.vector.tensor_tensor(out=work[j][:], in0=scores[j][:], in1=logit_scale[:, :, chunk(j)], op=ALU.mult)
+            nc.vector.tensor_tensor(out=work[j][:], in0=scores[j][:], in1=logit_scale[j][:], op=ALU.mult)
             nc.scalar.activation(out=work[j][:], in_=work[j][:], func=ACT.Sigmoid)
 
-        def turn_logits(j):
-            n = TURNED.index(j)
-            scaled = sb("scaled%d" % j, [P, LANES, P], F32)
-            nc.scalar.activation(out=scaled[:], in_=scores[j][:], func=ACT.Copy, scale=ts_col[:, n : n + 1])
-            scores[j] = psum.tile([P, LANES, CHUNK], F32, name="back%d" % j, tag="b%d" % j)
+        def turned_logits(j):
+            scaled = sb("scaled", [P, LANES, P], F32, "logit_scale%d" % (j - 1))
+            nc.scalar.activation(out=scaled[:], in_=scores[j][:], func=ACT.Copy, scale=ts_col[:])
+            scores[j] = psum.tile([P, LANES, CHUNK], F32, name="back", tag="b3")
             for u in range(LANES):
                 nc.tensor.transpose(scores[j][:, u, :], scaled[:, u, :], ident_f32[:])
 
         def turned_sigmoid(j):
             for u in range(LANES):
-                nc.scalar.activation(
-                    out=work[j][:, u, :], in_=scores[j][:, u, :], func=ACT.Sigmoid, scale=minus_us_col[:, u : u + 1]
-                )
-
-        misses = {}
-
-        def turn_labels(j):
-            misses[j] = psum.tile([P, LANES, P], F32, name="misses%d" % j, tag="b%d" % (j - 2))
-            for u in range(LANES):
-                nc.tensor.matmul(
-                    misses[j][:, u, :], labels[:, u, chunk(j)], ident_f32[:], start=(u == 0), stop=False, is_transpose=True
-                )
-
-        def add_sigmoid(j):
-            for u in range(LANES):
-                nc.tensor.matmul(
-                    misses[j][:, u, :], work[j][:, u, :], ident_f32[:], start=False, stop=(u == LANES - 1), is_transpose=True
-                )
-
-        g_turned = {}
-
-        def turned_gradient(j):
-            g_turned[j] = sb("g_turned%d" % j, [P, 2, P, 2], BF16)
-            for h in range(2):
-                nc.vector.scalar_tensor_tensor(
-                    out=g_turned[j][:, h, :, :],
-                    in0=misses[j][:, 2 * h : 2 * h + 2, :].rearrange("i e s -> i s e"),
-                    scalar=1.0,
-                    in1=minus_scale[TURNED.index(j)][:, h, :, :],
-                    op0=ALU.subtract,
-                    op1=ALU.mult,
-                )
-
-        def turn_gradient(j):
-            words = g_turned[j][:].rearrange("i h s e -> i (h s e)").bitcast(F32)
-            back = psum.tile([P, 2, P], F32, name="g_back%d" % j, tag="a%d" % j)
-            for h in range(2):
-                nc.tensor.transpose(back[:, h, :], words[:, h * P : (h + 1) * P], ident_f32[:])
-            nc.scalar.copy(
-                out=g_by_r[j][:].rearrange("s i u -> s (i u)").bitcast(F32).rearrange("s (i h) -> s i h", h=2),
-                in_=back[:].rearrange("s h i -> s i h"),
-            )
+                nc.scalar.activation(out=work[j][:, u, :], in_=scores[j][:, u, :], func=ACT.Sigmoid, scale=us_col[:, u : u + 1])
 
         def residual(j):
-            nc.vector.tensor_tensor(out=work[j][:], in0=work[j][:], in1=labels[:, :, chunk(j)], op=ALU.subtract)
+            sigmoid = work[j]
+            if j >= 2:
+                work[j] = sb("misses%d" % j, [P, LANES, CHUNK], F32, "g_by_r%d" % (j - 2))
+            nc.vector.tensor_tensor(out=work[j][:], in0=sigmoid[:], in1=labels[:, :, chunk(j)], op=ALU.subtract)
 
         def gradient(j):
             nc.vector.tensor_tensor(
@@ -326,18 +276,6 @@ def tile_attend_gahead_sam_log_pl_kernel(tc, wT, mT, xT, y, ts, us, wt, offs, ou
             )
 
         finish_w2(0, parts=2)
-        idle = psum.tile([P, R], F32, name="idle", tag="a3")
-        nc.tensor.transpose(idle[:, :P], m_table[3][:, :P], ident_f32[:])
-        for n in range(2):
-            nc.tensor.matmul_mx(
-                out=idle[:],
-                lhsT=xd_codes[:, :P].bitcast(E4M3),
-                lhsT_scale=xd_scales[:, :P],
-                rhs=xd_codes[:].bitcast(E4M3),
-                rhs_scale=xd_scales[:],
-                start=True,
-                stop=True,
-            )
         finish_w2(1)
         finish_w2(2)
         score(0)
@@ -347,35 +285,30 @@ def tile_attend_gahead_sam_log_pl_kernel(tc, wT, mT, xT, y, ts, us, wt, offs, ou
         first_logits(0)
         first_logits(1)
         score(3)
-        turn_logits(2)
         logits(1)
-        turn_logits(3)
-        turn_labels(2)
-        turn_labels(3)
-        turned_sigmoid(2)
-        add_sigmoid(2)
+        turned_logits(3)
+        logits(2)
         turned_sigmoid(3)
-        add_sigmoid(3)
-        residual(0)
-        residual(1)
-        gradient(0)
-        gradient(1)
-        quantise_g(0)
-        quantise_g(1)
-        turned_gradient(2)
-        dw_early = [sb("dw_early%d" % t, [P, half], F32, ("x", "ts_table")[t]) for t in range(2)]
-        table_gradient(0, "a0", first_half, dw_early[0], nc.scalar.copy)
-        turned_gradient(3)
-        turn_gradient(2)
-        turn_gradient(3)
-        table_gradient(1, "a2", first_half, dw_early[1], nc.scalar.copy)
-        quantise_g(2)
+        for pair in range(2):
+            chunks = (2 * pair, 2 * pair + 1)
+            for j in chunks:
+                residual(j)
+            for j in chunks:
+                gradient(j)
+            quantise_g(chunks[0])
+            if pair == 0:
+                quantise_g(chunks[1])
+        early = [sb("dw_early%d" % t, [P, half], F32) for t in range(2)]
+        table_gradient(0, "b0", first_half, early[0], nc.scalar.copy)
+        scatter(0, first_half, early[0], on_scalar=True)
+        table_gradient(1, "b3", first_half, early[1], nc.vector.tensor_copy)
         quantise_g(3)
 
         out_rows = out_0.rearrange("(p t) c -> p t c", t=LANES)
         near_cols = NEAR_PIECES * PIECE
         near, far = slice(0, near_cols), slice(near_cols, COLS)
-        woven = [sb("woven%d" % k, [P, PIECE, LANES], BF16, ("w_table%d", "m_table%d")[k % 2] % (k // 2)) for k in range(PIECES)]
+        dead = ("m_table0", "m_table1", "m_table2", "m_table3", "w_pair0", "w_pair1", "x", "ts_table")
+        woven = [sb("woven%d" % k, [P, PIECE, LANES], BF16, dead[k]) for k in range(PIECES)]
 
         def piece(k):
             return slice(k * PIECE, (k + 1) * PIECE)
@@ -383,18 +316,18 @@ def tile_attend_gahead_sam_log_pl_kernel(tc, wT, mT, xT, y, ts, us, wt, offs, ou
         def store_plane(t):
             nc.sync.dma_start(out=out_rows[:, t, :], in_=window[t][:])
 
-        scatter(0, first_half, dw_early[0])
-        scatter(1, first_half, dw_early[1])
+        scatter(1, first_half, early[1])
+        late = [sb("dw_late%d" % t, [P, half], F32) for t in range(LANES - 1)]
         dw_scalar = relay.tile([P, half], F32, name="dw_scalar", offset=1536)
-        table_gradient(0, "b0", second_half, dw[0], nc.scalar.copy)
-        table_gradient(2, "b0", first_half, dw_scalar, nc.scalar.copy)
-        table_gradient(1, "a1", second_half, dw[1], nc.scalar.copy)
-        table_gradient(2, "b2", second_half, dw[2], nc.scalar.copy)
+        table_gradient(0, "a0", second_half, late[0], nc.scalar.copy)
+        table_gradient(1, "a1", second_half, late[1], nc.scalar.copy)
+        table_gradient(2, "a0", first_half, dw_scalar, nc.scalar.copy)
+        table_gradient(2, "a2", second_half, late[2], nc.scalar.copy)
         scatter(2, first_half, dw_scalar, on_scalar=True)
-        dw.append(relay.tile([P, SLOTS], F32, name="dw3", offset=0))
-        table_gradient(3, "b3", every_slot, dw[3], nc.scalar.copy)
+        late.append(relay.tile([P, SLOTS], F32, name="dw_late3", offset=0))
+        table_gradient(3, "a3", every_slot, late[3], nc.scalar.copy)
         for t in range(LANES):
-            scatter(t, every_slot if t == LANES - 1 else second_half, dw[t])
+            scatter(t, every_slot if t == LANES - 1 else second_half, late[t])
             store_plane(t)
 
         def gpsimd_round(out, source):

@@ -25,8 +25,9 @@ PIECE = 256
 PIECES = COLS // PIECE
 WHOLE_WORDS = 16
 NEAR_PIECES = 4
-STORE_EDGES = (0, 4, 6, 7, 8)
+STORE_EDGES = (0, 3, 5, 7, 8)
 SCALAR_WEAVES = 4
+EXTRA = 192
 FOLD = COLS // P
 TURNED = CHUNKS - 1
 
@@ -81,6 +82,9 @@ def tile_attend_gahead_sam_log_pl_kernel(tc, wT, mT, xT, y, ts, us, wt, offs, ou
         window = [sb("window%d" % t, [P, COLS], F32) for t in range(LANES)]
         for t in range(LANES):
             nc.vector.memset(window[t][:], 0.0)
+
+        zeros = sb("zeros", [P, CHUNK], F32)
+        nc.vector.memset(zeros[:], 0.0)
 
         x_by_d = sb("x_by_d", [P, LANES, P, LANES], BF16)
         nc.scalar.copy(
@@ -142,7 +146,8 @@ def tile_attend_gahead_sam_log_pl_kernel(tc, wT, mT, xT, y, ts, us, wt, offs, ou
             nc.scalar.activation(out=grad_scale[:, u, :], in_=ts_all[:], func=ACT.Copy, scale=wu_col[:, u : u + 1])
 
         w_picked = [sb("w_picked%d" % t, [P, SLOTS], F32) for t in range(LANES)]
-        w2_early = sb("w2_early", [P, LANES - 1, SLOTS], F32)
+        w2_early = sb("w2_early", [P, 2, SLOTS], F32)
+        w2_late = [sb("w2_late%d" % j, [P, 2, CHUNK], F32) for j in range(CHUNKS)]
         w2_by_d = [sb("w2_by_d%d" % j, [P, CHUNK, LANES], BF16) for j in range(CHUNKS)]
         w2_codes = [sb("w2_codes%d" % j, [P, CHUNK], U32) for j in range(CHUNKS)]
         w2_scales = [sb("w2_scales%d" % j, [P, CHUNK], U8) for j in range(CHUNKS)]
@@ -150,14 +155,18 @@ def tile_attend_gahead_sam_log_pl_kernel(tc, wT, mT, xT, y, ts, us, wt, offs, ou
         def chunk(j):
             return slice(j * CHUNK, (j + 1) * CHUNK)
 
+        def add_listed(t, out, first, count):
+            nc.vector.tensor_tensor(
+                out=out, in0=m_table[t][:].indirect(slot_list(first, count)), in1=w_picked[t][:, first : first + count], op=ALU.add
+            )
+
         for t in range(LANES):
             nc.vector.tensor_copy(out=w_picked[t][:], in_=w_table[t].indirect(offsets[:]))
-            if t < LANES - 1:
-                nc.vector.tensor_tensor(
-                    out=w2_early[:, t, :], in0=m_table[t][:].indirect(offsets[:]), in1=w_picked[t][:], op=ALU.add
-                )
+            if t < 2:
+                add_listed(t, w2_early[:, t, :], 0, SLOTS)
         for j in range(CHUNKS):
-            nc.scalar.copy(out=w2_by_d[j][:, :, 0:3], in_=w2_early[:, :, chunk(j)].rearrange("p t i -> p i t"))
+            nc.scalar.copy(out=w2_by_d[j][:, :, 0:2], in_=w2_early[:, :, chunk(j)].rearrange("p t i -> p i t"))
+            add_listed(2, w2_late[j][:, 0, :], j * CHUNK, CHUNK)
 
         scores = [None] * CHUNKS
         work = [sb("work%d" % j, [P, LANES, CHUNK], F32) for j in range(CHUNKS)]
@@ -165,20 +174,22 @@ def tile_attend_gahead_sam_log_pl_kernel(tc, wT, mT, xT, y, ts, us, wt, offs, ou
         g_codes = sb("g_codes", [P, SLOTS], U32)
         g_scales = sb("g_scales", [P, SLOTS], U8)
         half = SLOTS // 2
-        first_half, second_half, every_slot = slice(0, half), slice(half, SLOTS), slice(0, SLOTS)
+        first_half, second_half = slice(0, half), slice(half, SLOTS)
 
-        def table_gradient(t, bank, slots, into, copy):
+        def table_gradient(t, bank, runs, into, copy):
             features = slice(t * P, (t + 1) * P)
-            sums = psum.tile([P, slots.stop - slots.start], F32, name="sums%d_%d" % (t, slots.start), tag=bank)
-            nc.tensor.matmul_mx(
-                out=sums[:],
-                lhsT=xr_codes[:, features].bitcast(E4M3),
-                lhsT_scale=xr_scales[:, features],
-                rhs=g_codes[:, slots].bitcast(E5M2),
-                rhs_scale=g_scales[:, slots],
-                start=True,
-                stop=True,
-            )
+            base = runs[0].start
+            sums = psum.tile([P, runs[-1].stop - base], F32, name="sums%d_%d" % (t, base), tag=bank)
+            for slots in runs:
+                nc.tensor.matmul_mx(
+                    out=sums[:, slots.start - base : slots.stop - base],
+                    lhsT=xr_codes[:, features].bitcast(E4M3),
+                    lhsT_scale=xr_scales[:, features],
+                    rhs=g_codes[:, slots].bitcast(E5M2),
+                    rhs_scale=g_scales[:, slots],
+                    start=True,
+                    stop=True,
+                )
             copy(out=into[:], in_=sums[:])
 
         def scatter(t, slots, source, on_scalar=False):
@@ -189,18 +200,11 @@ def tile_attend_gahead_sam_log_pl_kernel(tc, wT, mT, xT, y, ts, us, wt, offs, ou
                 nc.scalar.activation(out=out, in_=source[:], func=ACT.Copy)
 
         def finish_w2(j, parts=1):
-            tag = "w2_by_d0" if j == CHUNKS - 1 else "w2_last%d" % j
-            w2_last = keep.tile([P, CHUNK], F32, name="w2_last%d" % j, tag=tag, align_bytes=64)
             width = CHUNK // parts
             for first in range(0, CHUNK, width):
                 part = slice(first, first + width)
-                nc.vector.tensor_tensor(
-                    out=w2_last[:, part],
-                    in0=m_table[3][:].indirect(slot_list(j * CHUNK + first, width)),
-                    in1=w_picked[3][:, j * CHUNK + first : j * CHUNK + first + width],
-                    op=ALU.add,
-                )
-                nc.scalar.copy(out=w2_by_d[j][:, part, 3], in_=w2_last[:, part])
+                add_listed(3, w2_late[j][:, 1, part], j * CHUNK + first, width)
+                nc.scalar.copy(out=w2_by_d[j][:, part, 2:4], in_=w2_late[j][:, :, part].rearrange("p t i -> p i t"))
 
         def score(j):
             nc.vector.quantize_mx(
@@ -299,14 +303,17 @@ def tile_attend_gahead_sam_log_pl_kernel(tc, wT, mT, xT, y, ts, us, wt, offs, ou
             if pair == 0:
                 quantise_g(chunks[1])
         early = [sb("dw_early%d" % t, [P, half], F32) for t in range(2)]
-        table_gradient(0, "b0", first_half, early[0], nc.scalar.copy)
+        filler = sb("dw_filler", [P, CHUNK], F32)
+        table_gradient(2, "b2", [chunk(0)], filler, nc.scalar.copy)
+        table_gradient(0, "b0", [first_half], early[0], nc.scalar.copy)
+        table_gradient(1, "b3", [first_half], early[1], nc.scalar.copy)
         scatter(0, first_half, early[0], on_scalar=True)
-        table_gradient(1, "b3", first_half, early[1], nc.vector.tensor_copy)
         quantise_g(3)
+        nc.vector.tensor_tensor(out=window[2][:].indirect(slot_list(0, CHUNK)), in0=filler[:], in1=zeros[:], op=ALU.add)
 
         out_rows = out_0.rearrange("(p t) c -> p t c", t=LANES)
         near_cols = NEAR_PIECES * PIECE
-        near, far = slice(0, near_cols), slice(near_cols, COLS)
+        near = slice(0, near_cols)
         dead = ("m_table0", "m_table1", "m_table2", "m_table3", "w_pair0", "w_pair1", "x", "ts_table")
         woven = [sb("woven%d" % k, [P, PIECE, LANES], BF16, dead[k]) for k in range(PIECES)]
 
@@ -317,39 +324,47 @@ def tile_attend_gahead_sam_log_pl_kernel(tc, wT, mT, xT, y, ts, us, wt, offs, ou
             nc.sync.dma_start(out=out_rows[:, t, :], in_=window[t][:])
 
         scatter(1, first_half, early[1])
-        late = [sb("dw_late%d" % t, [P, half], F32) for t in range(LANES - 1)]
-        dw_scalar = relay.tile([P, half], F32, name="dw_scalar", offset=1536)
-        table_gradient(0, "a0", second_half, late[0], nc.scalar.copy)
-        table_gradient(1, "a1", second_half, late[1], nc.scalar.copy)
-        table_gradient(2, "a0", first_half, dw_scalar, nc.scalar.copy)
-        table_gradient(2, "a2", second_half, late[2], nc.scalar.copy)
-        scatter(2, first_half, dw_scalar, on_scalar=True)
-        late.append(relay.tile([P, SLOTS], F32, name="dw_late3", offset=0))
-        table_gradient(3, "a3", every_slot, late[3], nc.scalar.copy)
+        rest = slice(CHUNK, SLOTS)
+        late = [sb("dw_late%d" % t, [P, (half, half, SLOTS - CHUNK)[t]], F32) for t in range(LANES - 1)]
+        dw_scalar = relay.tile([P, half], F32, name="dw_scalar", offset=512)
+        table_gradient(0, "a0", [second_half], late[0], nc.scalar.copy)
+        table_gradient(1, "a1", [second_half], late[1], nc.scalar.copy)
+        table_gradient(2, "a2", [chunk(1), second_half], late[2], nc.scalar.copy)
+        table_gradient(3, "a0", [first_half], dw_scalar, nc.scalar.copy)
+        scatter(3, first_half, dw_scalar, on_scalar=True)
+        late.append(relay.tile([P, half], F32, name="dw_late3", offset=0))
+        table_gradient(3, "a3", [second_half], late[3], nc.scalar.copy)
         for t in range(LANES):
-            scatter(t, every_slot if t == LANES - 1 else second_half, late[t])
+            scatter(t, rest if t == 2 else second_half, late[t])
             store_plane(t)
 
         def gpsimd_round(out, source):
             nc.gpsimd.tensor_scalar(out=out, in0=source, scalar1=1.0, scalar2=0.0, op0=ALU.mult, op1=ALU.add)
 
         near_words = sb("near_words", [P, 2, near_cols, 2], BF16)
-        far_words = relay.tile([P, 2, COLS - near_cols, 2], BF16, name="far_words", offset=2048)
+        far_words = relay.tile([P, 2, COLS - near_cols, 2], BF16, name="far_words", offset=1024)
         for t in range(2):
             gpsimd_round(near_words[:, 0, :, t], window[t][:, near])
-        single = 2 * PIECE - WHOLE_WORDS
-        runs = near_words[:, 1, :, :].rearrange("p (n c) e -> p n c e", c=2 * PIECE)
-        source = window[2][:, near].rearrange("p (n c) -> p n c", c=2 * PIECE)
-        gpsimd_round(runs[:, :, :single, 0], source[:, :, :single])
-        gpsimd_round(runs[:, :, single:, :], source[:, :, single:].unsqueeze(3).to_broadcast([P, NEAR_PIECES // 2, WHOLE_WORDS, 2]))
+        for t in range(2):
+            gpsimd_round(far_words[:, 0, :EXTRA, t], window[t][:, near_cols : near_cols + EXTRA])
+        for first, last in ((0, 2 * PIECE), (2 * PIECE, 3 * PIECE)):
+            gpsimd_round(near_words[:, 1, first : last - WHOLE_WORDS, 0], window[2][:, first : last - WHOLE_WORDS])
+        ends = near_words[:, 1, :, :].rearrange("p (n c) e -> p n c e", c=PIECE)[:, 1:3, PIECE - WHOLE_WORDS :, :]
+        source = window[2][:, near].rearrange("p (n c) -> p n c", c=PIECE)[:, 1:3, PIECE - WHOLE_WORDS :]
+        gpsimd_round(ends, source.unsqueeze(3).to_broadcast([P, 2, WHOLE_WORDS, 2]))
+        nc.vector.tensor_copy(out=near_words[:, 1, piece(3), 0], in_=window[2][:, piece(3)])
         for t in range(LANES - 1):
-            nc.scalar.copy(out=far_words[:, t // 2, :, t % 2], in_=window[t][:, far])
+            skip = EXTRA if t < 2 else 0
+            nc.scalar.copy(out=far_words[:, t // 2, skip:, t % 2], in_=window[t][:, near_cols + skip :])
         for first in range(0, near_cols, 2 * PIECE):
             nc.vector.tensor_copy(out=near_words[:, 1, first : first + 2 * PIECE, 1], in_=window[3][:, first : first + 2 * PIECE])
         for k in range(NEAR_PIECES, PIECES):
             nc.scalar.copy(out=far_words[:, 1, piece(k - NEAR_PIECES), 1], in_=window[3][:, piece(k)])
 
-        out_codes = sb("out_codes", [P, COLS], U32)
+        out_codes = [
+            sb("out_codes%d" % first, [P, (last - first) * PIECE], U32)
+            for first, last in zip(STORE_EDGES, STORE_EDGES[1:])
+        ]
         out_scales = sb("out_scales", [P, 2 * PIECE], U8)
         code_rows = out_1[0].rearrange("p c l -> p (c l)").bitcast(I32)
 
@@ -364,14 +379,14 @@ def tile_attend_gahead_sam_log_pl_kernel(tc, wT, mT, xT, y, ts, us, wt, offs, ou
 
         def quantise_out(k):
             side = slice((k % 2) * PIECE, (k % 2 + 1) * PIECE)
+            n = max(e for e, first in enumerate(STORE_EDGES) if first <= k)
             nc.vector.quantize_mx(
-                out=out_codes[:, piece(k)].bitcast(E4M3),
+                out=out_codes[n][:, piece(k - STORE_EDGES[n])].bitcast(E4M3),
                 scales=out_scales[4 * (k // 2) :, side],
                 in_=woven[k][:].rearrange("p c t -> p (c t)"),
             )
-            if k + 1 in STORE_EDGES:
-                cols = slice(STORE_EDGES[list(STORE_EDGES).index(k + 1) - 1] * PIECE, (k + 1) * PIECE)
-                nc.sync.dma_start(out=code_rows[:, cols], in_=out_codes[:, cols].bitcast(I32))
+            if k + 1 == STORE_EDGES[n + 1]:
+                nc.sync.dma_start(out=code_rows[:, STORE_EDGES[n] * PIECE : (k + 1) * PIECE], in_=out_codes[n][:].bitcast(I32))
 
         weave(0)
         for k in range(PIECES):

@@ -280,6 +280,18 @@ def tile_attend_gahead_sam_log_pl_kernel(tc, wT, mT, xT, y, ts, us, wt, offs, ou
             )
 
         finish_w2(0, parts=2)
+        idle = psum.tile([P, R], F32, name="idle", tag="a3")
+        nc.tensor.transpose(idle[:, :P], m_table[3][:, :P], ident_f32[:])
+        for n in range(2):
+            nc.tensor.matmul_mx(
+                out=idle[:],
+                lhsT=xd_codes[:, :P].bitcast(E4M3),
+                lhsT_scale=xd_scales[:, :P],
+                rhs=xd_codes[:].bitcast(E4M3),
+                rhs_scale=xd_scales[:],
+                start=True,
+                stop=True,
+            )
         finish_w2(1)
         finish_w2(2)
         score(0)

@@ -24,10 +24,11 @@ CHUNKS = SLOTS // CHUNK
 PIECE = 256
 PIECES = COLS // PIECE
 WHOLE_WORDS = 16
-NEAR_PIECES = 4
+NEAR_PIECES = 3
 STORE_EDGES = (0, 3, 5, 7, 8)
 SCALAR_WEAVES = 4
-EXTRA = 192
+EXTRA = 256 + 192
+FILL = 64
 FOLD = COLS // P
 TURNED = CHUNKS - 1
 
@@ -83,7 +84,7 @@ def tile_attend_gahead_sam_log_pl_kernel(tc, wT, mT, xT, y, ts, us, wt, offs, ou
         for t in range(LANES):
             nc.vector.memset(window[t][:], 0.0)
 
-        zeros = sb("zeros", [P, CHUNK], F32)
+        zeros = sb("zeros", [P, FILL], F32)
         nc.vector.memset(zeros[:], 0.0)
 
         x_by_d = sb("x_by_d", [P, LANES, P, LANES], BF16)
@@ -190,14 +191,14 @@ def tile_attend_gahead_sam_log_pl_kernel(tc, wT, mT, xT, y, ts, us, wt, offs, ou
                     start=True,
                     stop=True,
                 )
-            copy(out=into[:], in_=sums[:])
+            copy(out=into, in_=sums[:])
 
         def scatter(t, slots, source, on_scalar=False):
             out = window[t][:].indirect(slot_list(slots.start, slots.stop - slots.start))
             if not on_scalar:
-                nc.vector.tensor_copy(out=out, in_=source[:])
+                nc.vector.tensor_copy(out=out, in_=source)
             else:
-                nc.scalar.activation(out=out, in_=source[:], func=ACT.Copy)
+                nc.scalar.activation(out=out, in_=source, func=ACT.Copy)
 
         def finish_w2(j, parts=1):
             width = CHUNK // parts
@@ -315,19 +316,17 @@ def tile_attend_gahead_sam_log_pl_kernel(tc, wT, mT, xT, y, ts, us, wt, offs, ou
             if pair == 0:
                 quantise_g(chunks[1])
         early = [sb("dw_early%d" % t, [P, half], F32) for t in range(2)]
-        filler = sb("dw_filler", [P, CHUNK], F32)
-        table_gradient(2, "b2", [chunk(0)], filler, nc.scalar.copy)
-        table_gradient(0, "b0", [first_half], early[0], nc.scalar.copy)
-        table_gradient(1, "b3", [first_half], early[1], nc.scalar.copy)
-        scatter(0, first_half, early[0], on_scalar=True)
+        dw2 = sb("dw2", [P, SLOTS], F32)
+        table_gradient(0, "b0", [first_half], early[0][:], nc.scalar.copy)
+        table_gradient(1, "b3", [first_half], early[1][:], nc.scalar.copy)
+        scatter(0, first_half, early[0][:], on_scalar=True)
+        table_gradient(2, "b2", [chunk(0)], dw2[:, chunk(0)], nc.vector.tensor_copy)
         quantise_g(3)
-        nc.vector.tensor_tensor(out=window[2][:].indirect(slot_list(0, CHUNK)), in0=filler[:], in1=zeros[:], op=ALU.add)
+        nc.vector.tensor_tensor(out=window[2][:].indirect(slot_list(0, FILL)), in0=dw2[:, :FILL], in1=zeros[:], op=ALU.add)
 
         out_rows = out_0.rearrange("(p t) c -> p t c", t=LANES)
         near_cols = NEAR_PIECES * PIECE
         near = slice(0, near_cols)
-        dead = ("m_table0", "m_table1", "m_table2", "m_table3", "w_pair0", "w_pair1", "x", "ts_table")
-        woven = [sb("woven%d" % k, [P, PIECE, LANES], BF16, dead[k]) for k in range(PIECES)]
 
         def piece(k):
             return slice(k * PIECE, (k + 1) * PIECE)
@@ -335,19 +334,19 @@ def tile_attend_gahead_sam_log_pl_kernel(tc, wT, mT, xT, y, ts, us, wt, offs, ou
         def store_plane(t):
             nc.sync.dma_start(out=out_rows[:, t, :], in_=window[t][:])
 
-        scatter(1, first_half, early[1])
-        rest = slice(CHUNK, SLOTS)
-        late = [sb("dw_late%d" % t, [P, (half, half, SLOTS - CHUNK)[t]], F32) for t in range(LANES - 1)]
+        scatter(1, first_half, early[1][:])
+        late = [sb("dw_late%d" % t, [P, half], F32) for t in range(2)]
         dw_scalar = relay.tile([P, half], F32, name="dw_scalar", offset=512)
-        table_gradient(0, "a0", [second_half], late[0], nc.scalar.copy)
-        table_gradient(1, "a1", [second_half], late[1], nc.scalar.copy)
-        table_gradient(2, "a2", [chunk(1), second_half], late[2], nc.scalar.copy)
-        table_gradient(3, "a0", [first_half], dw_scalar, nc.scalar.copy)
-        scatter(3, first_half, dw_scalar, on_scalar=True)
-        late.append(relay.tile([P, half], F32, name="dw_late3", offset=0))
-        table_gradient(3, "a3", [second_half], late[3], nc.scalar.copy)
-        for t in range(LANES):
-            scatter(t, rest if t == 2 else second_half, late[t])
+        dw_last = relay.tile([P, half], F32, name="dw_last", offset=0)
+        table_gradient(0, "a0", [second_half], late[0][:], nc.scalar.copy)
+        table_gradient(1, "a1", [second_half], late[1][:], nc.scalar.copy)
+        table_gradient(2, "a2", [chunk(1), second_half], dw2[:, CHUNK:], nc.scalar.copy)
+        table_gradient(3, "a0", [first_half], dw_scalar[:], nc.scalar.copy)
+        scatter(3, first_half, dw_scalar[:], on_scalar=True)
+        table_gradient(3, "a3", [second_half], dw_last[:], nc.scalar.copy)
+        last_runs = ((second_half, late[0][:]), (second_half, late[1][:]), (slice(FILL, SLOTS), dw2[:, FILL:]), (second_half, dw_last[:]))
+        for t, (slots, source) in enumerate(last_runs):
+            scatter(t, slots, source)
             store_plane(t)
 
         def gpsimd_round(out, source):
@@ -359,20 +358,28 @@ def tile_attend_gahead_sam_log_pl_kernel(tc, wT, mT, xT, y, ts, us, wt, offs, ou
             gpsimd_round(near_words[:, 0, :, t], window[t][:, near])
         for t in range(2):
             gpsimd_round(far_words[:, 0, :EXTRA, t], window[t][:, near_cols : near_cols + EXTRA])
-        for first, last in ((0, 2 * PIECE), (2 * PIECE, 3 * PIECE)):
-            gpsimd_round(near_words[:, 1, first : last - WHOLE_WORDS, 0], window[2][:, first : last - WHOLE_WORDS])
-        ends = near_words[:, 1, :, :].rearrange("p (n c) e -> p n c e", c=PIECE)[:, 1:3, PIECE - WHOLE_WORDS :, :]
-        source = window[2][:, near].rearrange("p (n c) -> p n c", c=PIECE)[:, 1:3, PIECE - WHOLE_WORDS :]
+        runs = (slice(0, 2 * PIECE), slice(2 * PIECE, near_cols))
+        for run in runs:
+            gpsimd_round(near_words[:, 1, run.start : run.stop - WHOLE_WORDS, 0], window[2][:, run.start : run.stop - WHOLE_WORDS])
+        ends = near_words[:, 1, :, :].rearrange("p (n c) e -> p n c e", c=PIECE)[:, 1:, PIECE - WHOLE_WORDS :, :]
+        source = window[2][:, near].rearrange("p (n c) -> p n c", c=PIECE)[:, 1:, PIECE - WHOLE_WORDS :]
         gpsimd_round(ends, source.unsqueeze(3).to_broadcast([P, 2, WHOLE_WORDS, 2]))
-        nc.vector.tensor_copy(out=near_words[:, 1, piece(3), 0], in_=window[2][:, piece(3)])
         for t in range(LANES - 1):
-            skip = EXTRA if t < 2 else 0
+            skip = EXTRA if t < 2 else PIECE
             nc.scalar.copy(out=far_words[:, t // 2, skip:, t % 2], in_=window[t][:, near_cols + skip :])
-        for first in range(0, near_cols, 2 * PIECE):
-            nc.vector.tensor_copy(out=near_words[:, 1, first : first + 2 * PIECE, 1], in_=window[3][:, first : first + 2 * PIECE])
-        for k in range(NEAR_PIECES, PIECES):
+        nc.vector.tensor_copy(
+            out=far_words[:, 1, :WHOLE_WORDS, :],
+            in_=window[3][:, near_cols : near_cols + WHOLE_WORDS].unsqueeze(2).to_broadcast([P, WHOLE_WORDS, 2]),
+        )
+        nc.vector.tensor_copy(out=far_words[:, 1, WHOLE_WORDS:PIECE, 1], in_=window[3][:, near_cols + WHOLE_WORDS : near_cols + PIECE])
+        nc.vector.tensor_copy(out=far_words[:, 1, :PIECE, 0], in_=window[2][:, piece(NEAR_PIECES)])
+        for run in runs:
+            nc.vector.tensor_copy(out=near_words[:, 1, run, 1], in_=window[3][:, run])
+        for k in range(NEAR_PIECES + 1, PIECES):
             nc.scalar.copy(out=far_words[:, 1, piece(k - NEAR_PIECES), 1], in_=window[3][:, piece(k)])
 
+        dead = ("m_table0", "m_table1", "m_table2", "near_words", "w_pair0", "w_pair1", "x", "ts_table")
+        woven = [sb("woven%d" % k, [P, PIECE, LANES], BF16, dead[k]) for k in range(PIECES)]
         out_codes = [
             sb("out_codes%d" % first, [P, (last - first) * PIECE], U32)
             for first, last in zip(STORE_EDGES, STORE_EDGES[1:])

@@ -27,7 +27,7 @@ WHOLE_WORDS = 16
 NEAR_PIECES = 3
 STORE_EDGES = (0, 3, 5, 7, 8)
 SCALAR_WEAVES = 4
-EXTRA = 256 + 192
+EXTRA = 256 + 256
 FILL = 64
 FOLD = COLS // P
 TURNED = CHUNKS - 1
@@ -337,13 +337,13 @@ def tile_attend_gahead_sam_log_pl_kernel(tc, wT, mT, xT, y, ts, us, wt, offs, ou
         scatter(1, first_half, early[1][:])
         late = [sb("dw_late%d" % t, [P, half], F32) for t in range(2)]
         dw_scalar = relay.tile([P, half], F32, name="dw_scalar", offset=512)
-        dw_last = relay.tile([P, half], F32, name="dw_last", offset=0)
+        dw_last = sb("dw_last", [P, half], F32)
         table_gradient(0, "a0", [second_half], late[0][:], nc.scalar.copy)
         table_gradient(1, "a1", [second_half], late[1][:], nc.scalar.copy)
         table_gradient(2, "a2", [chunk(1), second_half], dw2[:, CHUNK:], nc.scalar.copy)
         table_gradient(3, "a0", [first_half], dw_scalar[:], nc.scalar.copy)
         scatter(3, first_half, dw_scalar[:], on_scalar=True)
-        table_gradient(3, "a3", [second_half], dw_last[:], nc.scalar.copy)
+        table_gradient(3, "a1", [second_half], dw_last[:], nc.scalar.copy)
         last_runs = ((second_half, late[0][:]), (second_half, late[1][:]), (slice(FILL, SLOTS), dw2[:, FILL:]), (second_half, dw_last[:]))
         for t, (slots, source) in enumerate(last_runs):
             scatter(t, slots, source)

@@ -26,8 +26,8 @@ PIECES = COLS // PIECE
 WHOLE_WORDS = 16
 NEAR_PIECES = 3
 STORE_EDGES = (0, 3, 5, 7, 8)
-SCALAR_WEAVES = 4
-EXTRA = 256 + 256
+SCALAR_WEAVES = 3
+EXTRA = 512
 FILL = 64
 FOLD = COLS // P
 TURNED = CHUNKS - 1
@@ -365,20 +365,14 @@ def tile_attend_gahead_sam_log_pl_kernel(tc, wT, mT, xT, y, ts, us, wt, offs, ou
         source = window[2][:, near].rearrange("p (n c) -> p n c", c=PIECE)[:, 1:, PIECE - WHOLE_WORDS :]
         gpsimd_round(ends, source.unsqueeze(3).to_broadcast([P, 2, WHOLE_WORDS, 2]))
         for t in range(LANES - 1):
-            skip = EXTRA if t < 2 else PIECE
+            skip = EXTRA if t < 2 else 0
             nc.scalar.copy(out=far_words[:, t // 2, skip:, t % 2], in_=window[t][:, near_cols + skip :])
-        nc.vector.tensor_copy(
-            out=far_words[:, 1, :WHOLE_WORDS, :],
-            in_=window[3][:, near_cols : near_cols + WHOLE_WORDS].unsqueeze(2).to_broadcast([P, WHOLE_WORDS, 2]),
-        )
-        nc.vector.tensor_copy(out=far_words[:, 1, WHOLE_WORDS:PIECE, 1], in_=window[3][:, near_cols + WHOLE_WORDS : near_cols + PIECE])
-        nc.vector.tensor_copy(out=far_words[:, 1, :PIECE, 0], in_=window[2][:, piece(NEAR_PIECES)])
         for run in runs:
             nc.vector.tensor_copy(out=near_words[:, 1, run, 1], in_=window[3][:, run])
-        for k in range(NEAR_PIECES + 1, PIECES):
+        for k in range(NEAR_PIECES, PIECES):
             nc.scalar.copy(out=far_words[:, 1, piece(k - NEAR_PIECES), 1], in_=window[3][:, piece(k)])
 
-        dead = ("m_table0", "m_table1", "m_table2", "near_words", "w_pair0", "w_pair1", "x", "ts_table")
+        dead = ("m_table0", "m_table1", "m_table2", "m_table3", "w_pair0", "w_pair1", "x", "ts_table")
         woven = [sb("woven%d" % k, [P, PIECE, LANES], BF16, dead[k]) for k in range(PIECES)]
         out_codes = [
             sb("out_codes%d" % first, [P, (last - first) * PIECE], U32)

@@ -37,7 +37,6 @@ def tile_attend_gahead_sam_log_pl_kernel(tc, wT, mT, xT, y, ts, us, wt, offs, ou
     nc = tc.nc
     with ExitStack() as ctx:
         keep = ctx.enter_context(tc.tile_pool(name="keep", bufs=1))
-        relay = ctx.enter_context(tc.tile_pool(name="relay", bufs=1))
         psum = ctx.enter_context(tc.psum_pool(name="psum", bufs=1))
 
         def sb(name, shape, dtype, tag=None):
@@ -63,15 +62,16 @@ def tile_attend_gahead_sam_log_pl_kernel(tc, wT, mT, xT, y, ts, us, wt, offs, ou
 
         w_rows = wT.rearrange("(p t) c -> p t c", t=LANES)
         m_rows = mT.rearrange("(p t) c -> p t c", t=LANES)
-        w_table, m_table = [], []
-        for h in range(2):
-            w_pair = sb("w_pair%d" % h, [P, 2, COLS], F32)
-            nc.sync.dma_start(out=w_pair[:], in_=w_rows[:, 2 * h : 2 * h + 2, :])
-            for e in range(2):
-                t = 2 * h + e
-                w_table.append(w_pair[:, e, :])
-                m_table.append(sb("m_table%d" % t, [P, COLS], F32))
-                nc.sync.dma_start(out=m_table[t][:], in_=m_rows[:, t, :])
+        w_pair = [sb("w_pair%d" % h, [P, 2, COLS], F32) for h in range(2)]
+        m_pair = sb("m_pair", [P, 2 * COLS], F32)
+        m_table = {t: sb("m_table%d" % t, [P, COLS], F32) for t in (2, 3)}
+        nc.sync.dma_start(out=w_pair[0][:], in_=w_rows[:, 0:2, :])
+        nc.sync.dma_start(out=m_pair[:].rearrange("p (t c) -> p t c", t=2), in_=m_rows[:, 0:2, :])
+        nc.sync.dma_start(out=w_pair[1][:], in_=w_rows[:, 2:4, :])
+        for t in (2, 3):
+            nc.sync.dma_start(out=m_table[t][:], in_=m_rows[:, t, :])
+        m_table[0] = m_pair
+        w_table = [w_pair[t // 2][:, t % 2, :] for t in range(LANES)]
         labels = sb("labels", [P, LANES, SLOTS], F32)
         nc.sync.dma_start(out=labels[:], in_=y.rearrange("(p u) i -> p u i", u=LANES))
 
@@ -163,8 +163,11 @@ def tile_attend_gahead_sam_log_pl_kernel(tc, wT, mT, xT, y, ts, us, wt, offs, ou
 
         for t in range(LANES):
             nc.vector.tensor_copy(out=w_picked[t][:], in_=w_table[t].indirect(offsets[:]))
-            if t < 2:
-                add_listed(t, w2_early[:, t, :], 0, SLOTS)
+            if t == 1:
+                add_listed(0, w2_early[:, 0, :], 0, SLOTS)
+                m_picked = sb("m_picked", [P, SLOTS], F32)
+                nc.vector.tensor_copy(out=m_picked[:], in_=m_pair[:, COLS:].indirect(offsets[:]))
+                nc.vector.tensor_tensor(out=w2_early[:, 1, :], in0=m_picked[:], in1=w_picked[1][:], op=ALU.add)
         for j in range(CHUNKS):
             nc.scalar.copy(out=w2_by_d[j][:, :, 0:2], in_=w2_early[:, :, chunk(j)].rearrange("p t i -> p i t"))
             add_listed(2, w2_late[j][:, 0, :], j * CHUNK, CHUNK)
@@ -336,13 +339,16 @@ def tile_attend_gahead_sam_log_pl_kernel(tc, wT, mT, xT, y, ts, us, wt, offs, ou
 
         scatter(1, first_half, early[1][:])
         late = [sb("dw_late%d" % t, [P, half], F32) for t in range(2)]
-        dw_scalar = relay.tile([P, half], F32, name="dw_scalar", offset=512)
+        far_cols = COLS - near_cols
+        far_flat = sb("far_flat", [P, 4 * far_cols], BF16)
+        far_words = far_flat[:].rearrange("p (h c e) -> p h c e", h=2, e=2)
+        dw_scalar = far_flat[:].bitcast(F32)[:, far_cols - half // 2 : far_cols + half // 2]
         dw_last = sb("dw_last", [P, half], F32)
         table_gradient(0, "a0", [second_half], late[0][:], nc.scalar.copy)
         table_gradient(1, "a1", [second_half], late[1][:], nc.scalar.copy)
         table_gradient(2, "a2", [chunk(1), second_half], dw2[:, CHUNK:], nc.scalar.copy)
-        table_gradient(3, "a0", [first_half], dw_scalar[:], nc.scalar.copy)
-        scatter(3, first_half, dw_scalar[:], on_scalar=True)
+        table_gradient(3, "a0", [first_half], dw_scalar, nc.scalar.copy)
+        scatter(3, first_half, dw_scalar, on_scalar=True)
         table_gradient(3, "a1", [second_half], dw_last[:], nc.scalar.copy)
         last_runs = ((second_half, late[0][:]), (second_half, late[1][:]), (slice(FILL, SLOTS), dw2[:, FILL:]), (second_half, dw_last[:]))
         for t, (slots, source) in enumerate(last_runs):
@@ -353,10 +359,8 @@ def tile_attend_gahead_sam_log_pl_kernel(tc, wT, mT, xT, y, ts, us, wt, offs, ou
             nc.gpsimd.tensor_scalar(out=out, in0=source, scalar1=1.0, scalar2=0.0, op0=ALU.mult, op1=ALU.add)
 
         near_words = sb("near_words", [P, 2, near_cols, 2], BF16)
-        far_words = relay.tile([P, 2, COLS - near_cols, 2], BF16, name="far_words", offset=1024)
         for t in range(2):
             gpsimd_round(near_words[:, 0, :, t], window[t][:, near])
-        for t in range(2):
             gpsimd_round(far_words[:, 0, :EXTRA, t], window[t][:, near_cols : near_cols + EXTRA])
         runs = (slice(0, 2 * PIECE), slice(2 * PIECE, near_cols))
         for run in runs:
@@ -372,7 +376,7 @@ def tile_attend_gahead_sam_log_pl_kernel(tc, wT, mT, xT, y, ts, us, wt, offs, ou
         for k in range(NEAR_PIECES, PIECES):
             nc.scalar.copy(out=far_words[:, 1, piece(k - NEAR_PIECES), 1], in_=window[3][:, piece(k)])
 
-        dead = ("m_table0", "m_table1", "m_table2", "m_table3", "w_pair0", "w_pair1", "x", "ts_table")
+        dead = ("m_pair", "labels", "m_table2", "m_table3", "w_pair0", "w_pair1", "x", "ts_table")
         woven = [sb("woven%d" % k, [P, PIECE, LANES], BF16, dead[k]) for k in range(PIECES)]
         out_codes = [
             sb("out_codes%d" % first, [P, (last - first) * PIECE], U32)
@@ -382,8 +386,8 @@ def tile_attend_gahead_sam_log_pl_kernel(tc, wT, mT, xT, y, ts, us, wt, offs, ou
         code_rows = out_1[0].rearrange("p c l -> p (c l)").bitcast(I32)
 
         def weave(k):
-            halves, place = (near_words, k) if k < NEAR_PIECES else (far_words, k - NEAR_PIECES)
-            words = halves[:].rearrange("p h c e -> p (h c e)").bitcast(F32).rearrange("p (h c) -> p c h", h=2)
+            halves, place = (near_words[:], k) if k < NEAR_PIECES else (far_words, k - NEAR_PIECES)
+            words = halves.rearrange("p h c e -> p (h c e)").bitcast(F32).rearrange("p (h c) -> p c h", h=2)
             copy = nc.scalar.copy if k >= PIECES - SCALAR_WEAVES else nc.vector.tensor_copy
             copy(
                 out=woven[k][:].rearrange("p c t -> p (c t)").bitcast(F32).rearrange("p (c h) -> p c h", h=2),

@@ -63,14 +63,11 @@ def tile_attend_gahead_sam_log_pl_kernel(tc, wT, mT, xT, y, ts, us, wt, offs, ou
         w_rows = wT.rearrange("(p t) c -> p t c", t=LANES)
         m_rows = mT.rearrange("(p t) c -> p t c", t=LANES)
         w_pair = [sb("w_pair%d" % h, [P, 2, COLS], F32) for h in range(2)]
-        m_pair = sb("m_pair", [P, 2 * COLS], F32)
-        m_table = {t: sb("m_table%d" % t, [P, COLS], F32) for t in (2, 3)}
-        nc.sync.dma_start(out=w_pair[0][:], in_=w_rows[:, 0:2, :])
-        nc.sync.dma_start(out=m_pair[:].rearrange("p (t c) -> p t c", t=2), in_=m_rows[:, 0:2, :])
-        nc.sync.dma_start(out=w_pair[1][:], in_=w_rows[:, 2:4, :])
-        for t in (2, 3):
+        m_table = [sb("m_table%d" % t, [P, COLS], F32) for t in range(LANES)]
+        for t in range(LANES):
+            if t < 2:
+                nc.sync.dma_start(out=w_pair[t][:], in_=w_rows[:, 2 * t : 2 * t + 2, :])
             nc.sync.dma_start(out=m_table[t][:], in_=m_rows[:, t, :])
-        m_table[0] = m_pair
         w_table = [w_pair[t // 2][:, t % 2, :] for t in range(LANES)]
         labels = sb("labels", [P, LANES, SLOTS], F32)
         nc.sync.dma_start(out=labels[:], in_=y.rearrange("(p u) i -> p u i", u=LANES))
@@ -163,11 +160,8 @@ def tile_attend_gahead_sam_log_pl_kernel(tc, wT, mT, xT, y, ts, us, wt, offs, ou
 
         for t in range(LANES):
             nc.vector.tensor_copy(out=w_picked[t][:], in_=w_table[t].indirect(offsets[:]))
-            if t == 1:
-                add_listed(0, w2_early[:, 0, :], 0, SLOTS)
-                m_picked = sb("m_picked", [P, SLOTS], F32)
-                nc.vector.tensor_copy(out=m_picked[:], in_=m_pair[:, COLS:].indirect(offsets[:]))
-                nc.vector.tensor_tensor(out=w2_early[:, 1, :], in0=m_picked[:], in1=w_picked[1][:], op=ALU.add)
+            if t < 2:
+                add_listed(t, w2_early[:, t, :], 0, SLOTS)
         for j in range(CHUNKS):
             nc.scalar.copy(out=w2_by_d[j][:, :, 0:2], in_=w2_early[:, :, chunk(j)].rearrange("p t i -> p i t"))
             add_listed(2, w2_late[j][:, 0, :], j * CHUNK, CHUNK)
@@ -376,7 +370,7 @@ def tile_attend_gahead_sam_log_pl_kernel(tc, wT, mT, xT, y, ts, us, wt, offs, ou
         for k in range(NEAR_PIECES, PIECES):
             nc.scalar.copy(out=far_words[:, 1, piece(k - NEAR_PIECES), 1], in_=window[3][:, piece(k)])
 
-        dead = ("m_pair", "labels", "m_table2", "m_table3", "w_pair0", "w_pair1", "x", "ts_table")
+        dead = ("m_table0", "m_table1", "m_table2", "m_table3", "w_pair0", "w_pair1", "x", "ts_table")
         woven = [sb("woven%d" % k, [P, PIECE, LANES], BF16, dead[k]) for k in range(PIECES)]
         out_codes = [
             sb("out_codes%d" % first, [P, (last - first) * PIECE], U32)

@@ -62,14 +62,14 @@ def tile_attend_gahead_sam_log_pl_kernel(tc, wT, mT, xT, y, ts, us, wt, offs, ou
 
         w_rows = wT.rearrange("(p t) c -> p t c", t=LANES)
         m_rows = mT.rearrange("(p t) c -> p t c", t=LANES)
-        w_pair = [sb("w_pair%d" % h, [P, 2, COLS], F32) for h in range(2)]
+        w_table = [sb("w_table%d" % t, [P, COLS], F32) for t in range(LANES)]
         m_table = [sb("m_table%d" % t, [P, COLS], F32) for t in range(LANES)]
         for t in range(LANES):
             if t < 2:
-                nc.sync.dma_start(out=w_pair[t][:], in_=w_rows[:, 2 * t : 2 * t + 2, :])
+                for plane in (2 * t, 2 * t + 1):
+                    nc.sync.dma_start(out=w_table[plane][:], in_=w_rows[:, plane, :])
             nc.sync.dma_start(out=m_table[t][:], in_=m_rows[:, t, :])
-        w_table = [w_pair[t // 2][:, t % 2, :] for t in range(LANES)]
-        labels = sb("labels", [P, LANES, SLOTS], F32)
+        labels = sb("labels", [P, LANES, SLOTS], F32, "m_table2")
         nc.sync.dma_start(out=labels[:], in_=y.rearrange("(p u) i -> p u i", u=LANES))
 
         ident_f32 = sb("ident_f32", [P, P], F32)
@@ -159,7 +159,7 @@ def tile_attend_gahead_sam_log_pl_kernel(tc, wT, mT, xT, y, ts, us, wt, offs, ou
             )
 
         for t in range(LANES):
-            nc.vector.tensor_copy(out=w_picked[t][:], in_=w_table[t].indirect(offsets[:]))
+            nc.vector.tensor_copy(out=w_picked[t][:], in_=w_table[t][:].indirect(offsets[:]))
             if t < 2:
                 add_listed(t, w2_early[:, t, :], 0, SLOTS)
         for j in range(CHUNKS):
@@ -370,7 +370,7 @@ def tile_attend_gahead_sam_log_pl_kernel(tc, wT, mT, xT, y, ts, us, wt, offs, ou
         for k in range(NEAR_PIECES, PIECES):
             nc.scalar.copy(out=far_words[:, 1, piece(k - NEAR_PIECES), 1], in_=window[3][:, piece(k)])
 
-        dead = ("m_table0", "m_table1", "m_table2", "m_table3", "w_pair0", "w_pair1", "x", "ts_table")
+        dead = ("m_table0", "m_table1", "m_table2", "m_table3", "w_table0", "w_table1", "x", "ts_table")
         woven = [sb("woven%d" % k, [P, PIECE, LANES], BF16, dead[k]) for k in range(PIECES)]
         out_codes = [
             sb("out_codes%d" % first, [P, (last - first) * PIECE], U32)

@@ -31,6 +31,7 @@ EXTRA = 512
 FILL = 64
 FOLD = COLS // P
 TURNED = CHUNKS - 1
+HALVED = CHUNKS - 2
 
 
 def tile_attend_gahead_sam_log_pl_kernel(tc, wT, mT, xT, y, ts, us, wt, offs, out_0, out_1, out_2):
@@ -127,16 +128,17 @@ def tile_attend_gahead_sam_log_pl_kernel(tc, wT, mT, xT, y, ts, us, wt, offs, ou
             nc.scalar.copy(out=ts_table[:, 4 * b * P : 4 * (b + 1) * P], in_=spread[:].rearrange("p c n -> p (c n)"))
         ts_all = sb("ts_all", [P, SLOTS], F32)
         nc.vector.tensor_copy(out=ts_all[:], in_=ts_table[:].indirect(offsets[:]))
-        ts_turned = psum.tile([P, P], F32, name="ts_turned", tag="b0")
-        nc.tensor.transpose(ts_turned[:], ts_all[:, TURNED * P : (TURNED + 1) * P], ident_f32[:])
-        ts_col = sb("ts_col", [P, 1], F32)
-        nc.scalar.copy(out=ts_col[:], in_=ts_turned[:, 0:1])
+        ts_turned = psum.tile([P, 2, P], F32, name="ts_turned", tag="b0")
+        for j in (HALVED, TURNED):
+            nc.tensor.transpose(ts_turned[:, j - HALVED, :], ts_all[:, j * P : (j + 1) * P], ident_f32[:])
+        ts_col = sb("ts_col", [P, 2], F32)
+        nc.scalar.copy(out=ts_col[:], in_=ts_turned[:, :, 0])
         wu_col = sb("wu_col", [P, LANES], F32)
         nc.vector.tensor_tensor(out=wu_col[:], in0=wt_col[:], in1=us_col[:], op=ALU.mult)
         logit_scale = [sb("logit_scale%d" % j, [P, LANES, CHUNK], F32) for j in range(TURNED)]
         grad_scale = sb("grad_scale", [P, LANES, SLOTS], F32)
         for j in range(TURNED):
-            for u in range(LANES):
+            for u in range(2 if j == HALVED else LANES):
                 nc.scalar.activation(
                     out=logit_scale[j][:, u, :], in_=ts_all[:, j * CHUNK : (j + 1) * CHUNK], func=ACT.Copy, scale=us_col[:, u : u + 1]
                 )
@@ -222,7 +224,18 @@ def tile_attend_gahead_sam_log_pl_kernel(tc, wT, mT, xT, y, ts, us, wt, offs, ou
                     stop=True,
                 )
                 return
-            for u in range(LANES):
+            if j == HALVED:
+                scores.append(psum.tile([P, 2, P], F32, name="scores_across", tag="b0"))
+                nc.tensor.matmul_mx(
+                    out=scores[CHUNKS][:].rearrange("i u s -> i (u s)"),
+                    lhsT=w2_codes[j][:].bitcast(E4M3),
+                    lhsT_scale=w2_scales[j][:],
+                    rhs=xd_codes[:, 2 * P :].bitcast(E4M3),
+                    rhs_scale=xd_scales[:, 2 * P :],
+                    start=True,
+                    stop=True,
+                )
+            for u in range(2 if j == HALVED else LANES):
                 rows = slice(u * P, (u + 1) * P)
                 nc.tensor.matmul_mx(
                     out=(scores[j][u // 2] if j == 0 else scores[j])[:, u, :],
@@ -245,9 +258,24 @@ def tile_attend_gahead_sam_log_pl_kernel(tc, wT, mT, xT, y, ts, us, wt, offs, ou
             nc.vector.tensor_tensor(out=work[j][:], in0=scores[j][:], in1=logit_scale[j][:], op=ALU.mult)
             nc.scalar.activation(out=work[j][:], in_=work[j][:], func=ACT.Sigmoid)
 
+        def half_logits(j):
+            nc.vector.tensor_tensor(out=work[j][:, :2, :], in0=scores[j][:, :2, :], in1=logit_scale[j][:, :2, :], op=ALU.mult)
+            nc.scalar.activation(out=work[j][:, :2, :], in_=work[j][:, :2, :], func=ACT.Sigmoid)
+
+        def half_turn(j):
+            scaled = sb("half_scaled", [P, 2, P], F32, "logit_scale0")
+            nc.scalar.activation(out=scaled[:], in_=scores[CHUNKS][:], func=ACT.Copy, scale=ts_col[:, 0:1])
+            scores[CHUNKS] = psum.tile([P, 2, CHUNK], F32, name="half_back", tag="a1")
+            for u in range(2):
+                nc.tensor.transpose(scores[CHUNKS][:, u, :], scaled[:, u, :], ident_f32[:])
+
+        def half_sigmoid(j):
+            for u in range(2, LANES):
+                nc.scalar.activation(out=work[j][:, u, :], in_=scores[CHUNKS][:, u - 2, :], func=ACT.Sigmoid, scale=us_col[:, u : u + 1])
+
         def turned_logits(j):
             scaled = sb("scaled", [P, LANES, P], F32, "logit_scale%d" % (j - 1))
-            nc.scalar.activation(out=scaled[:], in_=scores[j][:], func=ACT.Copy, scale=ts_col[:])
+            nc.scalar.activation(out=scaled[:], in_=scores[j][:], func=ACT.Copy, scale=ts_col[:, 1:2])
             scores[j] = psum.tile([P, LANES, CHUNK], F32, name="back", tag="b3")
             for u in range(LANES):
                 nc.tensor.transpose(scores[j][:, u, :], scaled[:, u, :], ident_f32[:])
@@ -298,10 +326,12 @@ def tile_attend_gahead_sam_log_pl_kernel(tc, wT, mT, xT, y, ts, us, wt, offs, ou
         score(2)
         first_logits(0)
         first_logits(1)
-        score(3)
         logits(1)
+        half_turn(2)
+        score(3)
         turned_logits(3)
-        logits(2)
+        half_logits(2)
+        half_sigmoid(2)
         turned_sigmoid(3)
         for pair in range(2):
             chunks = (2 * pair, 2 * pair + 1)

@@ -344,7 +344,8 @@ def tile_attend_gahead_sam_log_pl_kernel(tc, wT, mT, xT, y, ts, us, wt, offs, ou
                 quantise_g(chunks[1])
         early = [sb("dw_early%d" % t, [P, half], F32) for t in range(2)]
         dw2 = sb("dw2", [P, SLOTS], F32)
-        table_gradient(0, "b0", [first_half], early[0][:], nc.scalar.copy)
+        table_gradient(0, "b0", [chunk(0)], early[0][:, chunk(0)], nc.scalar.copy)
+        table_gradient(0, "b1", [chunk(1)], early[0][:, chunk(1)], nc.scalar.copy)
         table_gradient(1, "b3", [first_half], early[1][:], nc.scalar.copy)
         scatter(0, first_half, early[0][:], on_scalar=True)
         table_gradient(2, "b2", [chunk(0)], dw2[:, chunk(0)], nc.vector.tensor_copy)
@@ -387,11 +388,11 @@ def tile_attend_gahead_sam_log_pl_kernel(tc, wT, mT, xT, y, ts, us, wt, offs, ou
             gpsimd_round(near_words[:, 0, :, t], window[t][:, near])
             gpsimd_round(far_words[:, 0, :EXTRA, t], window[t][:, near_cols : near_cols + EXTRA])
         runs = (slice(0, 2 * PIECE), slice(2 * PIECE, near_cols))
-        for run in runs:
-            gpsimd_round(near_words[:, 1, run.start : run.stop - WHOLE_WORDS, 0], window[2][:, run.start : run.stop - WHOLE_WORDS])
-        ends = near_words[:, 1, :, :].rearrange("p (n c) e -> p n c e", c=PIECE)[:, 1:, PIECE - WHOLE_WORDS :, :]
-        source = window[2][:, near].rearrange("p (n c) -> p n c", c=PIECE)[:, 1:, PIECE - WHOLE_WORDS :]
-        gpsimd_round(ends, source.unsqueeze(3).to_broadcast([P, 2, WHOLE_WORDS, 2]))
+        single = PIECE - WHOLE_WORDS
+        target = near_words[:, 1, :, :].rearrange("p (n c) e -> p n c e", c=PIECE)
+        source = window[2][:, near].rearrange("p (n c) -> p n c", c=PIECE)
+        gpsimd_round(target[:, :, :single, 0], source[:, :, :single])
+        gpsimd_round(target[:, :, single:, :], source[:, :, single:].unsqueeze(3).to_broadcast([P, NEAR_PIECES, WHOLE_WORDS, 2]))
         for t in range(LANES - 1):
             skip = EXTRA if t < 2 else 0
             nc.scalar.copy(out=far_words[:, t // 2, skip:, t % 2], in_=window[t][:, near_cols + skip :])

@@ -27,8 +27,7 @@ WHOLE_WORDS = 16
 NEAR_PIECES = 3
 STORE_EDGES = (0, 3, 5, 7, 8)
 SCALAR_WEAVES = 3
-EXTRA = 512
-FILL = 64
+POOL_COLS = 1280
 FOLD = COLS // P
 TURNED = CHUNKS - 1
 HALVED = CHUNKS - 2
@@ -80,10 +79,7 @@ def tile_attend_gahead_sam_log_pl_kernel(tc, wT, mT, xT, y, ts, us, wt, offs, ou
 
         window = [sb("window%d" % t, [P, COLS], F32) for t in range(LANES)]
         for t in range(LANES):
-            nc.vector.memset(window[t][:], 0.0)
-
-        zeros = sb("zeros", [P, FILL], F32)
-        nc.vector.memset(zeros[:], 0.0)
+            (nc.vector if t < 2 else nc.gpsimd).memset(window[t][:], 0.0)
 
         x_by_d = sb("x_by_d", [P, LANES, P, LANES], BF16)
         nc.scalar.copy(
@@ -343,14 +339,13 @@ def tile_attend_gahead_sam_log_pl_kernel(tc, wT, mT, xT, y, ts, us, wt, offs, ou
             if pair == 0:
                 quantise_g(chunks[1])
         early = [sb("dw_early%d" % t, [P, half], F32) for t in range(2)]
-        dw2 = sb("dw2", [P, SLOTS], F32)
         table_gradient(0, "b0", [chunk(0)], early[0][:, chunk(0)], nc.scalar.copy)
         table_gradient(0, "b1", [chunk(1)], early[0][:, chunk(1)], nc.scalar.copy)
-        table_gradient(1, "b3", [first_half], early[1][:], nc.scalar.copy)
+        table_gradient(1, "b3", [chunk(1)], early[1][:, chunk(1)], nc.scalar.copy)
         scatter(0, first_half, early[0][:], on_scalar=True)
-        table_gradient(2, "b2", [chunk(0)], dw2[:, chunk(0)], nc.vector.tensor_copy)
+        table_gradient(1, "b2", [chunk(0)], early[1][:, chunk(0)], nc.vector.tensor_copy)
         quantise_g(3)
-        nc.vector.tensor_tensor(out=window[2][:].indirect(slot_list(0, FILL)), in0=dw2[:, :FILL], in1=zeros[:], op=ALU.add)
+        scatter(1, first_half, early[1][:])
 
         out_rows = out_0.rearrange("(p t) c -> p t c", t=LANES)
         near_cols = NEAR_PIECES * PIECE
@@ -359,47 +354,40 @@ def tile_attend_gahead_sam_log_pl_kernel(tc, wT, mT, xT, y, ts, us, wt, offs, ou
         def piece(k):
             return slice(k * PIECE, (k + 1) * PIECE)
 
-        def store_plane(t):
-            nc.sync.dma_start(out=out_rows[:, t, :], in_=window[t][:])
-
-        scatter(1, first_half, early[1][:])
-        late = [sb("dw_late%d" % t, [P, half], F32) for t in range(2)]
-        far_cols = COLS - near_cols
-        far_flat = sb("far_flat", [P, 4 * far_cols], BF16)
-        far_words = far_flat[:].rearrange("p (h c e) -> p h c e", h=2, e=2)
-        dw_scalar = far_flat[:].bitcast(F32)[:, far_cols - half // 2 : far_cols + half // 2]
-        dw_last = sb("dw_last", [P, half], F32)
+        late = [sb("dw_late%d" % t, [P, half], F32) for t in range(3)]
+        pair_flat = sb("pair_flat", [P, LANES * COLS], BF16)
+        pairs = pair_flat[:].rearrange("p (h c e) -> p h c e", h=2, e=2)
+        dw_scalar = pair_flat[:].bitcast(F32)[:, COLS - half : COLS]
+        dw_last = sb("dw_last", [P, SLOTS], F32)
         table_gradient(0, "a0", [second_half], late[0][:], nc.scalar.copy)
         table_gradient(1, "a1", [second_half], late[1][:], nc.scalar.copy)
-        table_gradient(2, "a2", [chunk(1), second_half], dw2[:, CHUNK:], nc.scalar.copy)
-        table_gradient(3, "a0", [first_half], dw_scalar, nc.scalar.copy)
-        scatter(3, first_half, dw_scalar, on_scalar=True)
-        table_gradient(3, "a1", [second_half], dw_last[:], nc.scalar.copy)
-        last_runs = ((second_half, late[0][:]), (second_half, late[1][:]), (slice(FILL, SLOTS), dw2[:, FILL:]), (second_half, dw_last[:]))
+        table_gradient(2, "a2", [second_half], late[2][:], nc.scalar.copy)
+        table_gradient(2, "a0", [first_half], dw_scalar, nc.scalar.copy)
+        scatter(2, first_half, dw_scalar, on_scalar=True)
+        table_gradient(3, "a0", [slice(0, SLOTS)], dw_last[:], nc.scalar.copy)
+        last_runs = [(second_half, late[t][:]) for t in range(3)] + [(slice(0, SLOTS), dw_last[:])]
         for t, (slots, source) in enumerate(last_runs):
             scatter(t, slots, source)
-            store_plane(t)
+            nc.sync.dma_start(out=out_rows[:, t, :], in_=window[t][:])
 
         def gpsimd_round(out, source):
             nc.gpsimd.tensor_scalar(out=out, in0=source, scalar1=1.0, scalar2=0.0, op0=ALU.mult, op1=ALU.add)
 
-        near_words = sb("near_words", [P, 2, near_cols, 2], BF16)
         for t in range(2):
-            gpsimd_round(near_words[:, 0, :, t], window[t][:, near])
-            gpsimd_round(far_words[:, 0, :EXTRA, t], window[t][:, near_cols : near_cols + EXTRA])
+            gpsimd_round(pairs[:, 0, :POOL_COLS, t], window[t][:, :POOL_COLS])
         runs = (slice(0, 2 * PIECE), slice(2 * PIECE, near_cols))
         single = PIECE - WHOLE_WORDS
-        target = near_words[:, 1, :, :].rearrange("p (n c) e -> p n c e", c=PIECE)
+        target = pairs[:, 1, near, :].rearrange("p (n c) e -> p n c e", c=PIECE)
         source = window[2][:, near].rearrange("p (n c) -> p n c", c=PIECE)
         gpsimd_round(target[:, :, :single, 0], source[:, :, :single])
         gpsimd_round(target[:, :, single:, :], source[:, :, single:].unsqueeze(3).to_broadcast([P, NEAR_PIECES, WHOLE_WORDS, 2]))
         for t in range(LANES - 1):
-            skip = EXTRA if t < 2 else 0
-            nc.scalar.copy(out=far_words[:, t // 2, skip:, t % 2], in_=window[t][:, near_cols + skip :])
+            first = POOL_COLS if t < 2 else near_cols
+            nc.scalar.copy(out=pairs[:, t // 2, first:, t % 2], in_=window[t][:, first:])
         for run in runs:
-            nc.vector.tensor_copy(out=near_words[:, 1, run, 1], in_=window[3][:, run])
+            nc.vector.tensor_copy(out=pairs[:, 1, run, 1], in_=window[3][:, run])
         for k in range(NEAR_PIECES, PIECES):
-            nc.scalar.copy(out=far_words[:, 1, piece(k - NEAR_PIECES), 1], in_=window[3][:, piece(k)])
+            nc.scalar.copy(out=pairs[:, 1, piece(k), 1], in_=window[3][:, piece(k)])
 
         dead = ("m_table0", "m_table1", "m_table2", "m_table3", "w_table0", "w_table1", "x", "ts_table")
         woven = [sb("woven%d" % k, [P, PIECE, LANES], BF16, dead[k]) for k in range(PIECES)]
@@ -411,12 +399,11 @@ def tile_attend_gahead_sam_log_pl_kernel(tc, wT, mT, xT, y, ts, us, wt, offs, ou
         code_rows = out_1[0].rearrange("p c l -> p (c l)").bitcast(I32)
 
         def weave(k):
-            halves, place = (near_words[:], k) if k < NEAR_PIECES else (far_words, k - NEAR_PIECES)
-            words = halves.rearrange("p h c e -> p (h c e)").bitcast(F32).rearrange("p (h c) -> p c h", h=2)
+            words = pair_flat[:].bitcast(F32).rearrange("p (h c) -> p c h", h=2)
             copy = nc.scalar.copy if k >= PIECES - SCALAR_WEAVES else nc.vector.tensor_copy
             copy(
                 out=woven[k][:].rearrange("p c t -> p (c t)").bitcast(F32).rearrange("p (c h) -> p c h", h=2),
-                in_=words[:, piece(place), :],
+                in_=words[:, piece(k), :],
             )
 
         def quantise_out(k):

@@ -26,8 +26,9 @@ PIECES = COLS // PIECE
 WHOLE_WORDS = 16
 NEAR_PIECES = 3
 STORE_EDGES = (0, 3, 5, 7, 8)
-SCALAR_WEAVES = 3
+VECTOR_WEAVES = 1152
 POOL_COLS = 1280
+SHORT = 16
 FOLD = COLS // P
 TURNED = CHUNKS - 1
 HALVED = CHUNKS - 2
@@ -172,7 +173,7 @@ def tile_attend_gahead_sam_log_pl_kernel(tc, wT, mT, xT, y, ts, us, wt, offs, ou
         half = SLOTS // 2
         first_half, second_half = slice(0, half), slice(half, SLOTS)
 
-        def table_gradient(t, bank, runs, into, copy):
+        def table_gradient(t, bank, runs, into, copy, skip=0):
             features = slice(t * P, (t + 1) * P)
             base = runs[0].start
             sums = psum.tile([P, runs[-1].stop - base], F32, name="sums%d_%d" % (t, base), tag=bank)
@@ -186,7 +187,8 @@ def tile_attend_gahead_sam_log_pl_kernel(tc, wT, mT, xT, y, ts, us, wt, offs, ou
                     start=True,
                     stop=True,
                 )
-            copy(out=into, in_=sums[:])
+            copy(out=into, in_=sums[:, skip:])
+            return sums
 
         def scatter(t, slots, source, on_scalar=False):
             out = window[t][:].indirect(slot_list(slots.start, slots.stop - slots.start))
@@ -341,9 +343,9 @@ def tile_attend_gahead_sam_log_pl_kernel(tc, wT, mT, xT, y, ts, us, wt, offs, ou
         early = [sb("dw_early%d" % t, [P, half], F32) for t in range(2)]
         table_gradient(0, "b0", [chunk(0)], early[0][:, chunk(0)], nc.scalar.copy)
         table_gradient(0, "b1", [chunk(1)], early[0][:, chunk(1)], nc.scalar.copy)
-        table_gradient(1, "b3", [chunk(1)], early[1][:, chunk(1)], nc.scalar.copy)
+        sums = table_gradient(1, "b2", [first_half], early[1][:, SHORT:], nc.scalar.copy, SHORT)
         scatter(0, first_half, early[0][:], on_scalar=True)
-        table_gradient(1, "b2", [chunk(0)], early[1][:, chunk(0)], nc.vector.tensor_copy)
+        nc.vector.tensor_copy(out=early[1][:, :SHORT], in_=sums[:, :SHORT])
         quantise_g(3)
         scatter(1, first_half, early[1][:])
 
@@ -400,11 +402,12 @@ def tile_attend_gahead_sam_log_pl_kernel(tc, wT, mT, xT, y, ts, us, wt, offs, ou
 
         def weave(k):
             words = pair_flat[:].bitcast(F32).rearrange("p (h c) -> p c h", h=2)
-            copy = nc.scalar.copy if k >= PIECES - SCALAR_WEAVES else nc.vector.tensor_copy
-            copy(
-                out=woven[k][:].rearrange("p c t -> p (c t)").bitcast(F32).rearrange("p (c h) -> p c h", h=2),
-                in_=words[:, piece(k), :],
-            )
+            target = woven[k][:].rearrange("p c t -> p (c t)").bitcast(F32).rearrange("p (c h) -> p c h", h=2)
+            cut = min(max(VECTOR_WEAVES - k * PIECE, 0), PIECE)
+            if cut > 0:
+                nc.vector.tensor_copy(out=target[:, :cut, :], in_=words[:, k * PIECE : k * PIECE + cut, :])
+            if cut < PIECE:
+                nc.scalar.copy(out=target[:, cut:, :], in_=words[:, k * PIECE + cut : (k + 1) * PIECE, :])
 
         def quantise_out(k):
             side = slice((k % 2) * PIECE, (k % 2 + 1) * PIECE)

@@ -71,7 +71,10 @@ def tile_attend_gahead_sam_log_pl_kernel(tc, wT, mT, xT, y, ts, us, wt, offs, ou
                     nc.sync.dma_start(out=w_table[plane][:], in_=w_rows[:, plane, :])
             nc.sync.dma_start(out=m_table[t][:], in_=m_rows[:, t, :])
         labels = sb("labels", [P, LANES, SLOTS], F32, "m_table2")
-        nc.sync.dma_start(out=labels[:], in_=y.rearrange("(p u) i -> p u i", u=LANES))
+        y_rows = y.rearrange("(p u) i -> p u i", u=LANES)
+        for first in range(0, SLOTS, SLOTS // 2):
+            slots = slice(first, first + SLOTS // 2)
+            nc.sync.dma_start(out=labels[:, :, slots], in_=y_rows[:, :, slots])
 
         ident_f32 = sb("ident_f32", [P, P], F32)
         ident_bf16 = sb("ident_bf16", [P, P], BF16)
@@ -381,8 +384,8 @@ def tile_attend_gahead_sam_log_pl_kernel(tc, wT, mT, xT, y, ts, us, wt, offs, ou
         single = PIECE - WHOLE_WORDS
         target = pairs[:, 1, near, :].rearrange("p (n c) e -> p n c e", c=PIECE)
         source = window[2][:, near].rearrange("p (n c) -> p n c", c=PIECE)
-        gpsimd_round(target[:, :, :single, 0], source[:, :, :single])
-        gpsimd_round(target[:, :, single:, :], source[:, :, single:].unsqueeze(3).to_broadcast([P, NEAR_PIECES, WHOLE_WORDS, 2]))
+        gpsimd_round(pairs[:, 1, near, 0], window[2][:, near])
+        nc.vector.tensor_copy(out=target[:, :, single:, :], in_=source[:, :, single:].unsqueeze(3).to_broadcast([P, NEAR_PIECES, WHOLE_WORDS, 2]))
         for t in range(LANES - 1):
             first = POOL_COLS if t < 2 else near_cols
             nc.scalar.copy(out=pairs[:, t // 2, first:, t % 2], in_=window[t][:, first:])

@@ -24,6 +24,7 @@ CHUNKS = SLOTS // CHUNK
 PIECE = 256
 PIECES = COLS // PIECE
 WHOLE_WORDS = 16
+SHARED = 8
 NEAR_PIECES = 3
 STORE_EDGES = (0, 3, 5, 7, 8)
 VECTOR_WEAVES = 1152
@@ -384,8 +385,10 @@ def tile_attend_gahead_sam_log_pl_kernel(tc, wT, mT, xT, y, ts, us, wt, offs, ou
         single = PIECE - WHOLE_WORDS
         target = pairs[:, 1, near, :].rearrange("p (n c) e -> p n c e", c=PIECE)
         source = window[2][:, near].rearrange("p (n c) -> p n c", c=PIECE)
-        gpsimd_round(pairs[:, 1, near, 0], window[2][:, near])
+        own = slice(near_cols - PIECE, near_cols - WHOLE_WORDS)
+        gpsimd_round(pairs[:, 1, : own.start + SHARED, 0], window[2][:, : own.start + SHARED])
         nc.vector.tensor_copy(out=target[:, :, single:, :], in_=source[:, :, single:].unsqueeze(3).to_broadcast([P, NEAR_PIECES, WHOLE_WORDS, 2]))
+        nc.vector.tensor_copy(out=pairs[:, 1, own, 0], in_=window[2][:, own])
         for t in range(LANES - 1):
             first = POOL_COLS if t < 2 else near_cols
             nc.scalar.copy(out=pairs[:, t // 2, first:, t % 2], in_=window[t][:, first:])

@@ -309,7 +309,7 @@ def tile_attend_gahead_sam_log_pl_kernel(tc, wT, mT, xT, y, ts, us, wt, offs, ou
 
         finish_w2(0, parts=2)
         idle = psum.tile([P, R], F32, name="idle", tag="a3")
-        nc.tensor.transpose(idle[:, :P], m_table[3][:, :P], ident_f32[:])
+        nc.tensor.transpose(idle[:, :P], w2_late[2][:, 0, :], ident_f32[:])
         for n in range(2):
             nc.tensor.matmul_mx(
                 out=idle[:],

@@ -308,18 +308,6 @@ def tile_attend_gahead_sam_log_pl_kernel(tc, wT, mT, xT, y, ts, us, wt, offs, ou
             )
 
         finish_w2(0, parts=2)
-        idle = psum.tile([P, R], F32, name="idle", tag="a3")
-        nc.tensor.transpose(idle[:, :P], w2_late[2][:, 0, :], ident_f32[:])
-        for n in range(2):
-            nc.tensor.matmul_mx(
-                out=idle[:],
-                lhsT=xd_codes[:, :P].bitcast(E4M3),
-                lhsT_scale=xd_scales[:, :P],
-                rhs=xd_codes[:].bitcast(E4M3),
-                rhs_scale=xd_scales[:],
-                start=True,
-                stop=True,
-            )
         finish_w2(1)
         finish_w2(2)
         score(0)

@@ -148,7 +148,13 @@ def tile_attend_gahead_sam_log_pl_kernel(tc, wT, mT, xT, y, ts, us, wt, offs, ou
 
         w_picked = [sb("w_picked%d" % t, [P, SLOTS], F32) for t in range(LANES)]
         w2_early = sb("w2_early", [P, 2, SLOTS], F32)
-        w2_late = [sb("w2_late%d" % j, [P, 2, CHUNK], F32) for j in range(CHUNKS)]
+        shared = sb("w2_shared", [P, 3 * CHUNK], F32)
+        w2_late = [
+            sb("w2_late0", [P, 2, CHUNK], F32),
+            shared[:, CHUNK:].rearrange("p (t i) -> p t i", t=2),
+            sb("w2_late2", [P, 2, CHUNK], F32),
+            shared[:, : 2 * CHUNK].rearrange("p (t i) -> p t i", t=2),
+        ]
         w2_by_d = [sb("w2_by_d%d" % j, [P, CHUNK, LANES], BF16) for j in range(CHUNKS)]
         w2_codes = [sb("w2_codes%d" % j, [P, CHUNK], U32) for j in range(CHUNKS)]
         w2_scales = [sb("w2_scales%d" % j, [P, CHUNK], U8) for j in range(CHUNKS)]
@@ -216,15 +222,18 @@ def tile_attend_gahead_sam_log_pl_kernel(tc, wT, mT, xT, y, ts, us, wt, offs, ou
             if j == 0:
                 scores[j] = [scores[j], psum.tile([P, LANES, CHUNK], F32, name="scores0_late", tag="b1")]
             if j == TURNED:
-                nc.tensor.matmul_mx(
-                    out=scores[j][:].rearrange("i u s -> i (u s)"),
-                    lhsT=w2_codes[j][:].bitcast(E4M3),
-                    lhsT_scale=w2_scales[j][:],
-                    rhs=xd_codes[:].bitcast(E4M3),
-                    rhs_scale=xd_scales[:],
-                    start=True,
-                    stop=True,
-                )
+                scores[j] = [scores[j], psum.tile([P, LANES, CHUNK], F32, name="scores3_late", tag="b2")]
+                for h in range(2):
+                    rows = slice(2 * h * P, 2 * (h + 1) * P)
+                    nc.tensor.matmul_mx(
+                        out=scores[j][h][:, :2, :].rearrange("i u s -> i (u s)"),
+                        lhsT=w2_codes[j][:].bitcast(E4M3),
+                        lhsT_scale=w2_scales[j][:],
+                        rhs=xd_codes[:, rows].bitcast(E4M3),
+                        rhs_scale=xd_scales[:, rows],
+                        start=True,
+                        stop=True,
+                    )
                 return
             if j == HALVED:
                 scores.append(psum.tile([P, 2, P], F32, name="scores_across", tag="b0"))
@@ -277,14 +286,15 @@ def tile_attend_gahead_sam_log_pl_kernel(tc, wT, mT, xT, y, ts, us, wt, offs, ou
 
         def turned_logits(j):
             scaled = sb("scaled", [P, LANES, P], F32, "logit_scale%d" % (j - 1))
-            nc.scalar.activation(out=scaled[:], in_=scores[j][:], func=ACT.Copy, scale=ts_col[:, 1:2])
-            scores[j] = psum.tile([P, LANES, CHUNK], F32, name="back", tag="b3")
-            for u in range(LANES):
-                nc.tensor.transpose(scores[j][:, u, :], scaled[:, u, :], ident_f32[:])
+            for h, bank in enumerate(("b3", "a0")):
+                nc.scalar.activation(out=scaled[:, 2 * h : 2 * h + 2, :], in_=scores[j][h][:, :2, :], func=ACT.Copy, scale=ts_col[:, 1:2])
+                scores[j][h] = psum.tile([P, 2, CHUNK], F32, name="back%d" % h, tag=bank)
+                for u in range(2):
+                    nc.tensor.transpose(scores[j][h][:, u, :], scaled[:, 2 * h + u, :], ident_f32[:])
 
         def turned_sigmoid(j):
             for u in range(LANES):
-                nc.scalar.activation(out=work[j][:, u, :], in_=scores[j][:, u, :], func=ACT.Sigmoid, scale=us_col[:, u : u + 1])
+                nc.scalar.activation(out=work[j][:, u, :], in_=scores[j][u // 2][:, u % 2, :], func=ACT.Sigmoid, scale=us_col[:, u : u + 1])
 
         def residual(j):
             sigmoid = work[j]

@@ -219,8 +219,8 @@ def tile_attend_gahead_sam_log_pl_kernel(tc, wT, mT, xT, y, ts, us, wt, offs, ou
                 out=w2_codes[j][:].bitcast(E4M3), scales=w2_scales[j][:], in_=w2_by_d[j][:].rearrange("p i t -> p (i t)")
             )
             scores[j] = psum.tile([P, LANES, CHUNK], F32, name="scores%d" % j, tag="a%d" % j)
-            if j == 0:
-                scores[j] = [scores[j], psum.tile([P, LANES, CHUNK], F32, name="scores0_late", tag="b1")]
+            if j < 2:
+                scores[j] = [scores[j], psum.tile([P, LANES, CHUNK], F32, name="scores%d_late" % j, tag=("b1", "b3")[j])]
             if j == TURNED:
                 scores[j] = [scores[j], psum.tile([P, LANES, CHUNK], F32, name="scores3_late", tag="b2")]
                 for h in range(2):
@@ -249,7 +249,7 @@ def tile_attend_gahead_sam_log_pl_kernel(tc, wT, mT, xT, y, ts, us, wt, offs, ou
             for u in range(2 if j == HALVED else LANES):
                 rows = slice(u * P, (u + 1) * P)
                 nc.tensor.matmul_mx(
-                    out=(scores[j][u // 2] if j == 0 else scores[j])[:, u, :],
+                    out=(scores[j][u // 2] if j < 2 else scores[j])[:, u, :],
                     lhsT=xd_codes[:, rows].bitcast(E4M3),
                     lhsT_scale=xd_scales[:, rows],
                     rhs=w2_codes[j][:].bitcast(E4M3),
@@ -258,16 +258,13 @@ def tile_attend_gahead_sam_log_pl_kernel(tc, wT, mT, xT, y, ts, us, wt, offs, ou
                     stop=True,
                 )
 
-        def first_logits(h):
-            lanes = slice(2 * h, 2 * h + 2)
-            nc.vector.tensor_tensor(
-                out=work[0][:, lanes, :], in0=scores[0][h][:, lanes, :], in1=logit_scale[0][:, lanes, :], op=ALU.mult
-            )
-            nc.scalar.activation(out=work[0][:, lanes, :], in_=work[0][:, lanes, :], func=ACT.Sigmoid)
-
         def logits(j):
-            nc.vector.tensor_tensor(out=work[j][:], in0=scores[j][:], in1=logit_scale[j][:], op=ALU.mult)
-            nc.scalar.activation(out=work[j][:], in_=work[j][:], func=ACT.Sigmoid)
+            for h in range(2):
+                lanes = slice(2 * h, 2 * h + 2)
+                nc.vector.tensor_tensor(
+                    out=work[j][:, lanes, :], in0=scores[j][h][:, lanes, :], in1=logit_scale[j][:, lanes, :], op=ALU.mult
+                )
+                nc.scalar.activation(out=work[j][:, lanes, :], in_=work[j][:, lanes, :], func=ACT.Sigmoid)
 
         def half_logits(j):
             nc.vector.tensor_tensor(out=work[j][:, :2, :], in0=scores[j][:, :2, :], in1=logit_scale[j][:, :2, :], op=ALU.mult)
@@ -324,18 +321,18 @@ def tile_attend_gahead_sam_log_pl_kernel(tc, wT, mT, xT, y, ts, us, wt, offs, ou
         score(1)
         finish_w2(3)
         score(2)
-        first_logits(0)
-        first_logits(1)
+        logits(0)
         logits(1)
         half_turn(2)
         score(3)
         turned_logits(3)
+        residual(0)
         half_logits(2)
         half_sigmoid(2)
         turned_sigmoid(3)
         for pair in range(2):
             chunks = (2 * pair, 2 * pair + 1)
-            for j in chunks:
+            for j in chunks[1 - pair :]:
                 residual(j)
             for j in chunks:
                 gradient(j)

@@ -282,7 +282,7 @@ def tile_attend_gahead_sam_log_pl_kernel(tc, wT, mT, xT, y, ts, us, wt, offs, ou
                 nc.scalar.activation(out=work[j][:, u, :], in_=scores[CHUNKS][:, u - 2, :], func=ACT.Sigmoid, scale=us_col[:, u : u + 1])
 
         def turned_logits(j):
-            scaled = sb("scaled", [P, LANES, P], F32, "logit_scale%d" % (j - 1))
+            scaled = sb("scaled", [P, LANES, P], F32, "logit_scale1")
             for h, bank in enumerate(("b3", "a0")):
                 nc.scalar.activation(out=scaled[:, 2 * h : 2 * h + 2, :], in_=scores[j][h][:, :2, :], func=ACT.Copy, scale=ts_col[:, 1:2])
                 scores[j][h] = psum.tile([P, 2, CHUNK], F32, name="back%d" % h, tag=bank)

@@ -42,7 +42,7 @@ def tile_attend_gahead_sam_log_pl_kernel(tc, wT, mT, xT, y, ts, us, wt, offs, ou
         psum = ctx.enter_context(tc.psum_pool(name="psum", bufs=1))
 
         def sb(name, shape, dtype, tag=None):
-            return keep.tile(shape, dtype, name=name, tag=tag or name, align_bytes=64)
+            return keep.tile(shape, dtype, name=name, tag=tag or name, align_bytes=256)
 
         def slot_list(first, count):
             return offsets[:, first // 16 : (first + count) // 16]

from contextlib import ExitStack

import concourse.mybir as mybir
from concourse.masks import make_identity

D, R, SLOTS, COLS = 512, 512, 512, 2048
FLOPS = 2 * 2 * D * R * SLOTS

F32 = mybir.dt.float32
BF16 = mybir.dt.bfloat16
I32 = mybir.dt.int32
U32 = mybir.dt.uint32
U16 = mybir.dt.uint16
U8 = mybir.dt.uint8
E4M3 = mybir.dt.float8_e4m3fn_x4
E5M2 = mybir.dt.float8_e5m2_x4
ALU = mybir.AluOpType
ACT = mybir.ActivationFunctionType

P = 128
LANES = 4
CHUNK = 128
CHUNKS = SLOTS // CHUNK
PIECE = 256
PIECES = COLS // PIECE
WHOLE_WORDS = 16
SHARED = 8
NEAR_PIECES = 3
STORE_EDGES = (0, 3, 5, 7, 8)
VECTOR_WEAVES = 1152
POOL_COLS = 1280
SHORT = 16
FOLD = COLS // P
TURNED = CHUNKS - 1
HALVED = CHUNKS - 2


def tile_attend_gahead_sam_log_pl_kernel(tc, wT, mT, xT, y, ts, us, wt, offs, out_0, out_1, out_2):
    nc = tc.nc
    with ExitStack() as ctx:
        keep = ctx.enter_context(tc.tile_pool(name="keep", bufs=1))
        psum = ctx.enter_context(tc.psum_pool(name="psum", bufs=1))

        def sb(name, shape, dtype, tag=None):
            return keep.tile(shape, dtype, name=name, tag=tag or name, align_bytes=256)

        def slot_list(first, count):
            return offsets[:, first // 16 : (first + count) // 16]

        offsets = keep.tile([P, SLOTS // 16], U16, name="offsets")
        x = sb("x", [P, LANES, R], F32)
        nc.sync.dma_start(out=x[:], in_=xT.rearrange("(p t) r -> p t r", t=LANES))
        nc.sync.dma_start(offsets[:], offs)

        ts_rows = sb("ts_rows", [P, P], F32)
        row_scales = sb("row_scales", [P, R], F32)
        nc.vector.memset(ts_rows[:], 0.0)
        nc.vector.memset(row_scales[:], 0.0)
        nc.sync.dma_start(out=ts_rows[:FOLD, :], in_=ts[0].rearrange("(n c) -> n c", c=P))
        nc.sync.dma_start(out=row_scales[0:1, :], in_=us.rearrange("r one -> one r"))
        nc.sync.dma_start(out=row_scales[1:2, :], in_=wt.rearrange("r one -> one r"))
        warm = sb("warm", [P, 1], F32)
        nc.scalar.activation(out=warm[:], in_=ts_rows[:, 0:1], func=ACT.Sigmoid)

        w_rows = wT.rearrange("(p t) c -> p t c", t=LANES)
        m_rows = mT.rearrange("(p t) c -> p t c", t=LANES)
        w_table = [sb("w_table%d" % t, [P, COLS], F32) for t in range(LANES)]
        m_table = [sb("m_table%d" % t, [P, COLS], F32) for t in range(LANES)]
        for t in range(LANES):
            if t < 2:
                for plane in (2 * t, 2 * t + 1):
                    nc.sync.dma_start(out=w_table[plane][:], in_=w_rows[:, plane, :])
            nc.sync.dma_start(out=m_table[t][:], in_=m_rows[:, t, :])
        labels = sb("labels", [P, LANES, SLOTS], F32, "m_table2")
        y_rows = y.rearrange("(p u) i -> p u i", u=LANES)
        for first in range(0, SLOTS, SLOTS // 2):
            slots = slice(first, first + SLOTS // 2)
            nc.sync.dma_start(out=labels[:, :, slots], in_=y_rows[:, :, slots])

        ident_f32 = sb("ident_f32", [P, P], F32)
        ident_bf16 = sb("ident_bf16", [P, P], BF16)
        make_identity(nc, ident_f32[:])
        make_identity(nc, ident_bf16[:])

        window = [sb("window%d" % t, [P, COLS], F32) for t in range(LANES)]
        for t in range(LANES):
            (nc.vector if t < 2 else nc.gpsimd).memset(window[t][:], 0.0)

        x_by_d = sb("x_by_d", [P, LANES, P, LANES], BF16)
        nc.scalar.copy(
            out=x_by_d[:].rearrange("p u s t -> p s u t"),
            in_=x[:].rearrange("p t (s u) -> p s u t", u=LANES),
        )
        xd_codes = sb("xd_codes", [P, R], U32)
        xd_scales = sb("xd_scales", [P, R], U8)
        nc.vector.quantize_mx(
            out=xd_codes[:].bitcast(E4M3), scales=xd_scales[:], in_=x_by_d[:].rearrange("p u s t -> p (u s t)")
        )

        x_by_r = sb("x_by_r", [P, LANES, P, LANES], BF16)
        for t in range(LANES):
            turned = psum.tile([P, LANES, P], BF16, name="turned%d" % t, tag="a%d" % t)
            for u in range(LANES):
                nc.tensor.transpose(turned[:, u, :], x_by_d[:, u, :, t], ident_bf16[:])
            nc.scalar.copy(out=x_by_r[:, t, :, :], in_=turned[:].rearrange("s u p -> s p u"))
        xr_codes = sb("xr_codes", [P, D], U32)
        xr_scales = sb("xr_scales", [P, D], U8)
        nc.vector.quantize_mx(
            out=xr_codes[:].bitcast(E4M3), scales=xr_scales[:], in_=x_by_r[:].rearrange("s t p u -> s (t p u)")
        )

        ts_down = psum.tile([P, P], F32, name="ts_down", tag="b0")
        nc.tensor.transpose(ts_down[:], ts_rows[:], ident_f32[:])
        ts_folded = sb("ts_folded", [P, FOLD], F32)
        nc.scalar.copy(out=ts_folded[:], in_=ts_down[:, :FOLD])
        scales_down = psum.tile([P, LANES, P], F32, name="scales_down", tag="b1")
        for u in range(LANES):
            nc.tensor.transpose(scales_down[:, u, :], row_scales[:, u::LANES], ident_f32[:])
        us_col = sb("us_col", [P, LANES], F32)
        wt_col = sb("wt_col", [P, LANES], F32)
        nc.scalar.copy(out=us_col[:], in_=scales_down[:, :, 0])
        nc.scalar.copy(out=wt_col[:], in_=scales_down[:, :, 1])
        ts_table = sb("ts_table", [P, COLS], F32)
        for b in range(FOLD // 4):
            spread = psum.tile([P, 4, P], F32, name="spread%d" % b, tag="b%d" % b)
            for c in range(4):
                column = ts_folded[:, 4 * b + c : 4 * b + c + 1]
                nc.tensor.transpose(spread[:, c, :], column.to_broadcast([P, P]), ident_f32[:])
            nc.scalar.copy(out=ts_table[:, 4 * b * P : 4 * (b + 1) * P], in_=spread[:].rearrange("p c n -> p (c n)"))
        ts_all = sb("ts_all", [P, SLOTS], F32)
        nc.vector.tensor_copy(out=ts_all[:], in_=ts_table[:].indirect(offsets[:]))
        ts_turned = psum.tile([P, 2, P], F32, name="ts_turned", tag="b0")
        for j in (HALVED, TURNED):
            nc.tensor.transpose(ts_turned[:, j - HALVED, :], ts_all[:, j * P : (j + 1) * P], ident_f32[:])
        ts_col = sb("ts_col", [P, 2], F32)
        nc.scalar.copy(out=ts_col[:], in_=ts_turned[:, :, 0])
        wu_col = sb("wu_col", [P, LANES], F32)
        nc.vector.tensor_tensor(out=wu_col[:], in0=wt_col[:], in1=us_col[:], op=ALU.mult)
        logit_scale = [sb("logit_scale%d" % j, [P, LANES, CHUNK], F32) for j in range(TURNED)]
        grad_scale = sb("grad_scale", [P, LANES, SLOTS], F32)
        for j in range(TURNED):
            for u in range(2 if j == HALVED else LANES):
                nc.scalar.activation(
                    out=logit_scale[j][:, u, :], in_=ts_all[:, j * CHUNK : (j + 1) * CHUNK], func=ACT.Copy, scale=us_col[:, u : u + 1]
                )
        for u in range(LANES):
            nc.scalar.activation(out=grad_scale[:, u, :], in_=ts_all[:], func=ACT.Copy, scale=wu_col[:, u : u + 1])

        w_picked = [sb("w_picked%d" % t, [P, SLOTS], F32) for t in range(LANES)]
        w2_early = sb("w2_early", [P, 2, SLOTS], F32)
        shared = sb("w2_shared", [P, 3 * CHUNK], F32)
        w2_late = [
            sb("w2_late0", [P, 2, CHUNK], F32),
            shared[:, CHUNK:].rearrange("p (t i) -> p t i", t=2),
            sb("w2_late2", [P, 2, CHUNK], F32),
            shared[:, : 2 * CHUNK].rearrange("p (t i) -> p t i", t=2),
        ]
        w2_by_d = [sb("w2_by_d%d" % j, [P, CHUNK, LANES], BF16) for j in range(CHUNKS)]
        w2_codes = [sb("w2_codes%d" % j, [P, CHUNK], U32) for j in range(CHUNKS)]
        w2_scales = [sb("w2_scales%d" % j, [P, CHUNK], U8) for j in range(CHUNKS)]

        def chunk(j):
            return slice(j * CHUNK, (j + 1) * CHUNK)

        def add_listed(t, out, first, count):
            nc.vector.tensor_tensor(
                out=out, in0=m_table[t][:].indirect(slot_list(first, count)), in1=w_picked[t][:, first : first + count], op=ALU.add
            )

        for t in range(LANES):
            nc.vector.tensor_copy(out=w_picked[t][:], in_=w_table[t][:].indirect(offsets[:]))
            if t < 2:
                add_listed(t, w2_early[:, t, :], 0, SLOTS)
        for j in range(CHUNKS):
            nc.scalar.copy(out=w2_by_d[j][:, :, 0:2], in_=w2_early[:, :, chunk(j)].rearrange("p t i -> p i t"))
            add_listed(2, w2_late[j][:, 0, :], j * CHUNK, CHUNK)

        scores = [None] * CHUNKS
        work = [sb("work%d" % j, [P, LANES, CHUNK], F32) for j in range(CHUNKS)]
        g_by_r = [sb("g_by_r%d" % j, [P, CHUNK, LANES], BF16) for j in range(CHUNKS)]
        g_codes = sb("g_codes", [P, SLOTS], U32)
        g_scales = sb("g_scales", [P, SLOTS], U8)
        half = SLOTS // 2
        first_half, second_half = slice(0, half), slice(half, SLOTS)

        def table_gradient(t, bank, runs, into, copy, skip=0):
            features = slice(t * P, (t + 1) * P)
            base = runs[0].start
            sums = psum.tile([P, runs[-1].stop - base], F32, name="sums%d_%d" % (t, base), tag=bank)
            for slots in runs:
                nc.tensor.matmul_mx(
                    out=sums[:, slots.start - base : slots.stop - base],
                    lhsT=xr_codes[:, features].bitcast(E4M3),
                    lhsT_scale=xr_scales[:, features],
                    rhs=g_codes[:, slots].bitcast(E5M2),
                    rhs_scale=g_scales[:, slots],
                    start=True,
                    stop=True,
                )
            copy(out=into, in_=sums[:, skip:])
            return sums

        def scatter(t, slots, source, on_scalar=False):
            out = window[t][:].indirect(slot_list(slots.start, slots.stop - slots.start))
            if not on_scalar:
                nc.vector.tensor_copy(out=out, in_=source)
            else:
                nc.scalar.activation(out=out, in_=source, func=ACT.Copy)

        def finish_w2(j, parts=1):
            width = CHUNK // parts
            for first in range(0, CHUNK, width):
                part = slice(first, first + width)
                add_listed(3, w2_late[j][:, 1, part], j * CHUNK + first, width)
                nc.scalar.copy(out=w2_by_d[j][:, part, 2:4], in_=w2_late[j][:, :, part].rearrange("p t i -> p i t"))

        def score(j):
            nc.vector.quantize_mx(
                out=w2_codes[j][:].bitcast(E4M3), scales=w2_scales[j][:], in_=w2_by_d[j][:].rearrange("p i t -> p (i t)")
            )
            scores[j] = psum.tile([P, LANES, CHUNK], F32, name="scores%d" % j, tag="a%d" % j)
            if j < 2:
                scores[j] = [scores[j], psum.tile([P, LANES, CHUNK], F32, name="scores%d_late" % j, tag=("b1", "b3")[j])]
            if j == TURNED:
                scores[j] = [scores[j], psum.tile([P, LANES, CHUNK], F32, name="scores3_late", tag="b2")]
                for h in range(2):
                    rows = slice(2 * h * P, 2 * (h + 1) * P)
                    nc.tensor.matmul_mx(
                        out=scores[j][h][:, :2, :].rearrange("i u s -> i (u s)"),
                        lhsT=w2_codes[j][:].bitcast(E4M3),
                        lhsT_scale=w2_scales[j][:],
                        rhs=xd_codes[:, rows].bitcast(E4M3),
                        rhs_scale=xd_scales[:, rows],
                        start=True,
                        stop=True,
                    )
                return
            if j == HALVED:
                scores.append(psum.tile([P, 2, P], F32, name="scores_across", tag="b0"))
                nc.tensor.matmul_mx(
                    out=scores[CHUNKS][:].rearrange("i u s -> i (u s)"),
                    lhsT=w2_codes[j][:].bitcast(E4M3),
                    lhsT_scale=w2_scales[j][:],
                    rhs=xd_codes[:, 2 * P :].bitcast(E4M3),
                    rhs_scale=xd_scales[:, 2 * P :],
                    start=True,
                    stop=True,
                )
            for u in range(2 if j == HALVED else LANES):
                rows = slice(u * P, (u + 1) * P)
                nc.tensor.matmul_mx(
                    out=(scores[j][u // 2] if j < 2 else scores[j])[:, u, :],
                    lhsT=xd_codes[:, rows].bitcast(E4M3),
                    lhsT_scale=xd_scales[:, rows],
                    rhs=w2_codes[j][:].bitcast(E4M3),
                    rhs_scale=w2_scales[j][:],
                    start=True,
                    stop=True,
                )

        def logits(j):
            for h in range(2):
                lanes = slice(2 * h, 2 * h + 2)
                nc.vector.tensor_tensor(
                    out=work[j][:, lanes, :], in0=scores[j][h][:, lanes, :], in1=logit_scale[j][:, lanes, :], op=ALU.mult
                )
                nc.scalar.activation(out=work[j][:, lanes, :], in_=work[j][:, lanes, :], func=ACT.Sigmoid)

        def half_logits(j):
            nc.vector.tensor_tensor(out=work[j][:, :2, :], in0=scores[j][:, :2, :], in1=logit_scale[j][:, :2, :], op=ALU.mult)
            nc.scalar.activation(out=work[j][:, :2, :], in_=work[j][:, :2, :], func=ACT.Sigmoid)

        def half_turn(j):
            scaled = sb("half_scaled", [P, 2, P], F32, "logit_scale0")
            nc.scalar.activation(out=scaled[:], in_=scores[CHUNKS][:], func=ACT.Copy, scale=ts_col[:, 0:1])
            scores[CHUNKS] = psum.tile([P, 2, CHUNK], F32, name="half_back", tag="a1")
            for u in range(2):
                nc.tensor.transpose(scores[CHUNKS][:, u, :], scaled[:, u, :], ident_f32[:])

        def half_sigmoid(j):
            for u in range(2, LANES):
                nc.scalar.activation(out=work[j][:, u, :], in_=scores[CHUNKS][:, u - 2, :], func=ACT.Sigmoid, scale=us_col[:, u : u + 1])

        def turned_logits(j):
            scaled = sb("scaled", [P, LANES, P], F32, "logit_scale1")
            for h, bank in enumerate(("b3", "a0")):
                nc.scalar.activation(out=scaled[:, 2 * h : 2 * h + 2, :], in_=scores[j][h][:, :2, :], func=ACT.Copy, scale=ts_col[:, 1:2])
                scores[j][h] = psum.tile([P, 2, CHUNK], F32, name="back%d" % h, tag=bank)
                for u in range(2):
                    nc.tensor.transpose(scores[j][h][:, u, :], scaled[:, 2 * h + u, :], ident_f32[:])

        def turned_sigmoid(j):
            for u in range(LANES):
                nc.scalar.activation(out=work[j][:, u, :], in_=scores[j][u // 2][:, u % 2, :], func=ACT.Sigmoid, scale=us_col[:, u : u + 1])

        def residual(j):
            sigmoid = work[j]
            if j >= 2:
                work[j] = sb("misses%d" % j, [P, LANES, CHUNK], F32, "g_by_r%d" % (j - 2))
            nc.vector.tensor_tensor(out=work[j][:], in0=sigmoid[:], in1=labels[:, :, chunk(j)], op=ALU.subtract)

        def gradient(j):
            nc.vector.tensor_tensor(
                out=g_by_r[j][:].rearrange("p (c i) u -> p c u i", i=2),
                in0=work[j][:].rearrange("p u (c i) -> p c u i", i=2),
                in1=grad_scale[:, :, chunk(j)].rearrange("p u (c i) -> p c u i", i=2),
                op=ALU.mult,
            )

        def quantise_g(j):
            nc.vector.quantize_mx(
                out=g_codes[:, chunk(j)].bitcast(E5M2),
                scales=g_scales[:, chunk(j)],
                in_=g_by_r[j][:].rearrange("p i u -> p (i u)"),
            )

        finish_w2(0, parts=2)
        finish_w2(1)
        finish_w2(2)
        score(0)
        score(1)
        finish_w2(3)
        score(2)
        logits(0)
        logits(1)
        half_turn(2)
        score(3)
        turned_logits(3)
        residual(0)
        half_logits(2)
        half_sigmoid(2)
        turned_sigmoid(3)
        for pair in range(2):
            chunks = (2 * pair, 2 * pair + 1)
            for j in chunks[1 - pair :]:
                residual(j)
            for j in chunks:
                gradient(j)
            quantise_g(chunks[0])
            if pair == 0:
                quantise_g(chunks[1])
        early = [sb("dw_early%d" % t, [P, half], F32) for t in range(2)]
        table_gradient(0, "b0", [chunk(0)], early[0][:, chunk(0)], nc.scalar.copy)
        table_gradient(0, "b1", [chunk(1)], early[0][:, chunk(1)], nc.scalar.copy)
        sums = table_gradient(1, "b2", [first_half], early[1][:, SHORT:], nc.scalar.copy, SHORT)
        scatter(0, first_half, early[0][:], on_scalar=True)
        nc.vector.tensor_copy(out=early[1][:, :SHORT], in_=sums[:, :SHORT])
        quantise_g(3)
        scatter(1, first_half, early[1][:])

        out_rows = out_0.rearrange("(p t) c -> p t c", t=LANES)
        near_cols = NEAR_PIECES * PIECE
        near = slice(0, near_cols)

        def piece(k):
            return slice(k * PIECE, (k + 1) * PIECE)

        late = [sb("dw_late%d" % t, [P, half], F32) for t in range(3)]
        pair_flat = sb("pair_flat", [P, LANES * COLS], BF16)
        pairs = pair_flat[:].rearrange("p (h c e) -> p h c e", h=2, e=2)
        dw_scalar = pair_flat[:].bitcast(F32)[:, COLS - half : COLS]
        dw_last = sb("dw_last", [P, SLOTS], F32)
        table_gradient(0, "a0", [second_half], late[0][:], nc.scalar.copy)
        table_gradient(1, "a1", [second_half], late[1][:], nc.scalar.copy)
        table_gradient(2, "a2", [second_half], late[2][:], nc.scalar.copy)
        table_gradient(2, "a0", [first_half], dw_scalar, nc.scalar.copy)
        scatter(2, first_half, dw_scalar, on_scalar=True)
        table_gradient(3, "a0", [slice(0, SLOTS)], dw_last[:], nc.scalar.copy)
        last_runs = [(second_half, late[t][:]) for t in range(3)] + [(slice(0, SLOTS), dw_last[:])]
        for t, (slots, source) in enumerate(last_runs):
            scatter(t, slots, source)
            nc.sync.dma_start(out=out_rows[:, t, :], in_=window[t][:])

        def gpsimd_round(out, source):
            nc.gpsimd.tensor_scalar(out=out, in0=source, scalar1=1.0, scalar2=0.0, op0=ALU.mult, op1=ALU.add)

        for t in range(2):
            gpsimd_round(pairs[:, 0, :POOL_COLS, t], window[t][:, :POOL_COLS])
        runs = (slice(0, 2 * PIECE), slice(2 * PIECE, near_cols))
        single = PIECE - WHOLE_WORDS
        target = pairs[:, 1, near, :].rearrange("p (n c) e -> p n c e", c=PIECE)
        source = window[2][:, near].rearrange("p (n c) -> p n c", c=PIECE)
        own = slice(near_cols - PIECE, near_cols - WHOLE_WORDS)
        gpsimd_round(pairs[:, 1, : own.start + SHARED, 0], window[2][:, : own.start + SHARED])
        nc.vector.tensor_copy(out=target[:, :, single:, :], in_=source[:, :, single:].unsqueeze(3).to_broadcast([P, NEAR_PIECES, WHOLE_WORDS, 2]))
        nc.vector.tensor_copy(out=pairs[:, 1, own, 0], in_=window[2][:, own])
        for t in range(LANES - 1):
            first = POOL_COLS if t < 2 else near_cols
            nc.scalar.copy(out=pairs[:, t // 2, first:, t % 2], in_=window[t][:, first:])
        for run in runs:
            nc.vector.tensor_copy(out=pairs[:, 1, run, 1], in_=window[3][:, run])
        for k in range(NEAR_PIECES, PIECES):
            nc.scalar.copy(out=pairs[:, 1, piece(k), 1], in_=window[3][:, piece(k)])

        dead = ("m_table0", "m_table1", "m_table2", "m_table3", "w_table0", "w_table1", "x", "ts_table")
        woven = [sb("woven%d" % k, [P, PIECE, LANES], BF16, dead[k]) for k in range(PIECES)]
        out_codes = [
            sb("out_codes%d" % first, [P, (last - first) * PIECE], U32)
            for first, last in zip(STORE_EDGES, STORE_EDGES[1:])
        ]
        out_scales = sb("out_scales", [P, 2 * PIECE], U8)
        code_rows = out_1[0].rearrange("p c l -> p (c l)").bitcast(I32)

        def weave(k):
            words = pair_flat[:].bitcast(F32).rearrange("p (h c) -> p c h", h=2)
            target = woven[k][:].rearrange("p c t -> p (c t)").bitcast(F32).rearrange("p (c h) -> p c h", h=2)
            cut = min(max(VECTOR_WEAVES - k * PIECE, 0), PIECE)
            if cut > 0:
                nc.vector.tensor_copy(out=target[:, :cut, :], in_=words[:, k * PIECE : k * PIECE + cut, :])
            if cut < PIECE:
                nc.scalar.copy(out=target[:, cut:, :], in_=words[:, k * PIECE + cut : (k + 1) * PIECE, :])

        def quantise_out(k):
            side = slice((k % 2) * PIECE, (k % 2 + 1) * PIECE)
            n = max(e for e, first in enumerate(STORE_EDGES) if first <= k)
            nc.vector.quantize_mx(
                out=out_codes[n][:, piece(k - STORE_EDGES[n])].bitcast(E4M3),
                scales=out_scales[4 * (k // 2) :, side],
                in_=woven[k][:].rearrange("p c t -> p (c t)"),
            )
            if k + 1 == STORE_EDGES[n + 1]:
                nc.sync.dma_start(out=code_rows[:, STORE_EDGES[n] * PIECE : (k + 1) * PIECE], in_=out_codes[n][:].bitcast(I32))

        weave(0)
        for k in range(PIECES):
            if k + 1 < PIECES:
                weave(k + 1)
            quantise_out(k)
        scale_rows = out_2[0].bitcast(I32)
        for q in range(4):
            queue = nc.sync if q % 2 == 0 else nc.scalar
            queue.dma_start(
                out=scale_rows[4 * q : 4 * q + 4, :].rearrange("j (h c) -> h j c", h=4),
                in_=out_scales[32 * q : 32 * q + 16, :].bitcast(I32),
            )
